import numpy as np
import ml_dtypes


def mxq(x, axis, fmt="e4m3"):
    dtype, down = {"e4m3": (ml_dtypes.float8_e4m3fn, 7), "e5m2": (ml_dtypes.float8_e5m2, 14)}[fmt]
    v = np.moveaxis(np.asarray(x, np.float32).astype(ml_dtypes.bfloat16).astype(np.float64), axis, -1)
    blocks = v.reshape(v.shape[:-1] + (-1, 32))
    amax = np.abs(blocks).max(-1, keepdims=True)
    byte = np.maximum(np.where(amax > 0, np.frexp(amax)[1] - 1 + 127, 0) - down, 1)
    scale = np.exp2(byte - 127.0)
    codes = (blocks / scale).astype(np.float32).astype(dtype).astype(np.float64)
    return np.moveaxis((codes * scale).reshape(v.shape), -1, axis)


WIDE = False


def mx_kscale(k):
    if not WIDE:
        return np.ones(k)
    levels = np.array([18, -18])
    if k % 512:
        return np.exp2(np.random.permutation(np.resize(levels, k // 32))).repeat(32)
    a = np.empty((k // 512, 16))
    for p in range(k // 512):
        a[p, :8] = np.random.permutation(np.resize(levels, 8))
        for g in range(8):
            far = levels[np.abs(levels - a[p, g]) >= 10]
            a[p, g + 8] = far[np.random.randint(len(far))]
    return np.exp2(a.ravel()).repeat(32)


def f64(x):
    return np.asarray(x).astype(np.float64)


def striped(idx):
    return np.tile(np.asarray(idx).reshape(-1, 16).T, (8, 1)).astype(np.uint16)


def unstriped(offs):
    return offs[:16].T.reshape(-1).astype(np.int64)

def planes(y):
    n, m = y.shape
    v = y.astype(np.float32).astype(ml_dtypes.bfloat16).astype(np.float64).reshape(n // 32, 32, m)
    top = np.abs(v).max(1)
    byte = np.clip(np.where(top > 0, np.frexp(top)[1] - 1 + 127 - 7, 1), 1, 254)
    codes = (v * np.exp2(127.0 - byte)[:, None, :]).reshape(n, m).astype(np.float32).astype(ml_dtypes.float8_e4m3fn).view(np.uint8)
    words = codes.reshape(n // 512, 128, 4, m).transpose(0, 1, 3, 2)
    return np.ascontiguousarray(words), np.ascontiguousarray(byte.astype(np.uint8).reshape(n // 512, 16, m))


def sig(x):
    return 1.0 / (1.0 + np.exp(-x))


def setup_inputs():
    n = np.random.standard_normal
    uni = np.random.uniform
    idx = np.random.permutation(2048)[:512]
    f_d = mx_kscale(512)
    f_r = mx_kscale(512)
    return {
        "q1": (n((512, 512)) * f_d[:, None] * f_r[None, :]).astype(np.float32),
        "q2": (n((512, 512)) * f_d[:, None] * f_r[None, :]).astype(np.float32),
        "kT": (n((512, 2048)) / np.sqrt(512) / f_d[:, None]).astype(np.float32),
        "dp1": (n((512, 512))).astype(np.float32),
        "dp2": (n((512, 512))).astype(np.float32),
        "us": (uni(0.75, 1.3, (512, 1)) / f_r[:, None]).astype(np.float32),
        "ts": np.tile(uni(0.75, 1.3, 2048), (128, 1)).astype(np.float32),
        "w1": (uni(0.75, 1.3, (512, 1)) / np.sqrt(512)).astype(np.float32),
        "w2": (uni(0.75, 1.3, (512, 1)) / np.sqrt(512)).astype(np.float32),
        "offs": striped(idx),
    }


def reference(q1, q2, kT, dp1, dp2, us, ts, w1, w2, offs):
    idx = unstriped(offs)
    kT_i = f64(kT)[:, idx]
    ts_i = f64(ts)[:1][:, idx]
    q_kT_i = mxq(kT_i, 0, "e4m3")
    a1 = mxq(f64(q1), 0, "e4m3").T @ q_kT_i
    p1 = sig(f64(us) * ts_i * a1)
    g1 = f64(w1) * f64(us) * ts_i * f64(dp1) * p1 * (1.0 - p1)
    a2 = mxq(f64(q2), 0, "e4m3").T @ q_kT_i
    p2 = sig(f64(us) * ts_i * a2)
    g2 = f64(w2) * f64(us) * ts_i * f64(dp2) * p2 * (1.0 - p2)
    k1 = mxq(f64(q1), 1, "e4m3") @ mxq(g1, 0, "e5m2")
    k2 = mxq(f64(q2), 1, "e4m3") @ mxq(g2, 0, "e5m2")
    dk = k1 + k2
    out_0 = np.zeros((512, 2048))
    out_0[:, idx] = dk
    return (out_0,) + planes(out_0)

@@ -1,0 +1,254 @@
+from contextlib import ExitStack
+
+import concourse.mybir as mybir
+from concourse.masks import make_identity
+
+F32 = mybir.dt.float32
+BF16 = mybir.dt.bfloat16
+I32 = mybir.dt.int32
+U32 = mybir.dt.uint32
+U16 = mybir.dt.uint16
+U8 = mybir.dt.uint8
+E4M3 = mybir.dt.float8_e4m3fn_x4
+E5M2 = mybir.dt.float8_e5m2_x4
+ACT = mybir.ActivationFunctionType
+ALU = mybir.AluOpType
+
+P = 128
+D = 512
+R = 512
+SLOTS = 512
+TOKENS = 2048
+PACK = 4
+BLOCKS = SLOTS // P
+ODD = 1023
+CHUNKS = (256, 512, 512, 512, 256)
+ILS = "VVVSV"
+MODES = "GGGGGGGM"
+GT = "SVSVSVSV"
+FLOPS = 4 * 2 * D * R * SLOTS
+
+
+def tile_attend_ggqa_sig_k_pl_kernel(tc, q1, q2, kT, dp1, dp2, us, ts, w1, w2, offs, out_0, out_1, out_2):
+    nc = tc.nc
+    with ExitStack() as ctx:
+        keep = ctx.enter_context(tc.tile_pool(name="keep", bufs=1))
+        ring = ctx.enter_context(tc.tile_pool(name="ring", bufs=4))
+        psum = ctx.enter_context(tc.psum_pool(name="psum", bufs=1))
+
+        def held(shape, dtype, name, tag=None):
+            return keep.tile(shape, dtype, name=name, tag=tag or name, align_bytes=64)
+
+        def zero_on_vector(tile_):
+            nc.vector.memset(tile_[:, :ODD], 0.0)
+            nc.vector.memset(tile_[:, ODD:], 0.0)
+
+        def bank(tag, bufs):
+            return psum.tile([P, 512], F32, name=tag, tag=tag, bufs=bufs)
+
+        offsets = keep.tile([P, SLOTS // 16], U16, name="offsets")
+        nc.sync.dma_start(offsets[:], offs)
+        ts_row = held([P, TOKENS], F32, "ts_row")
+        zero_on_vector(ts_row)
+        q_raw = []
+        for h, q in enumerate((q1, q2)):
+            t_ = held([P, PACK, R], F32, "q_raw%d" % h)
+            nc.sync.dma_start(out=t_[:], in_=q.rearrange("(p j) r -> p j r", j=PACK))
+            q_raw.append(t_)
+            if h == 0:
+                nc.sync.dma_start(out=ts_row[0:1, :], in_=ts[0:1, :])
+        k_planes = kT.rearrange("(p j) c -> p j c", j=PACK)
+        k_raw = []
+        for j in range(PACK):
+            t_ = held([P, TOKENS], F32, "k_raw%d" % j)
+            nc.sync.dma_start(out=t_[:], in_=k_planes[:, j, :])
+            k_raw.append(t_)
+        dp_raw = []
+        for h, dp in enumerate((dp1, dp2)):
+            t_ = held([P, PACK, SLOTS], F32, "dp_raw%d" % h)
+            nc.sync.dma_start(out=t_[:], in_=dp.rearrange("(p b) i -> p b i", b=PACK))
+            dp_raw.append(t_)
+
+        cols = []
+        for name, vec in (("us_col", us), ("w1_col", w1), ("w2_col", w2)):
+            t_ = held([P, PACK], F32, name)
+            nc.scalar.dma_start(out=t_[:], in_=vec.rearrange("(p b) o -> p (b o)", b=PACK))
+            cols.append(t_)
+        us_col = cols[0]
+
+        ident = held([P, P], F32, "ident")
+        make_identity(nc, ident[:])
+        windows = [held([P, TOKENS], F32, "window%d" % j) for j in range(PACK - 1)]
+        zero_on_vector(windows[0])
+        for j in (1, 2):
+            nc.gpsimd.memset(windows[j][:], 0.0)
+
+        def quantize(grouped, codes, scales, fmt, lo, hi):
+            nc.vector.quantize_mx(out=codes[:, lo:hi].bitcast(fmt), scales=scales[:, lo:hi],
+                                  in_=grouped[:, PACK * lo:PACK * hi])
+
+        def mx_tiles(width, name):
+            return (held([P, width * PACK], BF16, name + "_grouped"), held([P, width], U32, name + "_codes"),
+                    held([P, width], U8, name + "_scales"))
+
+        qd = [mx_tiles(R, "qd%d" % h) for h in range(2)]
+        qr = [mx_tiles(D, "qr%d" % h) for h in range(2)]
+        keys = mx_tiles(SLOTS, "k")
+        qd_codes, qd_scales = [t_[1] for t_ in qd], [t_[2] for t_ in qd]
+        qr_codes, qr_scales = [t_[1] for t_ in qr], [t_[2] for t_ in qr]
+        k_grouped, k_codes, k_scales = keys
+
+        def group_along_d(h, mover):
+            mover(out=qd[h][0][:].rearrange("p (c i t) -> p c t i", i=4, t=PACK),
+                  in_=q_raw[h][:].rearrange("p t (c i) -> p c t i", i=4))
+
+        def group_along_r(h):
+            rounded = held([P, PACK * R], BF16, "q_rounded%d" % h)
+            nc.scalar.copy(out=rounded[:], in_=q_raw[h][:].rearrange("p j r -> p (j r)"))
+            words = rounded[:].bitcast(F32)
+            turned_words = qr[h][0][:].bitcast(F32)
+            for half in range(2):
+                ps = bank("a", 3)
+                for jj in range(2):
+                    j = 2 * half + jj
+                    for u in range(2):
+                        nc.tensor.transpose(ps[:, (2 * jj + u) * P:(2 * jj + u + 1) * P],
+                                            words[:, 256 * j + u:256 * (j + 1):2], ident[:])
+                nc.scalar.copy(
+                    out=turned_words[:, 512 * half:512 * (half + 1)].rearrange("p (j m u) -> p j m u", j=2, u=2),
+                    in_=ps[:].rearrange("p (j u m) -> p j m u", j=2, u=2))
+
+        k_view = k_grouped[:].rearrange("p (c t) -> p c t", t=PACK)
+
+        def gather_keys(j, lo, hi):
+            nc.vector.tensor_copy(out=k_view[:, lo:hi, j], in_=k_raw[j][:].indirect(offsets[:, lo // 16:hi // 16]))
+
+        ps = bank("c", 3)
+        for b in range(PACK):
+            nc.tensor.transpose(ps[:, b * P:(b + 1) * P], us_col[:, b:b + 1].to_broadcast([P, P]), ident[:])
+        us_half = held([P, R], F32, "us_half")
+        nc.scalar.activation(out=us_half[:].rearrange("p (u s e) -> p u s e", u=2, e=2),
+                             in_=ps[:].rearrange("p (u e s) -> p u s e", u=2, e=2), func=ACT.Copy, scale=0.5)
+
+        group_along_d(0, nc.vector.tensor_copy)
+        group_along_r(0)
+        quantize(*qd[0], E4M3, 0, R)
+
+        ts_listed = held([P, SLOTS], F32, "ts_listed")
+        nc.vector.tensor_copy(out=ts_listed[:], in_=ts_row[:].indirect(offsets[:]))
+        ps = bank("c", 3)
+        for b in range(BLOCKS):
+            nc.tensor.transpose(ps[:, b * P:(b + 1) * P], ts_listed[:, b * P:(b + 1) * P], ident[:])
+        ts_col = held([P, BLOCKS], F32, "ts_col")
+        nc.scalar.copy(out=ts_col[:], in_=ps[:, 0:512:P])
+        ts_neg = held([P, BLOCKS], F32, "ts_neg")
+        nc.scalar.activation(out=ts_neg[:], in_=ps[:, 0:512:P], func=ACT.Copy, scale=-1.0)
+        gate = []
+        for h in range(2):
+            t_ = held([P, PACK], F32, "gate%d" % h)
+            nc.vector.scalar_tensor_tensor(out=t_[:], in0=cols[1 + h][:], scalar=0.25, in1=us_col[:],
+                                           op0=ALU.mult, op1=ALU.mult)
+            gate.append(t_)
+
+        windows.append(held([P, TOKENS], F32, "window3", tag="q_raw0"))
+        for part in range(4):
+            nc.gpsimd.memset(windows[3][:, 512 * part:512 * (part + 1)], 0.0)
+        group_along_d(1, nc.scalar.copy)
+        group_along_r(1)
+        gather_keys(0, 0, SLOTS)
+        quantize(*qr[0], E4M3, 0, D)
+        gather_keys(1, 0, SLOTS)
+        quantize(*qd[1], E4M3, 0, R)
+        gather_keys(2, 0, SLOTS)
+        for half in range(2):
+            lo, hi = 256 * half, 256 * (half + 1)
+            gather_keys(3, lo, hi)
+            quantize(*keys, E4M3, lo, hi)
+
+        g_codes, g_scales = [], []
+        for h in range(2):
+            for b in range(PACK):
+                nc.gpsimd.tensor_scalar(out=dp_raw[h][:, b, :], in0=dp_raw[h][:, b, :], scalar1=gate[h][:, b:b + 1], scalar2=0.0, op0=ALU.mult, op1=ALU.add)
+            g_grouped = held([P, SLOTS * PACK], BF16, "g_grouped%d" % h)
+            g_words = g_grouped[:].bitcast(F32)
+            codes = held([P, SLOTS], U32, "g_codes%d" % h)
+            scales = held([P, SLOTS], U8, "g_scales%d" % h)
+            for ib in range(BLOCKS):
+                blk = slice(ib * P, (ib + 1) * P)
+                score = bank("a", 3)
+                nc.tensor.matmul_mx(out=score[:], lhsT=k_codes[:, blk].bitcast(E4M3), lhsT_scale=k_scales[:, blk],
+                                    rhs=qd_codes[h][:].bitcast(E4M3), rhs_scale=qd_scales[h][:], start=True, stop=True)
+                arg = ring.tile([P, R], F32, name="arg")
+                nc.vector.tensor_tensor(out=arg[:].rearrange("p (u s e) -> p u s e", u=2, e=2),
+                                        in0=score[:].rearrange("p (s u e) -> p u s e", u=2, e=2),
+                                        in1=us_half[:].rearrange("p (u s e) -> p u s e", u=2, e=2), op=ALU.mult)
+                nc.scalar.activation(out=arg[:], in_=arg[:], func=ACT.Tanh, scale=ts_col[:, ib:ib + 1])
+                mode = MODES[4 * h + ib]
+                dpt = bank("c", 3)
+                for b in range(PACK):
+                    nc.tensor.transpose(dpt[:, b * P:(b + 1) * P], dp_raw[h][:, b, blk], ident[:])
+                g_rows = ring.tile([P, R], BF16, name="g_rows", align_bytes=64)
+                if mode == "M":
+                    sq = ring.tile([P, R], F32, name="sq")
+                    nc.vector.scalar_tensor_tensor(out=sq[:], in0=arg[:], scalar=ts_neg[:, ib:ib + 1], in1=arg[:], op0=ALU.mult, op1=ALU.mult)
+                    for u in range(2):
+                        half = slice(256 * u, 256 * (u + 1))
+                        nc.vector.scalar_tensor_tensor(out=g_rows[:, half].rearrange("p (s e) -> p s e", e=2),
+                                                       in0=sq[:, half].rearrange("p (s e) -> p s e", e=2), scalar=ts_col[:, ib:ib + 1],
+                                                       in1=dpt[:, half].rearrange("p (e s) -> p s e", e=2), op0=ALU.add, op1=ALU.mult)
+                else:
+                    nc.scalar.activation(out=arg[:], in_=arg[:], func=ACT.Square)
+                    eng = nc.gpsimd if mode == "G" else nc.vector
+                    eng.tensor_scalar(out=arg[:], in0=arg[:], scalar1=ts_neg[:, ib:ib + 1], scalar2=ts_col[:, ib:ib + 1], op0=ALU.mult, op1=ALU.add)
+                    nc.vector.tensor_tensor(out=g_rows[:].rearrange("p (u s e) -> p u s e", u=2, e=2),
+                                            in0=arg[:].rearrange("p (u s e) -> p u s e", u=2, e=2),
+                                            in1=dpt[:].rearrange("p (u e s) -> p u s e", u=2, e=2), op=ALU.mult)
+                gt = bank("g", 2)
+                row_words = g_rows[:].bitcast(F32)
+                for u in range(2):
+                    nc.tensor.transpose(gt[:, u * P:(u + 1) * P], row_words[:, u * P:(u + 1) * P], ident[:])
+                mover = nc.vector.tensor_copy if GT[4 * h + ib] == "V" else nc.scalar.copy
+                mover(out=g_words[:, 256 * ib:256 * (ib + 1)].rearrange("p (i u) -> p i u", u=2),
+                      in_=gt[:, 0:256].rearrange("p (u i) -> p i u", u=2))
+                if ib % 2 == 1:
+                    quantize(g_grouped, codes, scales, E5M2, (ib - 1) * P, (ib + 1) * P)
+            g_codes.append(codes)
+            g_scales.append(scales)
+
+        quantize(*qr[1], E4M3, 0, D)
+        out_planes = out_0.rearrange("(p j) c -> p j c", j=PACK)
+        spans = []
+        for width in CHUNKS:
+            lo = sum(CHUNKS[:len(spans)])
+            spans.append(slice(lo, lo + width))
+        pairs = [held([P, 4 * width], BF16, "pairs%d" % c) for c, width in enumerate(CHUNKS)]
+        listed = []
+        for j in range(PACK):
+            blk = slice(j * P, (j + 1) * P)
+            dk = bank("a" if j % 2 == 0 else "c", 3)
+            for h in range(2):
+                nc.tensor.matmul_mx(out=dk[:], lhsT=qr_codes[h][:, blk].bitcast(E4M3), lhsT_scale=qr_scales[h][:, blk],
+                                    rhs=g_codes[h][:].bitcast(E5M2), rhs_scale=g_scales[h][:], start=(h == 0), stop=(h == 1))
+            t_ = held([P, SLOTS], F32, "dk%d" % j)
+            nc.scalar.copy(out=t_[:], in_=dk[:])
+            listed.append(t_)
+        y_codes = held([P, TOKENS], U32, "y_codes")
+        y_scales = held([P, TOKENS], U8, "y_scales")
+        words_out = out_1.rearrange("a p c t -> p (a c t)").bitcast(I32)
+        for j in range(PACK):
+            nc.vector.tensor_copy(out=windows[j][:].indirect(offsets[:]), in_=listed[j][:])
+            nc.sync.dma_start(out=out_planes[:, j, :], in_=windows[j][:])
+            for c, span in enumerate(spans):
+                view = pairs[c][:].rearrange("p (u c e) -> p u c e", u=2, e=2)
+                nc.scalar.copy(out=view[:, j // 2, :, j % 2], in_=windows[j][:, span])
+        for c, span in enumerate(spans):
+            y_grouped = held([P, CHUNKS[c] * PACK], BF16, "y_grouped%d" % c)
+            mover = nc.vector.tensor_copy if ILS[c] == "V" else nc.scalar.copy
+            mover(out=y_grouped[:].bitcast(F32).rearrange("p (c i u) -> p c u i", u=2, i=4),
+                  in_=pairs[c][:].bitcast(F32).rearrange("p (u c i) -> p c u i", u=2, i=4))
+            nc.vector.quantize_mx(out=y_codes[:, span].bitcast(E4M3), scales=y_scales[:, span], in_=y_grouped[:])
+            nc.sync.dma_start(out=words_out[:, span], in_=y_codes[:, span].bitcast(I32))
+        scales_out = out_2.rearrange("a f c -> (a f) c").bitcast(I32)
+        for quad in range(4):
+            queue = nc.sync if quad % 2 == 0 else nc.scalar
+            queue.dma_start(out=scales_out[4 * quad:4 * quad + 4, :], in_=y_scales[32 * quad:32 * quad + 4, :].bitcast(I32))

@@ -24,8 +24,8 @@ BLOCKS = SLOTS // P
 ODD = 1023
 CHUNKS = (256, 512, 512, 512, 256)
 ILS = "VVVSV"
-MODES = "GGGGGGGM"
-GT = "SVSVSVSV"
+MODES = "SVVVGGGV"
+P3 = "SSSSS"
 FLOPS = 4 * 2 * D * R * SLOTS
 
 
@@ -33,7 +33,6 @@ def tile_attend_ggqa_sig_k_pl_kernel(tc, q1, q2, kT, dp1, dp2, us, ts, w1, w2, o
     nc = tc.nc
     with ExitStack() as ctx:
         keep = ctx.enter_context(tc.tile_pool(name="keep", bufs=1))
-        ring = ctx.enter_context(tc.tile_pool(name="ring", bufs=4))
         psum = ctx.enter_context(tc.psum_pool(name="psum", bufs=1))
 
         def held(shape, dtype, name, tag=None):
@@ -55,8 +54,7 @@ def tile_attend_ggqa_sig_k_pl_kernel(tc, q1, q2, kT, dp1, dp2, us, ts, w1, w2, o
             t_ = held([P, PACK, R], F32, "q_raw%d" % h)
             nc.sync.dma_start(out=t_[:], in_=q.rearrange("(p j) r -> p j r", j=PACK))
             q_raw.append(t_)
-            if h == 0:
-                nc.sync.dma_start(out=ts_row[0:1, :], in_=ts[0:1, :])
+        nc.sync.dma_start(out=ts_row[0:1, :], in_=ts[0:1, :])
         k_planes = kT.rearrange("(p j) c -> p j c", j=PACK)
         k_raw = []
         for j in range(PACK):
@@ -108,7 +106,7 @@ def tile_attend_ggqa_sig_k_pl_kernel(tc, q1, q2, kT, dp1, dp2, us, ts, w1, w2, o
             words = rounded[:].bitcast(F32)
             turned_words = qr[h][0][:].bitcast(F32)
             for half in range(2):
-                ps = bank("a", 3)
+                ps = bank("a", 4)
                 for jj in range(2):
                     j = 2 * half + jj
                     for u in range(2):
@@ -123,12 +121,11 @@ def tile_attend_ggqa_sig_k_pl_kernel(tc, q1, q2, kT, dp1, dp2, us, ts, w1, w2, o
         def gather_keys(j, lo, hi):
             nc.vector.tensor_copy(out=k_view[:, lo:hi, j], in_=k_raw[j][:].indirect(offsets[:, lo // 16:hi // 16]))
 
-        ps = bank("c", 3)
+        ps = bank("c", 4)
         for b in range(PACK):
             nc.tensor.transpose(ps[:, b * P:(b + 1) * P], us_col[:, b:b + 1].to_broadcast([P, P]), ident[:])
         us_half = held([P, R], F32, "us_half")
-        nc.scalar.activation(out=us_half[:].rearrange("p (u s e) -> p u s e", u=2, e=2),
-                             in_=ps[:].rearrange("p (u e s) -> p u s e", u=2, e=2), func=ACT.Copy, scale=0.5)
+        nc.scalar.activation(out=us_half[:], in_=ps[:], func=ACT.Copy, scale=0.5)
 
         group_along_d(0, nc.vector.tensor_copy)
         group_along_r(0)
@@ -136,7 +133,7 @@ def tile_attend_ggqa_sig_k_pl_kernel(tc, q1, q2, kT, dp1, dp2, us, ts, w1, w2, o
 
         ts_listed = held([P, SLOTS], F32, "ts_listed")
         nc.vector.tensor_copy(out=ts_listed[:], in_=ts_row[:].indirect(offsets[:]))
-        ps = bank("c", 3)
+        ps = bank("c", 4)
         for b in range(BLOCKS):
             nc.tensor.transpose(ps[:, b * P:(b + 1) * P], ts_listed[:, b * P:(b + 1) * P], ident[:])
         ts_col = held([P, BLOCKS], F32, "ts_col")
@@ -160,62 +157,52 @@ def tile_attend_ggqa_sig_k_pl_kernel(tc, q1, q2, kT, dp1, dp2, us, ts, w1, w2, o
         gather_keys(1, 0, SLOTS)
         quantize(*qd[1], E4M3, 0, R)
         gather_keys(2, 0, SLOTS)
+        quantize(*qr[1], E4M3, 0, D)
         for half in range(2):
             lo, hi = 256 * half, 256 * (half + 1)
             gather_keys(3, lo, hi)
             quantize(*keys, E4M3, lo, hi)
 
+        squares = []
+        for h in range(2):
+            for ib in range(BLOCKS):
+                blk = slice(ib * P, (ib + 1) * P)
+                score = bank("a", 4)
+                nc.tensor.matmul_mx(out=score[:], lhsT=k_codes[:, blk].bitcast(E4M3), lhsT_scale=k_scales[:, blk],
+                                    rhs=qd_codes[h][:].bitcast(E4M3), rhs_scale=qd_scales[h][:], start=True, stop=True)
+                arg = held([P, R], F32, "arg%d_%d" % (h, ib))
+                nc.vector.tensor_tensor(out=arg[:].rearrange("p (t s) -> p t s", t=PACK),
+                                        in0=score[:].rearrange("p (s t) -> p t s", t=PACK),
+                                        in1=us_half[:].rearrange("p (t s) -> p t s", t=PACK), op=ALU.mult)
+                nc.scalar.activation(out=arg[:], in_=arg[:], func=ACT.Tanh, scale=ts_col[:, ib:ib + 1])
+                nc.scalar.activation(out=arg[:], in_=arg[:], func=ACT.Square)
+                if MODES[4 * h + ib] == "S":
+                    nc.scalar.activation(out=arg[:], in_=arg[:], func=ACT.Identity, scale=ts_neg[:, ib:ib + 1], bias=ts_col[:, ib:ib + 1])
+                squares.append(arg)
         g_codes, g_scales = [], []
         for h in range(2):
             for b in range(PACK):
                 nc.gpsimd.tensor_scalar(out=dp_raw[h][:, b, :], in0=dp_raw[h][:, b, :], scalar1=gate[h][:, b:b + 1], scalar2=0.0, op0=ALU.mult, op1=ALU.add)
-            g_grouped = held([P, SLOTS * PACK], BF16, "g_grouped%d" % h)
-            g_words = g_grouped[:].bitcast(F32)
-            codes = held([P, SLOTS], U32, "g_codes%d" % h)
-            scales = held([P, SLOTS], U8, "g_scales%d" % h)
+            g_grouped, codes, scales = mx_tiles(SLOTS, "g%d" % h)
             for ib in range(BLOCKS):
                 blk = slice(ib * P, (ib + 1) * P)
-                score = bank("a", 3)
-                nc.tensor.matmul_mx(out=score[:], lhsT=k_codes[:, blk].bitcast(E4M3), lhsT_scale=k_scales[:, blk],
-                                    rhs=qd_codes[h][:].bitcast(E4M3), rhs_scale=qd_scales[h][:], start=True, stop=True)
-                arg = ring.tile([P, R], F32, name="arg")
-                nc.vector.tensor_tensor(out=arg[:].rearrange("p (u s e) -> p u s e", u=2, e=2),
-                                        in0=score[:].rearrange("p (s u e) -> p u s e", u=2, e=2),
-                                        in1=us_half[:].rearrange("p (u s e) -> p u s e", u=2, e=2), op=ALU.mult)
-                nc.scalar.activation(out=arg[:], in_=arg[:], func=ACT.Tanh, scale=ts_col[:, ib:ib + 1])
+                arg = squares[4 * h + ib]
                 mode = MODES[4 * h + ib]
-                dpt = bank("c", 3)
-                for b in range(PACK):
-                    nc.tensor.transpose(dpt[:, b * P:(b + 1) * P], dp_raw[h][:, b, blk], ident[:])
-                g_rows = ring.tile([P, R], BF16, name="g_rows", align_bytes=64)
-                if mode == "M":
-                    sq = ring.tile([P, R], F32, name="sq")
-                    nc.vector.scalar_tensor_tensor(out=sq[:], in0=arg[:], scalar=ts_neg[:, ib:ib + 1], in1=arg[:], op0=ALU.mult, op1=ALU.mult)
-                    for u in range(2):
-                        half = slice(256 * u, 256 * (u + 1))
-                        nc.vector.scalar_tensor_tensor(out=g_rows[:, half].rearrange("p (s e) -> p s e", e=2),
-                                                       in0=sq[:, half].rearrange("p (s e) -> p s e", e=2), scalar=ts_col[:, ib:ib + 1],
-                                                       in1=dpt[:, half].rearrange("p (e s) -> p s e", e=2), op0=ALU.add, op1=ALU.mult)
-                else:
-                    nc.scalar.activation(out=arg[:], in_=arg[:], func=ACT.Square)
+                if mode != "S":
                     eng = nc.gpsimd if mode == "G" else nc.vector
                     eng.tensor_scalar(out=arg[:], in0=arg[:], scalar1=ts_neg[:, ib:ib + 1], scalar2=ts_col[:, ib:ib + 1], op0=ALU.mult, op1=ALU.add)
-                    nc.vector.tensor_tensor(out=g_rows[:].rearrange("p (u s e) -> p u s e", u=2, e=2),
-                                            in0=arg[:].rearrange("p (u s e) -> p u s e", u=2, e=2),
-                                            in1=dpt[:].rearrange("p (u e s) -> p u s e", u=2, e=2), op=ALU.mult)
-                gt = bank("g", 2)
-                row_words = g_rows[:].bitcast(F32)
-                for u in range(2):
-                    nc.tensor.transpose(gt[:, u * P:(u + 1) * P], row_words[:, u * P:(u + 1) * P], ident[:])
-                mover = nc.vector.tensor_copy if GT[4 * h + ib] == "V" else nc.scalar.copy
-                mover(out=g_words[:, 256 * ib:256 * (ib + 1)].rearrange("p (i u) -> p i u", u=2),
-                      in_=gt[:, 0:256].rearrange("p (u i) -> p i u", u=2))
+                slope = bank("c", 4)
+                for t in range(PACK):
+                    nc.tensor.transpose(slope[:, t * P:(t + 1) * P], arg[:, t * P:(t + 1) * P], ident[:])
+                nc.vector.tensor_tensor(
+                    out=g_grouped[:, PACK * P * ib:PACK * P * (ib + 1)].rearrange("p (c i t) -> p c t i", i=4, t=PACK),
+                    in0=dp_raw[h][:, :, blk].rearrange("p t (c i) -> p c t i", i=4),
+                    in1=slope[:].rearrange("p (t c i) -> p c t i", i=4, t=PACK), op=ALU.mult)
                 if ib % 2 == 1:
                     quantize(g_grouped, codes, scales, E5M2, (ib - 1) * P, (ib + 1) * P)
             g_codes.append(codes)
             g_scales.append(scales)
 
-        quantize(*qr[1], E4M3, 0, D)
         out_planes = out_0.rearrange("(p j) c -> p j c", j=PACK)
         spans = []
         for width in CHUNKS:
@@ -225,7 +212,7 @@ def tile_attend_ggqa_sig_k_pl_kernel(tc, q1, q2, kT, dp1, dp2, us, ts, w1, w2, o
         listed = []
         for j in range(PACK):
             blk = slice(j * P, (j + 1) * P)
-            dk = bank("a" if j % 2 == 0 else "c", 3)
+            dk = bank("a", 4)
             for h in range(2):
                 nc.tensor.matmul_mx(out=dk[:], lhsT=qr_codes[h][:, blk].bitcast(E4M3), lhsT_scale=qr_scales[h][:, blk],
                                     rhs=g_codes[h][:].bitcast(E5M2), rhs_scale=g_scales[h][:], start=(h == 0), stop=(h == 1))
@@ -240,7 +227,8 @@ def tile_attend_ggqa_sig_k_pl_kernel(tc, q1, q2, kT, dp1, dp2, us, ts, w1, w2, o
             nc.sync.dma_start(out=out_planes[:, j, :], in_=windows[j][:])
             for c, span in enumerate(spans):
                 view = pairs[c][:].rearrange("p (u c e) -> p u c e", u=2, e=2)
-                nc.scalar.copy(out=view[:, j // 2, :, j % 2], in_=windows[j][:, span])
+                mover = nc.vector.tensor_copy if j == 3 and P3[c] == "V" else nc.scalar.copy
+                mover(out=view[:, j // 2, :, j % 2], in_=windows[j][:, span])
         for c, span in enumerate(spans):
             y_grouped = held([P, CHUNKS[c] * PACK], BF16, "y_grouped%d" % c)
             mover = nc.vector.tensor_copy if ILS[c] == "V" else nc.scalar.copy

@@ -21,10 +21,9 @@ SLOTS = 512
 TOKENS = 2048
 PACK = 4
 BLOCKS = SLOTS // P
-ODD = 1023
-CHUNKS = (256, 512, 512, 512, 256)
-ILS = "VVVSV"
-MODES = "SVVVGGGV"
+CHUNKS = (256, 512, 512, 256, 512)
+ILS = "VVVVS"
+MODES = "GGVVVVVV"
 P3 = "SSSSS"
 FLOPS = 4 * 2 * D * R * SLOTS
 
@@ -38,17 +37,13 @@ def tile_attend_ggqa_sig_k_pl_kernel(tc, q1, q2, kT, dp1, dp2, us, ts, w1, w2, o
         def held(shape, dtype, name, tag=None):
             return keep.tile(shape, dtype, name=name, tag=tag or name, align_bytes=64)
 
-        def zero_on_vector(tile_):
-            nc.vector.memset(tile_[:, :ODD], 0.0)
-            nc.vector.memset(tile_[:, ODD:], 0.0)
-
         def bank(tag, bufs):
             return psum.tile([P, 512], F32, name=tag, tag=tag, bufs=bufs)
 
         offsets = keep.tile([P, SLOTS // 16], U16, name="offsets")
         nc.sync.dma_start(offsets[:], offs)
         ts_row = held([P, TOKENS], F32, "ts_row")
-        zero_on_vector(ts_row)
+        nc.vector.memset(ts_row[:], 0.0)
         q_raw = []
         for h, q in enumerate((q1, q2)):
             t_ = held([P, PACK, R], F32, "q_raw%d" % h)
@@ -76,10 +71,15 @@ def tile_attend_ggqa_sig_k_pl_kernel(tc, q1, q2, kT, dp1, dp2, us, ts, w1, w2, o
 
         ident = held([P, P], F32, "ident")
         make_identity(nc, ident[:])
-        windows = [held([P, TOKENS], F32, "window%d" % j) for j in range(PACK - 1)]
-        zero_on_vector(windows[0])
-        for j in (1, 2):
-            nc.gpsimd.memset(windows[j][:], 0.0)
+        windows = [held([P, TOKENS], F32, "window%d" % j) for j in range(2)]
+        nc.vector.memset(windows[0][:], 0.0)
+        nc.gpsimd.memset(windows[1][:], 0.0)
+
+        def late_window(h):
+            t_ = held([P, TOKENS], F32, "window%d" % (2 + h), tag="q_raw%d" % h)
+            for part in range(4):
+                nc.gpsimd.memset(t_[:, 512 * part:512 * (part + 1)], 0.0)
+            windows.append(t_)
 
         def quantize(grouped, codes, scales, fmt, lo, hi):
             nc.vector.quantize_mx(out=codes[:, lo:hi].bitcast(fmt), scales=scales[:, lo:hi],
@@ -147,26 +147,26 @@ def tile_attend_ggqa_sig_k_pl_kernel(tc, q1, q2, kT, dp1, dp2, us, ts, w1, w2, o
                                            op0=ALU.mult, op1=ALU.mult)
             gate.append(t_)
 
-        windows.append(held([P, TOKENS], F32, "window3", tag="q_raw0"))
-        for part in range(4):
-            nc.gpsimd.memset(windows[3][:, 512 * part:512 * (part + 1)], 0.0)
+        late_window(0)
         group_along_d(1, nc.scalar.copy)
         group_along_r(1)
-        gather_keys(0, 0, SLOTS)
+        late_window(1)
+        k_pair = held([P, 2, SLOTS], BF16, "k_pair")
+        nc.vector.tensor_copy(out=k_pair[:, 0, :], in_=k_raw[0][:].indirect(offsets[:]))
         quantize(*qr[0], E4M3, 0, D)
-        gather_keys(1, 0, SLOTS)
+        nc.vector.tensor_copy(out=k_pair[:, 1, :], in_=k_raw[1][:].indirect(offsets[:]))
+        nc.scalar.copy(out=k_view[:, :, 0:2], in_=k_pair[:].rearrange("p e c -> p c e"))
         quantize(*qd[1], E4M3, 0, R)
         gather_keys(2, 0, SLOTS)
         quantize(*qr[1], E4M3, 0, D)
-        for half in range(2):
-            lo, hi = 256 * half, 256 * (half + 1)
-            gather_keys(3, lo, hi)
-            quantize(*keys, E4M3, lo, hi)
 
         squares = []
         for h in range(2):
             for ib in range(BLOCKS):
                 blk = slice(ib * P, (ib + 1) * P)
+                if h == 0 and ib % 2 == 0:
+                    gather_keys(3, ib * P, (ib + 2) * P)
+                    quantize(*keys, E4M3, ib * P, (ib + 2) * P)
                 score = bank("a", 4)
                 nc.tensor.matmul_mx(out=score[:], lhsT=k_codes[:, blk].bitcast(E4M3), lhsT_scale=k_scales[:, blk],
                                     rhs=qd_codes[h][:].bitcast(E4M3), rhs_scale=qd_scales[h][:], start=True, stop=True)
@@ -198,7 +198,9 @@ def tile_attend_ggqa_sig_k_pl_kernel(tc, q1, q2, kT, dp1, dp2, us, ts, w1, w2, o
                     out=g_grouped[:, PACK * P * ib:PACK * P * (ib + 1)].rearrange("p (c i t) -> p c t i", i=4, t=PACK),
                     in0=dp_raw[h][:, :, blk].rearrange("p t (c i) -> p c t i", i=4),
                     in1=slope[:].rearrange("p (t c i) -> p c t i", i=4, t=PACK), op=ALU.mult)
-                if ib % 2 == 1:
+                if h == 1 and ib >= 2:
+                    quantize(g_grouped, codes, scales, E5M2, ib * P, (ib + 1) * P)
+                elif ib % 2 == 1:
                     quantize(g_grouped, codes, scales, E5M2, (ib - 1) * P, (ib + 1) * P)
             g_codes.append(codes)
             g_scales.append(scales)
@@ -230,12 +232,15 @@ def tile_attend_ggqa_sig_k_pl_kernel(tc, q1, q2, kT, dp1, dp2, us, ts, w1, w2, o
                 mover = nc.vector.tensor_copy if j == 3 and P3[c] == "V" else nc.scalar.copy
                 mover(out=view[:, j // 2, :, j % 2], in_=windows[j][:, span])
         for c, span in enumerate(spans):
-            y_grouped = held([P, CHUNKS[c] * PACK], BF16, "y_grouped%d" % c)
+            width = CHUNKS[c] if ILS[c] == "V" else 256
             mover = nc.vector.tensor_copy if ILS[c] == "V" else nc.scalar.copy
-            mover(out=y_grouped[:].bitcast(F32).rearrange("p (c i u) -> p c u i", u=2, i=4),
-                  in_=pairs[c][:].bitcast(F32).rearrange("p (u c i) -> p c u i", u=2, i=4))
-            nc.vector.quantize_mx(out=y_codes[:, span].bitcast(E4M3), scales=y_scales[:, span], in_=y_grouped[:])
-            nc.sync.dma_start(out=words_out[:, span], in_=y_codes[:, span].bitcast(I32))
+            pair_words = pairs[c][:].bitcast(F32).rearrange("p (u c) -> p c u", u=2)
+            for lo in range(0, CHUNKS[c], width):
+                y_grouped = held([P, width * PACK], BF16, "y_grouped%d_%d" % (c, lo))
+                mover(out=y_grouped[:].bitcast(F32).rearrange("p (c u) -> p c u", u=2), in_=pair_words[:, lo:lo + width, :])
+                part = slice(span.start + lo, span.start + lo + width)
+                nc.vector.quantize_mx(out=y_codes[:, part].bitcast(E4M3), scales=y_scales[:, part], in_=y_grouped[:])
+                nc.sync.dma_start(out=words_out[:, part], in_=y_codes[:, part].bitcast(I32))
         scales_out = out_2.rearrange("a f c -> (a f) c").bitcast(I32)
         for quad in range(4):
             queue = nc.sync if quad % 2 == 0 else nc.scalar

@@ -23,8 +23,7 @@ PACK = 4
 BLOCKS = SLOTS // P
 CHUNKS = (256, 512, 512, 256, 512)
 ILS = "VVVVS"
-MODES = "GGVVVVVV"
-P3 = "SSSSS"
+MODES = "VVVVGGGV"
 FLOPS = 4 * 2 * D * R * SLOTS
 
 
@@ -42,44 +41,49 @@ def tile_attend_ggqa_sig_k_pl_kernel(tc, q1, q2, kT, dp1, dp2, us, ts, w1, w2, o
 
         offsets = keep.tile([P, SLOTS // 16], U16, name="offsets")
         nc.sync.dma_start(offsets[:], offs)
-        ts_row = held([P, TOKENS], F32, "ts_row")
-        nc.vector.memset(ts_row[:], 0.0)
+        ts_runs = held([P, TOKENS // P], F32, "ts_runs")
+        nc.sync.dma_start(out=ts_runs[:], in_=ts[0:1, :].rearrange("o (p c) -> p (o c)", p=P))
+
+        def load_column(name, vec):
+            t_ = held([P, PACK], F32, name)
+            nc.sync.dma_start(out=t_[:], in_=vec.rearrange("(p b) o -> p (b o)", b=PACK))
+            return t_
+
+        us_col = load_column("us_col", us)
         q_raw = []
         for h, q in enumerate((q1, q2)):
             t_ = held([P, PACK, R], F32, "q_raw%d" % h)
             nc.sync.dma_start(out=t_[:], in_=q.rearrange("(p j) r -> p j r", j=PACK))
             q_raw.append(t_)
-        nc.sync.dma_start(out=ts_row[0:1, :], in_=ts[0:1, :])
         k_planes = kT.rearrange("(p j) c -> p j c", j=PACK)
         k_raw = []
         for j in range(PACK):
             t_ = held([P, TOKENS], F32, "k_raw%d" % j)
             nc.sync.dma_start(out=t_[:], in_=k_planes[:, j, :])
             k_raw.append(t_)
+        cols = [us_col, load_column("w1_col", w1), load_column("w2_col", w2)]
         dp_raw = []
         for h, dp in enumerate((dp1, dp2)):
             t_ = held([P, PACK, SLOTS], F32, "dp_raw%d" % h)
             nc.sync.dma_start(out=t_[:], in_=dp.rearrange("(p b) i -> p b i", b=PACK))
             dp_raw.append(t_)
 
-        cols = []
-        for name, vec in (("us_col", us), ("w1_col", w1), ("w2_col", w2)):
-            t_ = held([P, PACK], F32, name)
-            nc.scalar.dma_start(out=t_[:], in_=vec.rearrange("(p b) o -> p (b o)", b=PACK))
-            cols.append(t_)
-        us_col = cols[0]
-
         ident = held([P, P], F32, "ident")
         make_identity(nc, ident[:])
-        windows = [held([P, TOKENS], F32, "window%d" % j) for j in range(2)]
-        nc.vector.memset(windows[0][:], 0.0)
-        nc.gpsimd.memset(windows[1][:], 0.0)
+        windows = [held([P, TOKENS], F32, "window%d" % j) for j in range(PACK)]
+        for j, lo, hi in ((0, 0, 1025), (0, 1025, TOKENS), (1, 0, 513), (1, 513, 1024)):
+            nc.vector.memset(windows[j][:, lo:hi], 0.0)
+        nc.gpsimd.memset(windows[2][:], 0.0)
+        nc.gpsimd.memset(windows[3][:], 0.0)
+        nc.gpsimd.memset(windows[1][:, 1024:TOKENS], 0.0)
 
-        def late_window(h):
-            t_ = held([P, TOKENS], F32, "window%d" % (2 + h), tag="q_raw%d" % h)
-            for part in range(4):
-                nc.gpsimd.memset(t_[:, 512 * part:512 * (part + 1)], 0.0)
-            windows.append(t_)
+        ts_row = held([P, TOKENS], F32, "ts_row")
+        for b in range(4):
+            ps = bank("c", 4)
+            for c in range(4):
+                nc.tensor.transpose(ps[:, c * P:(c + 1) * P], ts_runs[:, 4 * b + c:4 * b + c + 1].to_broadcast([P, P]), ident[:])
+            nc.scalar.copy(out=ts_row[:].rearrange("m (p b c) -> m p b c", b=4, c=4)[:, :, b, :],
+                           in_=ps[:].rearrange("m (c p) -> m p c", c=4))
 
         def quantize(grouped, codes, scales, fmt, lo, hi):
             nc.vector.quantize_mx(out=codes[:, lo:hi].bitcast(fmt), scales=scales[:, lo:hi],
@@ -91,32 +95,22 @@ def tile_attend_ggqa_sig_k_pl_kernel(tc, q1, q2, kT, dp1, dp2, us, ts, w1, w2, o
 
         qd = [mx_tiles(R, "qd%d" % h) for h in range(2)]
         qr = [mx_tiles(D, "qr%d" % h) for h in range(2)]
-        keys = mx_tiles(SLOTS, "k")
         qd_codes, qd_scales = [t_[1] for t_ in qd], [t_[2] for t_ in qd]
         qr_codes, qr_scales = [t_[1] for t_ in qr], [t_[2] for t_ in qr]
-        k_grouped, k_codes, k_scales = keys
 
         def group_along_d(h, mover):
-            mover(out=qd[h][0][:].rearrange("p (c i t) -> p c t i", i=4, t=PACK),
-                  in_=q_raw[h][:].rearrange("p t (c i) -> p c t i", i=4))
+            mover(out=qd[h][0][:].rearrange("p (i m t) -> p m t i", i=PACK, t=PACK),
+                  in_=q_raw[h][:].rearrange("p t (m i) -> p m t i", i=PACK))
 
         def group_along_r(h):
-            rounded = held([P, PACK * R], BF16, "q_rounded%d" % h)
-            nc.scalar.copy(out=rounded[:], in_=q_raw[h][:].rearrange("p j r -> p (j r)"))
-            words = rounded[:].bitcast(F32)
-            turned_words = qr[h][0][:].bitcast(F32)
-            for half in range(2):
+            words = qd[h][0][:].bitcast(F32)
+            for u in range(2):
                 ps = bank("a", 4)
-                for jj in range(2):
-                    j = 2 * half + jj
-                    for u in range(2):
-                        nc.tensor.transpose(ps[:, (2 * jj + u) * P:(2 * jj + u + 1) * P],
-                                            words[:, 256 * j + u:256 * (j + 1):2], ident[:])
+                for i in range(PACK):
+                    nc.tensor.transpose(ps[:, i * P:(i + 1) * P], words[:, 256 * i + u:256 * (i + 1):2], ident[:])
                 nc.scalar.copy(
-                    out=turned_words[:, 512 * half:512 * (half + 1)].rearrange("p (j m u) -> p j m u", j=2, u=2),
-                    in_=ps[:].rearrange("p (j u m) -> p j m u", j=2, u=2))
-
-        k_view = k_grouped[:].rearrange("p (c t) -> p c t", t=PACK)
+                    out=qr[h][0][:, 1024 * u:1024 * (u + 1)].rearrange("m (e p i) -> m e p i", e=2, i=PACK),
+                    in_=ps[:].bitcast(BF16).rearrange("m (i p e) -> m e p i", i=PACK, e=2))
 
         def gather_keys(j, lo, hi):
             nc.vector.tensor_copy(out=k_view[:, lo:hi, j], in_=k_raw[j][:].indirect(offsets[:, lo // 16:hi // 16]))
@@ -133,32 +127,36 @@ def tile_attend_ggqa_sig_k_pl_kernel(tc, q1, q2, kT, dp1, dp2, us, ts, w1, w2, o
 
         ts_listed = held([P, SLOTS], F32, "ts_listed")
         nc.vector.tensor_copy(out=ts_listed[:], in_=ts_row[:].indirect(offsets[:]))
+        gate = []
+        for h in range(2):
+            t_ = held([P, PACK], F32, "gate%d" % h)
+            nc.gpsimd.tensor_tensor(out=t_[:], in0=cols[1 + h][:], in1=us_col[:], op=ALU.mult)
+            gate.append(t_)
+
+        group_along_d(1, nc.vector.tensor_copy)
+        group_along_r(1)
+        quantize(*qd[1], E4M3, 0, R)
+        quantize(*qr[0], E4M3, 0, D)
+        k_pair = held([P, 2, SLOTS], BF16, "k_pair", tag="qr0_grouped")
+        for j in range(2):
+            nc.vector.tensor_copy(out=k_pair[:, j, :], in_=k_raw[j][:].indirect(offsets[:]))
+        quantize(*qr[1], E4M3, 0, D)
+        k_grouped = held([P, SLOTS * PACK], BF16, "k_grouped", tag="qr1_grouped")
+        k_codes = held([P, SLOTS], U32, "k_codes")
+        k_scales = held([P, SLOTS], U8, "k_scales")
+        keys = (k_grouped, k_codes, k_scales)
+        k_view = k_grouped[:].rearrange("p (c t) -> p c t", t=PACK)
+        nc.scalar.copy(out=k_view[:, :, 0:2], in_=k_pair[:].rearrange("p e c -> p c e"))
+        gather_keys(2, 0, SLOTS)
         ps = bank("c", 4)
         for b in range(BLOCKS):
             nc.tensor.transpose(ps[:, b * P:(b + 1) * P], ts_listed[:, b * P:(b + 1) * P], ident[:])
         ts_col = held([P, BLOCKS], F32, "ts_col")
         nc.scalar.copy(out=ts_col[:], in_=ps[:, 0:512:P])
         ts_neg = held([P, BLOCKS], F32, "ts_neg")
-        nc.scalar.activation(out=ts_neg[:], in_=ps[:, 0:512:P], func=ACT.Copy, scale=-1.0)
-        gate = []
-        for h in range(2):
-            t_ = held([P, PACK], F32, "gate%d" % h)
-            nc.vector.scalar_tensor_tensor(out=t_[:], in0=cols[1 + h][:], scalar=0.25, in1=us_col[:],
-                                           op0=ALU.mult, op1=ALU.mult)
-            gate.append(t_)
-
-        late_window(0)
-        group_along_d(1, nc.scalar.copy)
-        group_along_r(1)
-        late_window(1)
-        k_pair = held([P, 2, SLOTS], BF16, "k_pair")
-        nc.vector.tensor_copy(out=k_pair[:, 0, :], in_=k_raw[0][:].indirect(offsets[:]))
-        quantize(*qr[0], E4M3, 0, D)
-        nc.vector.tensor_copy(out=k_pair[:, 1, :], in_=k_raw[1][:].indirect(offsets[:]))
-        nc.scalar.copy(out=k_view[:, :, 0:2], in_=k_pair[:].rearrange("p e c -> p c e"))
-        quantize(*qd[1], E4M3, 0, R)
-        gather_keys(2, 0, SLOTS)
-        quantize(*qr[1], E4M3, 0, D)
+        nc.scalar.activation(out=ts_neg[:], in_=ps[:, 0:512:P], func=ACT.Copy, scale=-0.25)
+        ts_pos = held([P, BLOCKS], F32, "ts_pos")
+        nc.scalar.activation(out=ts_pos[:], in_=ps[:, 0:512:P], func=ACT.Copy, scale=0.25)
 
         squares = []
         for h in range(2):
@@ -171,26 +169,38 @@ def tile_attend_ggqa_sig_k_pl_kernel(tc, q1, q2, kT, dp1, dp2, us, ts, w1, w2, o
                 nc.tensor.matmul_mx(out=score[:], lhsT=k_codes[:, blk].bitcast(E4M3), lhsT_scale=k_scales[:, blk],
                                     rhs=qd_codes[h][:].bitcast(E4M3), rhs_scale=qd_scales[h][:], start=True, stop=True)
                 arg = held([P, R], F32, "arg%d_%d" % (h, ib))
-                nc.vector.tensor_tensor(out=arg[:].rearrange("p (t s) -> p t s", t=PACK),
-                                        in0=score[:].rearrange("p (s t) -> p t s", t=PACK),
-                                        in1=us_half[:].rearrange("p (t s) -> p t s", t=PACK), op=ALU.mult)
+                nc.vector.tensor_tensor(out=arg[:], in0=score[:], in1=us_half[:], op=ALU.mult)
                 nc.scalar.activation(out=arg[:], in_=arg[:], func=ACT.Tanh, scale=ts_col[:, ib:ib + 1])
                 nc.scalar.activation(out=arg[:], in_=arg[:], func=ACT.Square)
                 if MODES[4 * h + ib] == "S":
-                    nc.scalar.activation(out=arg[:], in_=arg[:], func=ACT.Identity, scale=ts_neg[:, ib:ib + 1], bias=ts_col[:, ib:ib + 1])
+                    nc.scalar.activation(out=arg[:], in_=arg[:], func=ACT.Identity, scale=ts_neg[:, ib:ib + 1], bias=ts_pos[:, ib:ib + 1])
                 squares.append(arg)
-        g_codes, g_scales = [], []
         for h in range(2):
             for b in range(PACK):
                 nc.gpsimd.tensor_scalar(out=dp_raw[h][:, b, :], in0=dp_raw[h][:, b, :], scalar1=gate[h][:, b:b + 1], scalar2=0.0, op0=ALU.mult, op1=ALU.add)
-            g_grouped, codes, scales = mx_tiles(SLOTS, "g%d" % h)
+        g_all_codes = held([P, 2 * SLOTS], U32, "g_codes")
+        g_all_scales = held([P, 2 * SLOTS], U8, "g_scales")
+        HALF = SLOTS // 2
+
+        def product(ps, h, j, lo, start, stop):
+            blk = slice(j * P, (j + 1) * P)
+            nc.tensor.matmul_mx(out=ps[:], lhsT=qr_codes[h][:, blk].bitcast(E4M3), lhsT_scale=qr_scales[h][:, blk],
+                                rhs=g_all_codes[:, lo:lo + SLOTS].bitcast(E5M2), rhs_scale=g_all_scales[:, lo:lo + SLOTS],
+                                start=start, stop=stop)
+
+        first_part = held([P, SLOTS], F32, "first_part")
+        second_part = []
+        for h in range(2):
+            g_grouped = held([P, SLOTS * PACK], BF16, "g%d_grouped" % h)
+            codes = g_all_codes[:, h * SLOTS:(h + 1) * SLOTS]
+            scales = g_all_scales[:, h * SLOTS:(h + 1) * SLOTS]
             for ib in range(BLOCKS):
                 blk = slice(ib * P, (ib + 1) * P)
                 arg = squares[4 * h + ib]
                 mode = MODES[4 * h + ib]
                 if mode != "S":
                     eng = nc.gpsimd if mode == "G" else nc.vector
-                    eng.tensor_scalar(out=arg[:], in0=arg[:], scalar1=ts_neg[:, ib:ib + 1], scalar2=ts_col[:, ib:ib + 1], op0=ALU.mult, op1=ALU.add)
+                    eng.tensor_scalar(out=arg[:], in0=arg[:], scalar1=ts_neg[:, ib:ib + 1], scalar2=ts_pos[:, ib:ib + 1], op0=ALU.mult, op1=ALU.add)
                 slope = bank("c", 4)
                 for t in range(PACK):
                     nc.tensor.transpose(slope[:, t * P:(t + 1) * P], arg[:, t * P:(t + 1) * P], ident[:])
@@ -202,22 +212,34 @@ def tile_attend_ggqa_sig_k_pl_kernel(tc, q1, q2, kT, dp1, dp2, us, ts, w1, w2, o
                     quantize(g_grouped, codes, scales, E5M2, ib * P, (ib + 1) * P)
                 elif ib % 2 == 1:
                     quantize(g_grouped, codes, scales, E5M2, (ib - 1) * P, (ib + 1) * P)
-            g_codes.append(codes)
-            g_scales.append(scales)
+                if h == 0 and ib == 3:
+                    ps = bank("a", 4)
+                    product(ps, 0, 0, 0, True, True)
+                    nc.scalar.copy(out=first_part[:], in_=ps[:])
+                if h == 1 and ib == 1:
+                    ps = bank("a", 4)
+                    product(ps, 1, 0, HALF, True, True)
+                    early = ps
 
         out_planes = out_0.rearrange("(p j) c -> p j c", j=PACK)
         spans = []
         for width in CHUNKS:
             lo = sum(CHUNKS[:len(spans)])
             spans.append(slice(lo, lo + width))
-        pairs = [held([P, 4 * width], BF16, "pairs%d" % c) for c, width in enumerate(CHUNKS)]
-        listed = []
-        for j in range(PACK):
-            blk = slice(j * P, (j + 1) * P)
+        pairs = held([P, PACK * TOKENS], BF16, "pairs")
+        pair_view = pairs[:].rearrange("p (u c e) -> p u c e", u=2, e=2)
+        pair_words = pairs[:].bitcast(F32).rearrange("p (u c) -> p c u", u=2)
+        second_part.append(held([P, HALF], F32, "second_low", tag="dp_raw1"))
+        nc.scalar.copy(out=second_part[0][:], in_=early[:, HALF:SLOTS])
+        ps = bank("a", 4)
+        product(ps, 1, 0, SLOTS, True, True)
+        second_part.append(held([P, HALF], F32, "second_high"))
+        nc.scalar.copy(out=second_part[1][:], in_=ps[:, HALF:SLOTS])
+        listed = [None]
+        for j in range(1, PACK):
             dk = bank("a", 4)
             for h in range(2):
-                nc.tensor.matmul_mx(out=dk[:], lhsT=qr_codes[h][:, blk].bitcast(E4M3), lhsT_scale=qr_scales[h][:, blk],
-                                    rhs=g_codes[h][:].bitcast(E5M2), rhs_scale=g_scales[h][:], start=(h == 0), stop=(h == 1))
+                product(dk, h, j, h * SLOTS, h == 0, h == 1)
             t_ = held([P, SLOTS], F32, "dk%d" % j)
             nc.scalar.copy(out=t_[:], in_=dk[:])
             listed.append(t_)
@@ -225,19 +247,21 @@ def tile_attend_ggqa_sig_k_pl_kernel(tc, q1, q2, kT, dp1, dp2, us, ts, w1, w2, o
         y_scales = held([P, TOKENS], U8, "y_scales")
         words_out = out_1.rearrange("a p c t -> p (a c t)").bitcast(I32)
         for j in range(PACK):
-            nc.vector.tensor_copy(out=windows[j][:].indirect(offsets[:]), in_=listed[j][:])
+            if j == 0:
+                for lo in (0, HALF):
+                    nc.vector.tensor_tensor(out=windows[0][:].indirect(offsets[:, lo // 16:(lo + HALF) // 16]),
+                                            in0=first_part[:, lo:lo + HALF], in1=second_part[lo // HALF][:], op=ALU.add)
+            else:
+                nc.vector.tensor_copy(out=windows[j][:].indirect(offsets[:]), in_=listed[j][:])
             nc.sync.dma_start(out=out_planes[:, j, :], in_=windows[j][:])
-            for c, span in enumerate(spans):
-                view = pairs[c][:].rearrange("p (u c e) -> p u c e", u=2, e=2)
-                mover = nc.vector.tensor_copy if j == 3 and P3[c] == "V" else nc.scalar.copy
-                mover(out=view[:, j // 2, :, j % 2], in_=windows[j][:, span])
+            for span in (spans if j == PACK - 1 else [slice(0, TOKENS)]):
+                nc.scalar.copy(out=pair_view[:, j // 2, span, j % 2], in_=windows[j][:, span])
         for c, span in enumerate(spans):
             width = CHUNKS[c] if ILS[c] == "V" else 256
             mover = nc.vector.tensor_copy if ILS[c] == "V" else nc.scalar.copy
-            pair_words = pairs[c][:].bitcast(F32).rearrange("p (u c) -> p c u", u=2)
             for lo in range(0, CHUNKS[c], width):
                 y_grouped = held([P, width * PACK], BF16, "y_grouped%d_%d" % (c, lo))
-                mover(out=y_grouped[:].bitcast(F32).rearrange("p (c u) -> p c u", u=2), in_=pair_words[:, lo:lo + width, :])
+                mover(out=y_grouped[:].bitcast(F32).rearrange("p (c u) -> p c u", u=2), in_=pair_words[:, span.start + lo:span.start + lo + width, :])
                 part = slice(span.start + lo, span.start + lo + width)
                 nc.vector.quantize_mx(out=y_codes[:, part].bitcast(E4M3), scales=y_scales[:, part], in_=y_grouped[:])
                 nc.sync.dma_start(out=words_out[:, part], in_=y_codes[:, part].bitcast(I32))

@@ -41,8 +41,13 @@ def tile_attend_ggqa_sig_k_pl_kernel(tc, q1, q2, kT, dp1, dp2, us, ts, w1, w2, o
 
         offsets = keep.tile([P, SLOTS // 16], U16, name="offsets")
         nc.sync.dma_start(offsets[:], offs)
-        ts_runs = held([P, TOKENS // P], F32, "ts_runs")
-        nc.sync.dma_start(out=ts_runs[:], in_=ts[0:1, :].rearrange("o (p c) -> p (o c)", p=P))
+        ts_row = held([P, TOKENS], F32, "ts_row")
+
+        def zero_beside_gpsimd(t_):
+            nc.vector.memset(t_[:, 0:1025], 0.0)
+            nc.vector.memset(t_[:, 1025:TOKENS], 0.0)
+
+        zero_beside_gpsimd(ts_row)
 
         def load_column(name, vec):
             t_ = held([P, PACK], F32, name)
@@ -55,6 +60,8 @@ def tile_attend_ggqa_sig_k_pl_kernel(tc, q1, q2, kT, dp1, dp2, us, ts, w1, w2, o
             t_ = held([P, PACK, R], F32, "q_raw%d" % h)
             nc.sync.dma_start(out=t_[:], in_=q.rearrange("(p j) r -> p j r", j=PACK))
             q_raw.append(t_)
+            if h == 0:
+                nc.sync.dma_start(out=ts_row[0:1, :], in_=ts[0:1, :])
         k_planes = kT.rearrange("(p j) c -> p j c", j=PACK)
         k_raw = []
         for j in range(PACK):
@@ -70,20 +77,10 @@ def tile_attend_ggqa_sig_k_pl_kernel(tc, q1, q2, kT, dp1, dp2, us, ts, w1, w2, o
 
         ident = held([P, P], F32, "ident")
         make_identity(nc, ident[:])
-        windows = [held([P, TOKENS], F32, "window%d" % j) for j in range(PACK)]
-        for j, lo, hi in ((0, 0, 1025), (0, 1025, TOKENS), (1, 0, 513), (1, 513, 1024)):
-            nc.vector.memset(windows[j][:, lo:hi], 0.0)
+        windows = [held([P, TOKENS], F32, "window%d" % j) for j in range(PACK - 1)]
+        zero_beside_gpsimd(windows[0])
+        nc.gpsimd.memset(windows[1][:], 0.0)
         nc.gpsimd.memset(windows[2][:], 0.0)
-        nc.gpsimd.memset(windows[3][:], 0.0)
-        nc.gpsimd.memset(windows[1][:, 1024:TOKENS], 0.0)
-
-        ts_row = held([P, TOKENS], F32, "ts_row")
-        for b in range(4):
-            ps = bank("c", 4)
-            for c in range(4):
-                nc.tensor.transpose(ps[:, c * P:(c + 1) * P], ts_runs[:, 4 * b + c:4 * b + c + 1].to_broadcast([P, P]), ident[:])
-            nc.scalar.copy(out=ts_row[:].rearrange("m (p b c) -> m p b c", b=4, c=4)[:, :, b, :],
-                           in_=ps[:].rearrange("m (c p) -> m p c", c=4))
 
         def quantize(grouped, codes, scales, fmt, lo, hi):
             nc.vector.quantize_mx(out=codes[:, lo:hi].bitcast(fmt), scales=scales[:, lo:hi],
@@ -98,19 +95,29 @@ def tile_attend_ggqa_sig_k_pl_kernel(tc, q1, q2, kT, dp1, dp2, us, ts, w1, w2, o
         qd_codes, qd_scales = [t_[1] for t_ in qd], [t_[2] for t_ in qd]
         qr_codes, qr_scales = [t_[1] for t_ in qr], [t_[2] for t_ in qr]
 
-        def group_along_d(h, mover):
-            mover(out=qd[h][0][:].rearrange("p (i m t) -> p m t i", i=PACK, t=PACK),
-                  in_=q_raw[h][:].rearrange("p t (m i) -> p m t i", i=PACK))
+        def group_along_d(h, mover, lo=0, hi=P):
+            mover(out=qd[h][0][:].rearrange("p (c i t) -> p c t i", i=4, t=PACK)[:, lo:hi],
+                  in_=q_raw[h][:].rearrange("p t (c i) -> p c t i", i=4)[:, lo:hi])
+
+        rounded = []
+        for h in range(2):
+            t_ = held([P, PACK * R], BF16, "q_rounded%d" % h)
+            nc.scalar.copy(out=t_[:], in_=q_raw[h][:].rearrange("p j r -> p (j r)"))
+            rounded.append(t_)
 
         def group_along_r(h):
-            words = qd[h][0][:].bitcast(F32)
-            for u in range(2):
+            words = rounded[h][:].bitcast(F32)
+            turned_words = qr[h][0][:].bitcast(F32)
+            for half in range(2):
                 ps = bank("a", 4)
-                for i in range(PACK):
-                    nc.tensor.transpose(ps[:, i * P:(i + 1) * P], words[:, 256 * i + u:256 * (i + 1):2], ident[:])
+                for jj in range(2):
+                    j = 2 * half + jj
+                    for u in range(2):
+                        nc.tensor.transpose(ps[:, (2 * jj + u) * P:(2 * jj + u + 1) * P],
+                                            words[:, 256 * j + u:256 * (j + 1):2], ident[:])
                 nc.scalar.copy(
-                    out=qr[h][0][:, 1024 * u:1024 * (u + 1)].rearrange("m (e p i) -> m e p i", e=2, i=PACK),
-                    in_=ps[:].bitcast(BF16).rearrange("m (i p e) -> m e p i", i=PACK, e=2))
+                    out=turned_words[:, 512 * half:512 * (half + 1)].rearrange("p (j m u) -> p j m u", j=2, u=2),
+                    in_=ps[:].rearrange("p (j u m) -> p j m u", j=2, u=2))
 
         def gather_keys(j, lo, hi):
             nc.vector.tensor_copy(out=k_view[:, lo:hi, j], in_=k_raw[j][:].indirect(offsets[:, lo // 16:hi // 16]))
@@ -137,7 +144,7 @@ def tile_attend_ggqa_sig_k_pl_kernel(tc, q1, q2, kT, dp1, dp2, us, ts, w1, w2, o
         group_along_r(1)
         quantize(*qd[1], E4M3, 0, R)
         quantize(*qr[0], E4M3, 0, D)
-        k_pair = held([P, 2, SLOTS], BF16, "k_pair", tag="qr0_grouped")
+        k_pair = held([P, 2, SLOTS], BF16, "k_pair", tag="ts_row")
         for j in range(2):
             nc.vector.tensor_copy(out=k_pair[:, j, :], in_=k_raw[j][:].indirect(offsets[:]))
         quantize(*qr[1], E4M3, 0, D)
@@ -169,9 +176,12 @@ def tile_attend_ggqa_sig_k_pl_kernel(tc, q1, q2, kT, dp1, dp2, us, ts, w1, w2, o
                 nc.tensor.matmul_mx(out=score[:], lhsT=k_codes[:, blk].bitcast(E4M3), lhsT_scale=k_scales[:, blk],
                                     rhs=qd_codes[h][:].bitcast(E4M3), rhs_scale=qd_scales[h][:], start=True, stop=True)
                 arg = held([P, R], F32, "arg%d_%d" % (h, ib))
-                nc.vector.tensor_tensor(out=arg[:], in0=score[:], in1=us_half[:], op=ALU.mult)
+                nc.vector.tensor_tensor(out=arg[:].rearrange("p (t s) -> p t s", t=PACK),
+                                        in0=score[:].rearrange("p (s t) -> p t s", t=PACK),
+                                        in1=us_half[:].rearrange("p (t s) -> p t s", t=PACK), op=ALU.mult)
                 nc.scalar.activation(out=arg[:], in_=arg[:], func=ACT.Tanh, scale=ts_col[:, ib:ib + 1])
-                nc.scalar.activation(out=arg[:], in_=arg[:], func=ACT.Square)
+                if MODES[4 * h + ib] != "W":
+                    nc.scalar.activation(out=arg[:], in_=arg[:], func=ACT.Square)
                 if MODES[4 * h + ib] == "S":
                     nc.scalar.activation(out=arg[:], in_=arg[:], func=ACT.Identity, scale=ts_neg[:, ib:ib + 1], bias=ts_pos[:, ib:ib + 1])
                 squares.append(arg)
@@ -198,6 +208,8 @@ def tile_attend_ggqa_sig_k_pl_kernel(tc, q1, q2, kT, dp1, dp2, us, ts, w1, w2, o
                 blk = slice(ib * P, (ib + 1) * P)
                 arg = squares[4 * h + ib]
                 mode = MODES[4 * h + ib]
+                if mode == "W":
+                    nc.vector.tensor_tensor(out=arg[:], in0=arg[:], in1=arg[:], op=ALU.mult)
                 if mode != "S":
                     eng = nc.gpsimd if mode == "G" else nc.vector
                     eng.tensor_scalar(out=arg[:], in0=arg[:], scalar1=ts_neg[:, ib:ib + 1], scalar2=ts_pos[:, ib:ib + 1], op0=ALU.mult, op1=ALU.add)
@@ -221,6 +233,8 @@ def tile_attend_ggqa_sig_k_pl_kernel(tc, q1, q2, kT, dp1, dp2, us, ts, w1, w2, o
                     product(ps, 1, 0, HALF, True, True)
                     early = ps
 
+        windows.append(held([P, TOKENS], F32, "window3", tag="g1_grouped"))
+        nc.gpsimd.memset(windows[3][:], 0.0)
         out_planes = out_0.rearrange("(p j) c -> p j c", j=PACK)
         spans = []
         for width in CHUNKS:

@@ -58,7 +58,7 @@ def tile_attend_ggqa_sig_k_pl_kernel(tc, q1, q2, kT, dp1, dp2, us, ts, w1, w2, o
         q_raw = []
         for h, q in enumerate((q1, q2)):
             t_ = held([P, PACK, R], F32, "q_raw%d" % h)
-            nc.sync.dma_start(out=t_[:], in_=q.rearrange("(p j) r -> p j r", j=PACK))
+            nc.sync.dma_start(out=t_[:].rearrange("p j r -> p (j r)"), in_=q.rearrange("(p j) r -> p (j r)", j=PACK))
             q_raw.append(t_)
             if h == 0:
                 nc.sync.dma_start(out=ts_row[0:1, :], in_=ts[0:1, :])
@@ -72,7 +72,7 @@ def tile_attend_ggqa_sig_k_pl_kernel(tc, q1, q2, kT, dp1, dp2, us, ts, w1, w2, o
         dp_raw = []
         for h, dp in enumerate((dp1, dp2)):
             t_ = held([P, PACK, SLOTS], F32, "dp_raw%d" % h)
-            nc.sync.dma_start(out=t_[:], in_=dp.rearrange("(p b) i -> p b i", b=PACK))
+            nc.sync.dma_start(out=t_[:].rearrange("p b i -> p (b i)"), in_=dp.rearrange("(p b) i -> p (b i)", b=PACK))
             dp_raw.append(t_)
 
         ident = held([P, P], F32, "ident")
@@ -180,11 +180,10 @@ def tile_attend_ggqa_sig_k_pl_kernel(tc, q1, q2, kT, dp1, dp2, us, ts, w1, w2, o
                                         in0=score[:].rearrange("p (s t) -> p t s", t=PACK),
                                         in1=us_half[:].rearrange("p (t s) -> p t s", t=PACK), op=ALU.mult)
                 nc.scalar.activation(out=arg[:], in_=arg[:], func=ACT.Tanh, scale=ts_col[:, ib:ib + 1])
-                if MODES[4 * h + ib] != "W":
-                    nc.scalar.activation(out=arg[:], in_=arg[:], func=ACT.Square)
-                if MODES[4 * h + ib] == "S":
-                    nc.scalar.activation(out=arg[:], in_=arg[:], func=ACT.Identity, scale=ts_neg[:, ib:ib + 1], bias=ts_pos[:, ib:ib + 1])
+                if squares:
+                    nc.scalar.activation(out=squares[-1][:], in_=squares[-1][:], func=ACT.Square)
                 squares.append(arg)
+        nc.scalar.activation(out=squares[-1][:], in_=squares[-1][:], func=ACT.Square)
         for h in range(2):
             for b in range(PACK):
                 nc.gpsimd.tensor_scalar(out=dp_raw[h][:, b, :], in0=dp_raw[h][:, b, :], scalar1=gate[h][:, b:b + 1], scalar2=0.0, op0=ALU.mult, op1=ALU.add)
@@ -208,8 +207,6 @@ def tile_attend_ggqa_sig_k_pl_kernel(tc, q1, q2, kT, dp1, dp2, us, ts, w1, w2, o
                 blk = slice(ib * P, (ib + 1) * P)
                 arg = squares[4 * h + ib]
                 mode = MODES[4 * h + ib]
-                if mode == "W":
-                    nc.vector.tensor_tensor(out=arg[:], in0=arg[:], in1=arg[:], op=ALU.mult)
                 if mode != "S":
                     eng = nc.gpsimd if mode == "G" else nc.vector
                     eng.tensor_scalar(out=arg[:], in0=arg[:], scalar1=ts_neg[:, ib:ib + 1], scalar2=ts_pos[:, ib:ib + 1], op0=ALU.mult, op1=ALU.add)
@@ -240,7 +237,7 @@ def tile_attend_ggqa_sig_k_pl_kernel(tc, q1, q2, kT, dp1, dp2, us, ts, w1, w2, o
         for width in CHUNKS:
             lo = sum(CHUNKS[:len(spans)])
             spans.append(slice(lo, lo + width))
-        pairs = held([P, PACK * TOKENS], BF16, "pairs")
+        pairs = held([P, PACK * TOKENS], BF16, "pairs", tag="g_codes")
         pair_view = pairs[:].rearrange("p (u c e) -> p u c e", u=2, e=2)
         pair_words = pairs[:].bitcast(F32).rearrange("p (u c) -> p c u", u=2)
         second_part.append(held([P, HALF], F32, "second_low", tag="dp_raw1"))

@@ -21,8 +21,8 @@ SLOTS = 512
 TOKENS = 2048
 PACK = 4
 BLOCKS = SLOTS // P
-CHUNKS = (256, 512, 512, 256, 512)
-ILS = "VVVVS"
+PIECE = 256
+VECTOR_PIECES = 6
 MODES = "VVVVGGGV"
 FLOPS = 4 * 2 * D * R * SLOTS
 
@@ -96,8 +96,8 @@ def tile_attend_ggqa_sig_k_pl_kernel(tc, q1, q2, kT, dp1, dp2, us, ts, w1, w2, o
         qr_codes, qr_scales = [t_[1] for t_ in qr], [t_[2] for t_ in qr]
 
         def group_along_d(h, mover, lo=0, hi=P):
-            mover(out=qd[h][0][:].rearrange("p (c i t) -> p c t i", i=4, t=PACK)[:, lo:hi],
-                  in_=q_raw[h][:].rearrange("p t (c i) -> p c t i", i=4)[:, lo:hi])
+            mover(out=qd[h][0][:].rearrange("p (i m t) -> p m t i", i=PACK, t=PACK)[:, lo:hi],
+                  in_=q_raw[h][:].rearrange("p t (m i) -> p m t i", i=PACK)[:, lo:hi])
 
         rounded = []
         for h in range(2):
@@ -176,9 +176,7 @@ def tile_attend_ggqa_sig_k_pl_kernel(tc, q1, q2, kT, dp1, dp2, us, ts, w1, w2, o
                 nc.tensor.matmul_mx(out=score[:], lhsT=k_codes[:, blk].bitcast(E4M3), lhsT_scale=k_scales[:, blk],
                                     rhs=qd_codes[h][:].bitcast(E4M3), rhs_scale=qd_scales[h][:], start=True, stop=True)
                 arg = held([P, R], F32, "arg%d_%d" % (h, ib))
-                nc.vector.tensor_tensor(out=arg[:].rearrange("p (t s) -> p t s", t=PACK),
-                                        in0=score[:].rearrange("p (s t) -> p t s", t=PACK),
-                                        in1=us_half[:].rearrange("p (t s) -> p t s", t=PACK), op=ALU.mult)
+                nc.vector.tensor_tensor(out=arg[:], in0=score[:], in1=us_half[:], op=ALU.mult)
                 nc.scalar.activation(out=arg[:], in_=arg[:], func=ACT.Tanh, scale=ts_col[:, ib:ib + 1])
                 if squares:
                     nc.scalar.activation(out=squares[-1][:], in_=squares[-1][:], func=ACT.Square)
@@ -233,10 +231,7 @@ def tile_attend_ggqa_sig_k_pl_kernel(tc, q1, q2, kT, dp1, dp2, us, ts, w1, w2, o
         windows.append(held([P, TOKENS], F32, "window3", tag="g1_grouped"))
         nc.gpsimd.memset(windows[3][:], 0.0)
         out_planes = out_0.rearrange("(p j) c -> p j c", j=PACK)
-        spans = []
-        for width in CHUNKS:
-            lo = sum(CHUNKS[:len(spans)])
-            spans.append(slice(lo, lo + width))
+        spans = [slice(lo, lo + PIECE) for lo in range(0, TOKENS, PIECE)]
         pairs = held([P, PACK * TOKENS], BF16, "pairs", tag="g_codes")
         pair_view = pairs[:].rearrange("p (u c e) -> p u c e", u=2, e=2)
         pair_words = pairs[:].bitcast(F32).rearrange("p (u c) -> p c u", u=2)
@@ -267,15 +262,21 @@ def tile_attend_ggqa_sig_k_pl_kernel(tc, q1, q2, kT, dp1, dp2, us, ts, w1, w2, o
             nc.sync.dma_start(out=out_planes[:, j, :], in_=windows[j][:])
             for span in (spans if j == PACK - 1 else [slice(0, TOKENS)]):
                 nc.scalar.copy(out=pair_view[:, j // 2, span, j % 2], in_=windows[j][:, span])
+        y_grouped = []
+
+        def quantize_piece(c):
+            nc.vector.quantize_mx(out=y_codes[:, spans[c]].bitcast(E4M3), scales=y_scales[:, spans[c]], in_=y_grouped[c][:])
+            if c % 2 == 1:
+                both = slice(spans[c - 1].start, spans[c].stop)
+                nc.sync.dma_start(out=words_out[:, both], in_=y_codes[:, both].bitcast(I32))
+
         for c, span in enumerate(spans):
-            width = CHUNKS[c] if ILS[c] == "V" else 256
-            mover = nc.vector.tensor_copy if ILS[c] == "V" else nc.scalar.copy
-            for lo in range(0, CHUNKS[c], width):
-                y_grouped = held([P, width * PACK], BF16, "y_grouped%d_%d" % (c, lo))
-                mover(out=y_grouped[:].bitcast(F32).rearrange("p (c u) -> p c u", u=2), in_=pair_words[:, span.start + lo:span.start + lo + width, :])
-                part = slice(span.start + lo, span.start + lo + width)
-                nc.vector.quantize_mx(out=y_codes[:, part].bitcast(E4M3), scales=y_scales[:, part], in_=y_grouped[:])
-                nc.sync.dma_start(out=words_out[:, part], in_=y_codes[:, part].bitcast(I32))
+            mover = nc.vector.tensor_copy if c < VECTOR_PIECES else nc.scalar.copy
+            y_grouped.append(held([P, PIECE * PACK], BF16, "y_grouped%d" % c))
+            mover(out=y_grouped[c][:].bitcast(F32).rearrange("p (c u) -> p c u", u=2), in_=pair_words[:, span, :])
+            if c > 0:
+                quantize_piece(c - 1)
+        quantize_piece(len(spans) - 1)
         scales_out = out_2.rearrange("a f c -> (a f) c").bitcast(I32)
         for quad in range(4):
             queue = nc.sync if quad % 2 == 0 else nc.scalar

@@ -23,7 +23,8 @@ PACK = 4
 BLOCKS = SLOTS // P
 PIECE = 256
 VECTOR_PIECES = 6
-MODES = "VVVVGGGV"
+MODES = "VVVGWGGV"
+STORE_AFTER = (1, 3, 5, 6, 7)
 FLOPS = 4 * 2 * D * R * SLOTS
 
 
@@ -143,6 +144,8 @@ def tile_attend_ggqa_sig_k_pl_kernel(tc, q1, q2, kT, dp1, dp2, us, ts, w1, w2, o
         group_along_d(1, nc.vector.tensor_copy)
         group_along_r(1)
         quantize(*qd[1], E4M3, 0, R)
+        windows.append(held([P, TOKENS], F32, "window3", tag="q_raw1"))
+        nc.gpsimd.memset(windows[3][:], 0.0)
         quantize(*qr[0], E4M3, 0, D)
         k_pair = held([P, 2, SLOTS], BF16, "k_pair", tag="ts_row")
         for j in range(2):
@@ -178,7 +181,7 @@ def tile_attend_ggqa_sig_k_pl_kernel(tc, q1, q2, kT, dp1, dp2, us, ts, w1, w2, o
                 arg = held([P, R], F32, "arg%d_%d" % (h, ib))
                 nc.vector.tensor_tensor(out=arg[:], in0=score[:], in1=us_half[:], op=ALU.mult)
                 nc.scalar.activation(out=arg[:], in_=arg[:], func=ACT.Tanh, scale=ts_col[:, ib:ib + 1])
-                if squares:
+                if squares and MODES[len(squares) - 1] != "W":
                     nc.scalar.activation(out=squares[-1][:], in_=squares[-1][:], func=ACT.Square)
                 squares.append(arg)
         nc.scalar.activation(out=squares[-1][:], in_=squares[-1][:], func=ACT.Square)
@@ -205,6 +208,8 @@ def tile_attend_ggqa_sig_k_pl_kernel(tc, q1, q2, kT, dp1, dp2, us, ts, w1, w2, o
                 blk = slice(ib * P, (ib + 1) * P)
                 arg = squares[4 * h + ib]
                 mode = MODES[4 * h + ib]
+                if mode == "W":
+                    nc.vector.tensor_tensor(out=arg[:], in0=arg[:], in1=arg[:], op=ALU.mult)
                 if mode != "S":
                     eng = nc.gpsimd if mode == "G" else nc.vector
                     eng.tensor_scalar(out=arg[:], in0=arg[:], scalar1=ts_neg[:, ib:ib + 1], scalar2=ts_pos[:, ib:ib + 1], op0=ALU.mult, op1=ALU.add)
@@ -228,8 +233,6 @@ def tile_attend_ggqa_sig_k_pl_kernel(tc, q1, q2, kT, dp1, dp2, us, ts, w1, w2, o
                     product(ps, 1, 0, HALF, True, True)
                     early = ps
 
-        windows.append(held([P, TOKENS], F32, "window3", tag="g1_grouped"))
-        nc.gpsimd.memset(windows[3][:], 0.0)
         out_planes = out_0.rearrange("(p j) c -> p j c", j=PACK)
         spans = [slice(lo, lo + PIECE) for lo in range(0, TOKENS, PIECE)]
         pairs = held([P, PACK * TOKENS], BF16, "pairs", tag="g_codes")
@@ -266,9 +269,10 @@ def tile_attend_ggqa_sig_k_pl_kernel(tc, q1, q2, kT, dp1, dp2, us, ts, w1, w2, o
 
         def quantize_piece(c):
             nc.vector.quantize_mx(out=y_codes[:, spans[c]].bitcast(E4M3), scales=y_scales[:, spans[c]], in_=y_grouped[c][:])
-            if c % 2 == 1:
-                both = slice(spans[c - 1].start, spans[c].stop)
-                nc.sync.dma_start(out=words_out[:, both], in_=y_codes[:, both].bitcast(I32))
+            if c in STORE_AFTER:
+                done = [-1] + [e for e in STORE_AFTER if e < c]
+                part = slice(PIECE * (done[-1] + 1), spans[c].stop)
+                nc.sync.dma_start(out=words_out[:, part], in_=y_codes[:, part].bitcast(I32))
 
         for c, span in enumerate(spans):
             mover = nc.vector.tensor_copy if c < VECTOR_PIECES else nc.scalar.copy

@@ -25,6 +25,8 @@ PIECE = 256
 VECTOR_PIECES = 6
 MODES = "VVVGWGGV"
 STORE_AFTER = (1, 3, 5, 6, 7)
+SPLIT_PLANES = 2
+GPSIMD_COLUMNS = 640
 FLOPS = 4 * 2 * D * R * SLOTS
 
 
@@ -198,8 +200,7 @@ def tile_attend_ggqa_sig_k_pl_kernel(tc, q1, q2, kT, dp1, dp2, us, ts, w1, w2, o
                                 rhs=g_all_codes[:, lo:lo + SLOTS].bitcast(E5M2), rhs_scale=g_all_scales[:, lo:lo + SLOTS],
                                 start=start, stop=stop)
 
-        first_part = held([P, SLOTS], F32, "first_part")
-        second_part = []
+        first_part, early = [], []
         for h in range(2):
             g_grouped = held([P, SLOTS * PACK], BF16, "g%d_grouped" % h)
             codes = g_all_codes[:, h * SLOTS:(h + 1) * SLOTS]
@@ -225,27 +226,32 @@ def tile_attend_ggqa_sig_k_pl_kernel(tc, q1, q2, kT, dp1, dp2, us, ts, w1, w2, o
                 elif ib % 2 == 1:
                     quantize(g_grouped, codes, scales, E5M2, (ib - 1) * P, (ib + 1) * P)
                 if h == 0 and ib == 3:
-                    ps = bank("a", 4)
-                    product(ps, 0, 0, 0, True, True)
-                    nc.scalar.copy(out=first_part[:], in_=ps[:])
+                    for j in range(SPLIT_PLANES):
+                        ps = bank("a", 4)
+                        product(ps, 0, j, 0, True, True)
+                        first_part.append(held([P, SLOTS], F32, "first_part%d" % j))
+                        nc.scalar.copy(out=first_part[j][:], in_=ps[:])
                 if h == 1 and ib == 1:
-                    ps = bank("a", 4)
-                    product(ps, 1, 0, HALF, True, True)
-                    early = ps
+                    for j in range(SPLIT_PLANES):
+                        early.append(bank("a", 4))
+                        product(early[j], 1, j, HALF, True, True)
 
         out_planes = out_0.rearrange("(p j) c -> p j c", j=PACK)
         spans = [slice(lo, lo + PIECE) for lo in range(0, TOKENS, PIECE)]
         pairs = held([P, PACK * TOKENS], BF16, "pairs", tag="g_codes")
         pair_view = pairs[:].rearrange("p (u c e) -> p u c e", u=2, e=2)
         pair_words = pairs[:].bitcast(F32).rearrange("p (u c) -> p c u", u=2)
-        second_part.append(held([P, HALF], F32, "second_low", tag="dp_raw1"))
-        nc.scalar.copy(out=second_part[0][:], in_=early[:, HALF:SLOTS])
-        ps = bank("a", 4)
-        product(ps, 1, 0, SLOTS, True, True)
-        second_part.append(held([P, HALF], F32, "second_high"))
-        nc.scalar.copy(out=second_part[1][:], in_=ps[:, HALF:SLOTS])
-        listed = [None]
-        for j in range(1, PACK):
+        second_part = {}
+        for j in range(SPLIT_PLANES):
+            second_part[j, 0] = held([P, HALF], F32, "second_low%d" % j, tag=("arg1_3", "dp_raw1")[j])
+            nc.scalar.copy(out=second_part[j, 0][:], in_=early[j][:, HALF:SLOTS])
+        for j in range(SPLIT_PLANES):
+            ps = bank("a", 4)
+            product(ps, 1, j, SLOTS, True, True)
+            second_part[j, HALF] = held([P, HALF], F32, "second_high%d" % j)
+            nc.scalar.copy(out=second_part[j, HALF][:], in_=ps[:, HALF:SLOTS])
+        listed = [None] * SPLIT_PLANES
+        for j in range(SPLIT_PLANES, PACK):
             dk = bank("a", 4)
             for h in range(2):
                 product(dk, h, j, h * SLOTS, h == 0, h == 1)
@@ -255,16 +261,25 @@ def tile_attend_ggqa_sig_k_pl_kernel(tc, q1, q2, kT, dp1, dp2, us, ts, w1, w2, o
         y_codes = held([P, TOKENS], U32, "y_codes")
         y_scales = held([P, TOKENS], U8, "y_scales")
         words_out = out_1.rearrange("a p c t -> p (a c t)").bitcast(I32)
+
+        def scatter_half(j, lo):
+            nc.vector.tensor_tensor(out=windows[j][:].indirect(offsets[:, lo // 16:(lo + HALF) // 16]),
+                                    in0=first_part[j][:, lo:lo + HALF], in1=second_part[j, lo][:], op=ALU.add)
+
+        for j in range(SPLIT_PLANES):
+            scatter_half(j, 0)
         for j in range(PACK):
-            if j == 0:
-                for lo in (0, HALF):
-                    nc.vector.tensor_tensor(out=windows[0][:].indirect(offsets[:, lo // 16:(lo + HALF) // 16]),
-                                            in0=first_part[:, lo:lo + HALF], in1=second_part[lo // HALF][:], op=ALU.add)
+            if j < SPLIT_PLANES:
+                scatter_half(j, HALF)
             else:
                 nc.vector.tensor_copy(out=windows[j][:].indirect(offsets[:]), in_=listed[j][:])
             nc.sync.dma_start(out=out_planes[:, j, :], in_=windows[j][:])
-            for span in (spans if j == PACK - 1 else [slice(0, TOKENS)]):
+            scalar_end = TOKENS - GPSIMD_COLUMNS if j < 2 else TOKENS
+            for span in (spans if j == PACK - 1 else [slice(0, scalar_end)]):
                 nc.scalar.copy(out=pair_view[:, j // 2, span, j % 2], in_=windows[j][:, span])
+            if j < 2:
+                nc.gpsimd.tensor_scalar(out=pair_view[:, 0, scalar_end:TOKENS, j], in0=windows[j][:, scalar_end:TOKENS],
+                                        scalar1=1.0, scalar2=-0.0, op0=ALU.mult, op1=ALU.add)
         y_grouped = []
 
         def quantize_piece(c):

@@ -43,12 +43,10 @@ def tile_attend_ggqa_sig_k_pl_kernel(tc, q1, q2, kT, dp1, dp2, us, ts, w1, w2, o
             return psum.tile([P, 512], F32, name=tag, tag=tag, bufs=bufs)
 
         offsets = keep.tile([P, SLOTS // 16], U16, name="offsets")
-        nc.sync.dma_start(offsets[:], offs)
         ts_row = held([P, TOKENS], F32, "ts_row")
 
         def zero_beside_gpsimd(t_):
-            nc.vector.memset(t_[:, 0:1025], 0.0)
-            nc.vector.memset(t_[:, 1025:TOKENS], 0.0)
+            nc.vector.memset(t_[:].bitcast(I32), 0)
 
         zero_beside_gpsimd(ts_row)
 
@@ -57,13 +55,14 @@ def tile_attend_ggqa_sig_k_pl_kernel(tc, q1, q2, kT, dp1, dp2, us, ts, w1, w2, o
             nc.sync.dma_start(out=t_[:], in_=vec.rearrange("(p b) o -> p (b o)", b=PACK))
             return t_
 
-        us_col = load_column("us_col", us)
         q_raw = []
         for h, q in enumerate((q1, q2)):
             t_ = held([P, PACK, R], F32, "q_raw%d" % h)
             nc.sync.dma_start(out=t_[:].rearrange("p j r -> p (j r)"), in_=q.rearrange("(p j) r -> p (j r)", j=PACK))
             q_raw.append(t_)
             if h == 0:
+                nc.sync.dma_start(offsets[:], offs)
+                us_col = load_column("us_col", us)
                 nc.sync.dma_start(out=ts_row[0:1, :], in_=ts[0:1, :])
         k_planes = kT.rearrange("(p j) c -> p j c", j=PACK)
         k_raw = []
@@ -80,10 +79,9 @@ def tile_attend_ggqa_sig_k_pl_kernel(tc, q1, q2, kT, dp1, dp2, us, ts, w1, w2, o
 
         ident = held([P, P], F32, "ident")
         make_identity(nc, ident[:])
-        windows = [held([P, TOKENS], F32, "window%d" % j) for j in range(PACK - 1)]
+        windows = [held([P, TOKENS], F32, "window%d" % j) for j in range(2)]
         zero_beside_gpsimd(windows[0])
-        nc.gpsimd.memset(windows[1][:], 0.0)
-        nc.gpsimd.memset(windows[2][:], 0.0)
+        zero_beside_gpsimd(windows[1])
 
         def quantize(grouped, codes, scales, fmt, lo, hi):
             nc.vector.quantize_mx(out=codes[:, lo:hi].bitcast(fmt), scales=scales[:, lo:hi],
@@ -146,8 +144,6 @@ def tile_attend_ggqa_sig_k_pl_kernel(tc, q1, q2, kT, dp1, dp2, us, ts, w1, w2, o
         group_along_d(1, nc.vector.tensor_copy)
         group_along_r(1)
         quantize(*qd[1], E4M3, 0, R)
-        windows.append(held([P, TOKENS], F32, "window3", tag="q_raw1"))
-        nc.gpsimd.memset(windows[3][:], 0.0)
         quantize(*qr[0], E4M3, 0, D)
         k_pair = held([P, 2, SLOTS], BF16, "k_pair", tag="ts_row")
         for j in range(2):
@@ -259,7 +255,7 @@ def tile_attend_ggqa_sig_k_pl_kernel(tc, q1, q2, kT, dp1, dp2, us, ts, w1, w2, o
             nc.scalar.copy(out=t_[:], in_=dk[:])
             listed.append(t_)
         y_codes = held([P, TOKENS], U32, "y_codes")
-        y_scales = held([P, TOKENS], U8, "y_scales")
+        y_scales = held([P, TOKENS // PACK], U8, "y_scales")
         words_out = out_1.rearrange("a p c t -> p (a c t)").bitcast(I32)
 
         def scatter_half(j, lo):
@@ -268,6 +264,9 @@ def tile_attend_ggqa_sig_k_pl_kernel(tc, q1, q2, kT, dp1, dp2, us, ts, w1, w2, o
 
         for j in range(SPLIT_PLANES):
             scatter_half(j, 0)
+        for j, tag in ((2, "g1_grouped"), (3, "dp_raw1")):
+            windows.append(held([P, TOKENS], F32, "window%d" % j, tag=tag))
+            nc.gpsimd.memset(windows[j][:], 0.0)
         for j in range(PACK):
             if j < SPLIT_PLANES:
                 scatter_half(j, HALF)
@@ -283,7 +282,7 @@ def tile_attend_ggqa_sig_k_pl_kernel(tc, q1, q2, kT, dp1, dp2, us, ts, w1, w2, o
         y_grouped = []
 
         def quantize_piece(c):
-            nc.vector.quantize_mx(out=y_codes[:, spans[c]].bitcast(E4M3), scales=y_scales[:, spans[c]], in_=y_grouped[c][:])
+            nc.vector.quantize_mx(out=y_codes[:, spans[c]].bitcast(E4M3), scales=y_scales[4 * (c // 2):P, (c % 2) * PIECE:(c % 2 + 1) * PIECE], in_=y_grouped[c][:])
             if c in STORE_AFTER:
                 done = [-1] + [e for e in STORE_AFTER if e < c]
                 part = slice(PIECE * (done[-1] + 1), spans[c].stop)
@@ -296,7 +295,7 @@ def tile_attend_ggqa_sig_k_pl_kernel(tc, q1, q2, kT, dp1, dp2, us, ts, w1, w2, o
             if c > 0:
                 quantize_piece(c - 1)
         quantize_piece(len(spans) - 1)
-        scales_out = out_2.rearrange("a f c -> (a f) c").bitcast(I32)
+        scales_out = out_2.rearrange("a f c -> (a f) c").bitcast(I32).rearrange("f (a c) -> a f c", a=PACK)
         for quad in range(4):
             queue = nc.sync if quad % 2 == 0 else nc.scalar
-            queue.dma_start(out=scales_out[4 * quad:4 * quad + 4, :], in_=y_scales[32 * quad:32 * quad + 4, :].bitcast(I32))
+            queue.dma_start(out=scales_out[:, 4 * quad:4 * quad + 4, :], in_=y_scales[32 * quad:32 * quad + 16, :].bitcast(I32))

@@ -23,7 +23,6 @@ PACK = 4
 BLOCKS = SLOTS // P
 PIECE = 256
 VECTOR_PIECES = 6
-MODES = "VVVGWGGV"
 STORE_AFTER = (1, 3, 5, 6, 7)
 SPLIT_PLANES = 2
 GPSIMD_COLUMNS = 640
@@ -46,13 +45,14 @@ def tile_attend_ggqa_sig_k_pl_kernel(tc, q1, q2, kT, dp1, dp2, us, ts, w1, w2, o
         ts_row = held([P, TOKENS], F32, "ts_row")
 
         def zero_beside_gpsimd(t_):
-            nc.vector.memset(t_[:].bitcast(I32), 0)
+            nc.vector.memset(t_[:, 0:1025], 0.0)
+            nc.vector.memset(t_[:, 1025:TOKENS], 0.0)
 
         zero_beside_gpsimd(ts_row)
 
         def load_column(name, vec):
             t_ = held([P, PACK], F32, name)
-            nc.sync.dma_start(out=t_[:], in_=vec.rearrange("(p b) o -> p (b o)", b=PACK))
+            nc.scalar.dma_start(out=t_[:], in_=vec.rearrange("(p b) o -> p (b o)", b=PACK))
             return t_
 
         q_raw = []
@@ -63,25 +63,35 @@ def tile_attend_ggqa_sig_k_pl_kernel(tc, q1, q2, kT, dp1, dp2, us, ts, w1, w2, o
             if h == 0:
                 nc.sync.dma_start(offsets[:], offs)
                 us_col = load_column("us_col", us)
-                nc.sync.dma_start(out=ts_row[0:1, :], in_=ts[0:1, :])
+                cols = [us_col, load_column("w1_col", w1), load_column("w2_col", w2)]
+
+        nc.sync.dma_start(out=ts_row[0:1, :], in_=ts[0:1, :])
         k_planes = kT.rearrange("(p j) c -> p j c", j=PACK)
         k_raw = []
         for j in range(PACK):
             t_ = held([P, TOKENS], F32, "k_raw%d" % j)
             nc.sync.dma_start(out=t_[:], in_=k_planes[:, j, :])
             k_raw.append(t_)
-        cols = [us_col, load_column("w1_col", w1), load_column("w2_col", w2)]
-        dp_raw = []
-        for h, dp in enumerate((dp1, dp2)):
-            t_ = held([P, PACK, SLOTS], F32, "dp_raw%d" % h)
-            nc.sync.dma_start(out=t_[:].rearrange("p b i -> p (b i)"), in_=dp.rearrange("(p b) i -> p (b i)", b=PACK))
-            dp_raw.append(t_)
+        HALF = SLOTS // 2
+        dp_first = held([P, PACK, SLOTS], F32, "dp_first")
+        nc.sync.dma_start(out=dp_first[:].rearrange("p b i -> p (b i)"), in_=dp1.rearrange("(p b) i -> p (b i)", b=PACK))
+        dp_part = {(0, half): dp_first[:, :, half * HALF:(half + 1) * HALF] for half in range(2)}
+        for half in range(2):
+            t_ = held([P, PACK, HALF], F32, "dp_second%d" % half)
+            nc.sync.dma_start(out=t_[:], in_=dp2.rearrange("(p b) i -> p b i", b=PACK)[:, :, half * HALF:(half + 1) * HALF])
+            dp_part[1, half] = t_[:]
 
         ident = held([P, P], F32, "ident")
         make_identity(nc, ident[:])
         windows = [held([P, TOKENS], F32, "window%d" % j) for j in range(2)]
-        zero_beside_gpsimd(windows[0])
-        zero_beside_gpsimd(windows[1])
+        nc.vector.memset(windows[0][:, 0:513], 0.0)
+        nc.vector.memset(windows[0][:, 513:1024], 0.0)
+        nc.gpsimd.memset(windows[1][:], 0.0)
+        nc.gpsimd.memset(windows[0][:, 1024:TOKENS], 0.0)
+        g_all_codes = held([P, 2 * SLOTS], U32, "g_codes")
+        g_all_scales = held([P, 2 * SLOTS], U8, "g_scales")
+        nc.vector.memset(g_all_codes[:].bitcast(I32).rearrange("p (h u c) -> p h u c", h=2, u=2)[:, :, 1, :], 0)
+        nc.vector.memset(g_all_scales[:].bitcast(I32), 0)
 
         def quantize(grouped, codes, scales, fmt, lo, hi):
             nc.vector.quantize_mx(out=codes[:, lo:hi].bitcast(fmt), scales=scales[:, lo:hi],
@@ -154,8 +164,6 @@ def tile_attend_ggqa_sig_k_pl_kernel(tc, q1, q2, kT, dp1, dp2, us, ts, w1, w2, o
         k_scales = held([P, SLOTS], U8, "k_scales")
         keys = (k_grouped, k_codes, k_scales)
         k_view = k_grouped[:].rearrange("p (c t) -> p c t", t=PACK)
-        nc.scalar.copy(out=k_view[:, :, 0:2], in_=k_pair[:].rearrange("p e c -> p c e"))
-        gather_keys(2, 0, SLOTS)
         ps = bank("c", 4)
         for b in range(BLOCKS):
             nc.tensor.transpose(ps[:, b * P:(b + 1) * P], ts_listed[:, b * P:(b + 1) * P], ident[:])
@@ -163,94 +171,119 @@ def tile_attend_ggqa_sig_k_pl_kernel(tc, q1, q2, kT, dp1, dp2, us, ts, w1, w2, o
         nc.scalar.copy(out=ts_col[:], in_=ps[:, 0:512:P])
         ts_neg = held([P, BLOCKS], F32, "ts_neg")
         nc.scalar.activation(out=ts_neg[:], in_=ps[:, 0:512:P], func=ACT.Copy, scale=-0.25)
-        ts_pos = held([P, BLOCKS], F32, "ts_pos")
-        nc.scalar.activation(out=ts_pos[:], in_=ps[:, 0:512:P], func=ACT.Copy, scale=0.25)
+        ts_bank = bank("c", 4)
+        for b in range(BLOCKS):
+            nc.tensor.transpose(ts_bank[:, b * P:(b + 1) * P], ts_neg[:, b:b + 1].to_broadcast([P, P]), ident[:])
+        factor = []
 
-        squares = []
-        for h in range(2):
-            for ib in range(BLOCKS):
-                blk = slice(ib * P, (ib + 1) * P)
-                if h == 0 and ib % 2 == 0:
-                    gather_keys(3, ib * P, (ib + 2) * P)
-                    quantize(*keys, E4M3, ib * P, (ib + 2) * P)
-                score = bank("a", 4)
-                nc.tensor.matmul_mx(out=score[:], lhsT=k_codes[:, blk].bitcast(E4M3), lhsT_scale=k_scales[:, blk],
-                                    rhs=qd_codes[h][:].bitcast(E4M3), rhs_scale=qd_scales[h][:], start=True, stop=True)
-                arg = held([P, R], F32, "arg%d_%d" % (h, ib))
-                nc.vector.tensor_tensor(out=arg[:], in0=score[:], in1=us_half[:], op=ALU.mult)
-                nc.scalar.activation(out=arg[:], in_=arg[:], func=ACT.Tanh, scale=ts_col[:, ib:ib + 1])
-                if squares and MODES[len(squares) - 1] != "W":
-                    nc.scalar.activation(out=squares[-1][:], in_=squares[-1][:], func=ACT.Square)
-                squares.append(arg)
-        nc.scalar.activation(out=squares[-1][:], in_=squares[-1][:], func=ACT.Square)
-        for h in range(2):
+        def make_factor(h):
+            factor.append(held([P, PACK, SLOTS], F32, "factor%d" % h, tag="q_raw%d" % h))
             for b in range(PACK):
-                nc.gpsimd.tensor_scalar(out=dp_raw[h][:, b, :], in0=dp_raw[h][:, b, :], scalar1=gate[h][:, b:b + 1], scalar2=0.0, op0=ALU.mult, op1=ALU.add)
-        g_all_codes = held([P, 2 * SLOTS], U32, "g_codes")
-        g_all_scales = held([P, 2 * SLOTS], U8, "g_scales")
-        HALF = SLOTS // 2
+                nc.scalar.activation(out=factor[h][:, b, :], in_=ts_bank[:], func=ACT.Copy, scale=gate[h][:, b:b + 1])
 
-        def product(ps, h, j, lo, start, stop):
+        make_factor(0)
+        nc.scalar.copy(out=k_view[:, :, 0:2], in_=k_pair[:].rearrange("p e c -> p c e"))
+        make_factor(1)
+        gather_keys(2, 0, SLOTS)
+
+        order = [(h, 2 * half + b) for half in range(2) for h in range(2) for b in range(2)]
+        squares = []
+        for h, ib in order:
+            blk = slice(ib * P, (ib + 1) * P)
+            if h == 0 and ib % 2 == 0:
+                gather_keys(3, ib * P, (ib + 2) * P)
+                quantize(*keys, E4M3, ib * P, (ib + 2) * P)
+            score = bank("a", 4)
+            nc.tensor.matmul_mx(out=score[:], lhsT=k_codes[:, blk].bitcast(E4M3), lhsT_scale=k_scales[:, blk],
+                                rhs=qd_codes[h][:].bitcast(E4M3), rhs_scale=qd_scales[h][:], start=True, stop=True)
+            arg = held([P, R], F32, "arg%d_%d" % (h, ib))
+            nc.vector.tensor_tensor(out=arg[:], in0=score[:], in1=us_half[:], op=ALU.mult)
+            nc.scalar.activation(out=arg[:], in_=arg[:], func=ACT.Tanh, scale=ts_col[:, ib:ib + 1])
+            if squares:
+                nc.scalar.activation(out=squares[-1][:], in_=squares[-1][:], func=ACT.Square)
+            squares.append(arg)
+        nc.scalar.activation(out=squares[-1][:], in_=squares[-1][:], func=ACT.Square)
+        scaled = {}
+
+        def scale_dp(h, half, tag):
+            scaled[h, half] = held([P, HALF * PACK], F32, "scaled%d_%d" % (h, half), tag=tag)
+            nc.gpsimd.tensor_tensor(
+                out=scaled[h, half][:].rearrange("p (i t) -> p i t", t=PACK),
+                in0=dp_part[h, half].rearrange("p t i -> p i t"),
+                in1=factor[h][:, :, half * HALF:(half + 1) * HALF].rearrange("p t i -> p i t"), op=ALU.mult)
+
+        scale_dp(0, 0, "qr1_grouped")
+        scale_dp(1, 0, None)
+        scale_dp(0, 1, "dp_second0")
+        g_grouped = {(h, half): held([P, HALF * PACK], BF16, "g%d_%d" % (h, half), tag="us_half" if h + half == 0 else None)
+                     for h in range(2) for half in range(2)}
+
+        def products(j):
+            ps = bank("a", 4)
             blk = slice(j * P, (j + 1) * P)
-            nc.tensor.matmul_mx(out=ps[:], lhsT=qr_codes[h][:, blk].bitcast(E4M3), lhsT_scale=qr_scales[h][:, blk],
-                                rhs=g_all_codes[:, lo:lo + SLOTS].bitcast(E5M2), rhs_scale=g_all_scales[:, lo:lo + SLOTS],
-                                start=start, stop=stop)
+            for h in range(2):
+                lo = h * SLOTS
+                nc.tensor.matmul_mx(out=ps[:], lhsT=qr_codes[h][:, blk].bitcast(E4M3), lhsT_scale=qr_scales[h][:, blk],
+                                    rhs=g_all_codes[:, lo:lo + SLOTS].bitcast(E5M2), rhs_scale=g_all_scales[:, lo:lo + SLOTS],
+                                    start=h == 0, stop=h == 1)
+            return ps
 
-        first_part, early = [], []
-        for h in range(2):
-            g_grouped = held([P, SLOTS * PACK], BF16, "g%d_grouped" % h)
-            codes = g_all_codes[:, h * SLOTS:(h + 1) * SLOTS]
-            scales = g_all_scales[:, h * SLOTS:(h + 1) * SLOTS]
-            for ib in range(BLOCKS):
-                blk = slice(ib * P, (ib + 1) * P)
-                arg = squares[4 * h + ib]
-                mode = MODES[4 * h + ib]
-                if mode == "W":
-                    nc.vector.tensor_tensor(out=arg[:], in0=arg[:], in1=arg[:], op=ALU.mult)
-                if mode != "S":
-                    eng = nc.gpsimd if mode == "G" else nc.vector
-                    eng.tensor_scalar(out=arg[:], in0=arg[:], scalar1=ts_neg[:, ib:ib + 1], scalar2=ts_pos[:, ib:ib + 1], op0=ALU.mult, op1=ALU.add)
-                slope = bank("c", 4)
-                for t in range(PACK):
-                    nc.tensor.transpose(slope[:, t * P:(t + 1) * P], arg[:, t * P:(t + 1) * P], ident[:])
-                nc.vector.tensor_tensor(
-                    out=g_grouped[:, PACK * P * ib:PACK * P * (ib + 1)].rearrange("p (c i t) -> p c t i", i=4, t=PACK),
-                    in0=dp_raw[h][:, :, blk].rearrange("p t (c i) -> p c t i", i=4),
-                    in1=slope[:].rearrange("p (t c i) -> p c t i", i=4, t=PACK), op=ALU.mult)
-                if h == 1 and ib >= 2:
-                    quantize(g_grouped, codes, scales, E5M2, ib * P, (ib + 1) * P)
-                elif ib % 2 == 1:
-                    quantize(g_grouped, codes, scales, E5M2, (ib - 1) * P, (ib + 1) * P)
-                if h == 0 and ib == 3:
-                    for j in range(SPLIT_PLANES):
-                        ps = bank("a", 4)
-                        product(ps, 0, j, 0, True, True)
-                        first_part.append(held([P, SLOTS], F32, "first_part%d" % j))
-                        nc.scalar.copy(out=first_part[j][:], in_=ps[:])
-                if h == 1 and ib == 1:
-                    for j in range(SPLIT_PLANES):
-                        early.append(bank("a", 4))
-                        product(early[j], 1, j, HALF, True, True)
+        parts = {}
+        slopes = {}
+
+        def turn(n):
+            slopes[n] = bank("c", 4)
+            for t in range(PACK):
+                nc.tensor.transpose(slopes[n][:, t * P:(t + 1) * P], squares[n][:, t * P:(t + 1) * P], ident[:])
+
+        def gradient(n):
+            h, ib = order[n]
+            span = slice(PACK * P * (ib % 2), PACK * P * (ib % 2 + 1))
+            nc.vector.scalar_tensor_tensor(
+                out=g_grouped[h, ib // 2][:, span].rearrange("p (i t) -> p i t", t=PACK),
+                in0=slopes[n][:].rearrange("p (t i) -> p i t", t=PACK), scalar=-1.0,
+                in1=scaled[h, ib // 2][:, PACK * P * (ib % 2):PACK * P * (ib % 2 + 1)].rearrange("p (i t) -> p i t", t=PACK), op0=ALU.add, op1=ALU.mult)
+
+        def quantize_half(half):
+            for h in range(2):
+                lo = h * SLOTS + half * HALF
+                quantize(g_grouped[h, half], g_all_codes[:, lo:lo + HALF], g_all_scales[:, lo:lo + HALF], E5M2, 0, HALF)
+
+        def scatter_half(j, lo):
+            nc.vector.tensor_copy(out=windows[j][:].indirect(offsets[:, lo // 16:(lo + HALF) // 16]), in_=parts[j, lo][:])
+
+        for n in range(4):
+            turn(n)
+            gradient(n)
+        turn(4)
+        turn(5)
+        quantize_half(0)
+        scale_dp(1, 1, "g1_0")
+        early = [products(j) for j in range(SPLIT_PLANES)]
+        gradient(4)
+        gradient(5)
+        parts[0, 0] = held([P, HALF], F32, "low0", tag="arg0_3")
+        nc.vector.tensor_copy(out=parts[0, 0][:], in_=early[0][:, 0:HALF])
+        scatter_half(0, 0)
+        for n in (6, 7):
+            turn(n)
+            gradient(n)
+        quantize_half(1)
+        parts[1, 0] = held([P, HALF], F32, "low1", tag="g1_0")
+        nc.scalar.copy(out=parts[1, 0][:], in_=early[1][:, 0:HALF])
 
         out_planes = out_0.rearrange("(p j) c -> p j c", j=PACK)
         spans = [slice(lo, lo + PIECE) for lo in range(0, TOKENS, PIECE)]
         pairs = held([P, PACK * TOKENS], BF16, "pairs", tag="g_codes")
         pair_view = pairs[:].rearrange("p (u c e) -> p u c e", u=2, e=2)
         pair_words = pairs[:].bitcast(F32).rearrange("p (u c) -> p c u", u=2)
-        second_part = {}
         for j in range(SPLIT_PLANES):
-            second_part[j, 0] = held([P, HALF], F32, "second_low%d" % j, tag=("arg1_3", "dp_raw1")[j])
-            nc.scalar.copy(out=second_part[j, 0][:], in_=early[j][:, HALF:SLOTS])
-        for j in range(SPLIT_PLANES):
-            ps = bank("a", 4)
-            product(ps, 1, j, SLOTS, True, True)
-            second_part[j, HALF] = held([P, HALF], F32, "second_high%d" % j)
-            nc.scalar.copy(out=second_part[j, HALF][:], in_=ps[:, HALF:SLOTS])
+            ps = products(j)
+            parts[j, HALF] = held([P, HALF], F32, "high%d" % j)
+            nc.scalar.copy(out=parts[j, HALF][:], in_=ps[:, HALF:SLOTS])
         listed = [None] * SPLIT_PLANES
         for j in range(SPLIT_PLANES, PACK):
-            dk = bank("a", 4)
-            for h in range(2):
-                product(dk, h, j, h * SLOTS, h == 0, h == 1)
+            dk = products(j)
             t_ = held([P, SLOTS], F32, "dk%d" % j)
             nc.scalar.copy(out=t_[:], in_=dk[:])
             listed.append(t_)
@@ -258,13 +291,8 @@ def tile_attend_ggqa_sig_k_pl_kernel(tc, q1, q2, kT, dp1, dp2, us, ts, w1, w2, o
         y_scales = held([P, TOKENS // PACK], U8, "y_scales")
         words_out = out_1.rearrange("a p c t -> p (a c t)").bitcast(I32)
 
-        def scatter_half(j, lo):
-            nc.vector.tensor_tensor(out=windows[j][:].indirect(offsets[:, lo // 16:(lo + HALF) // 16]),
-                                    in0=first_part[j][:, lo:lo + HALF], in1=second_part[j, lo][:], op=ALU.add)
-
-        for j in range(SPLIT_PLANES):
-            scatter_half(j, 0)
-        for j, tag in ((2, "g1_grouped"), (3, "dp_raw1")):
+        scatter_half(1, 0)
+        for j, tag in ((2, "g0_1"), (3, "g1_1")):
             windows.append(held([P, TOKENS], F32, "window%d" % j, tag=tag))
             nc.gpsimd.memset(windows[j][:], 0.0)
         for j in range(PACK):

@@ -22,10 +22,12 @@ TOKENS = 2048
 PACK = 4
 BLOCKS = SLOTS // P
 PIECE = 256
-VECTOR_PIECES = 6
-STORE_AFTER = (1, 3, 5, 6, 7)
+VECTOR_PIECES = 5
+MODES = "SVVVGGGG"
+STORE_AFTER = (3, 6, 7)
 SPLIT_PLANES = 2
-GPSIMD_COLUMNS = 640
+GPSIMD_COLUMNS = 896
+DIRECT = 512
 FLOPS = 4 * 2 * D * R * SLOTS
 
 
@@ -52,20 +54,19 @@ def tile_attend_ggqa_sig_k_pl_kernel(tc, q1, q2, kT, dp1, dp2, us, ts, w1, w2, o
 
         def load_column(name, vec):
             t_ = held([P, PACK], F32, name)
-            nc.scalar.dma_start(out=t_[:], in_=vec.rearrange("(p b) o -> p (b o)", b=PACK))
+            nc.sync.dma_start(out=t_[:], in_=vec.rearrange("(p b) o -> p (b o)", b=PACK))
             return t_
 
+        nc.sync.dma_start(offsets[:], offs)
+        us_col = load_column("us_col", us)
         q_raw = []
         for h, q in enumerate((q1, q2)):
             t_ = held([P, PACK, R], F32, "q_raw%d" % h)
             nc.sync.dma_start(out=t_[:].rearrange("p j r -> p (j r)"), in_=q.rearrange("(p j) r -> p (j r)", j=PACK))
             q_raw.append(t_)
             if h == 0:
-                nc.sync.dma_start(offsets[:], offs)
-                us_col = load_column("us_col", us)
-                cols = [us_col, load_column("w1_col", w1), load_column("w2_col", w2)]
+                nc.sync.dma_start(out=ts_row[0:1, :], in_=ts[0:1, :])
 
-        nc.sync.dma_start(out=ts_row[0:1, :], in_=ts[0:1, :])
         k_planes = kT.rearrange("(p j) c -> p j c", j=PACK)
         k_raw = []
         for j in range(PACK):
@@ -73,13 +74,12 @@ def tile_attend_ggqa_sig_k_pl_kernel(tc, q1, q2, kT, dp1, dp2, us, ts, w1, w2, o
             nc.sync.dma_start(out=t_[:], in_=k_planes[:, j, :])
             k_raw.append(t_)
         HALF = SLOTS // 2
-        dp_first = held([P, PACK, SLOTS], F32, "dp_first")
-        nc.sync.dma_start(out=dp_first[:].rearrange("p b i -> p (b i)"), in_=dp1.rearrange("(p b) i -> p (b i)", b=PACK))
-        dp_part = {(0, half): dp_first[:, :, half * HALF:(half + 1) * HALF] for half in range(2)}
-        for half in range(2):
-            t_ = held([P, PACK, HALF], F32, "dp_second%d" % half)
-            nc.sync.dma_start(out=t_[:], in_=dp2.rearrange("(p b) i -> p b i", b=PACK)[:, :, half * HALF:(half + 1) * HALF])
-            dp_part[1, half] = t_[:]
+        cols = [us_col, load_column("w1_col", w1), load_column("w2_col", w2)]
+        dp_raw = []
+        for h, dp in enumerate((dp1, dp2)):
+            t_ = held([P, PACK, SLOTS], F32, "dp_raw%d" % h)
+            nc.sync.dma_start(out=t_[:].rearrange("p b i -> p (b i)"), in_=dp.rearrange("(p b) i -> p (b i)", b=PACK))
+            dp_raw.append(t_)
 
         ident = held([P, P], F32, "ident")
         make_identity(nc, ident[:])
@@ -171,23 +171,21 @@ def tile_attend_ggqa_sig_k_pl_kernel(tc, q1, q2, kT, dp1, dp2, us, ts, w1, w2, o
         nc.scalar.copy(out=ts_col[:], in_=ps[:, 0:512:P])
         ts_neg = held([P, BLOCKS], F32, "ts_neg")
         nc.scalar.activation(out=ts_neg[:], in_=ps[:, 0:512:P], func=ACT.Copy, scale=-0.25)
-        ts_bank = bank("c", 4)
-        for b in range(BLOCKS):
-            nc.tensor.transpose(ts_bank[:, b * P:(b + 1) * P], ts_neg[:, b:b + 1].to_broadcast([P, P]), ident[:])
-        factor = []
-
-        def make_factor(h):
-            factor.append(held([P, PACK, SLOTS], F32, "factor%d" % h, tag="q_raw%d" % h))
-            for b in range(PACK):
-                nc.scalar.activation(out=factor[h][:, b, :], in_=ts_bank[:], func=ACT.Copy, scale=gate[h][:, b:b + 1])
-
-        make_factor(0)
+        ts_pos = held([P, BLOCKS], F32, "ts_pos")
+        nc.scalar.activation(out=ts_pos[:], in_=ps[:, 0:512:P], func=ACT.Copy, scale=0.25)
         nc.scalar.copy(out=k_view[:, :, 0:2], in_=k_pair[:].rearrange("p e c -> p c e"))
-        make_factor(1)
         gather_keys(2, 0, SLOTS)
 
         order = [(h, 2 * half + b) for half in range(2) for h in range(2) for b in range(2)]
         squares = []
+
+        def square(n):
+            nc.scalar.activation(out=squares[n][:], in_=squares[n][:], func=ACT.Square)
+            if MODES[n] == "S":
+                ib = order[n][1]
+                nc.scalar.activation(out=squares[n][:], in_=squares[n][:], func=ACT.Identity,
+                                     scale=ts_neg[:, ib:ib + 1], bias=ts_pos[:, ib:ib + 1])
+
         for h, ib in order:
             blk = slice(ib * P, (ib + 1) * P)
             if h == 0 and ib % 2 == 0:
@@ -197,24 +195,18 @@ def tile_attend_ggqa_sig_k_pl_kernel(tc, q1, q2, kT, dp1, dp2, us, ts, w1, w2, o
             nc.tensor.matmul_mx(out=score[:], lhsT=k_codes[:, blk].bitcast(E4M3), lhsT_scale=k_scales[:, blk],
                                 rhs=qd_codes[h][:].bitcast(E4M3), rhs_scale=qd_scales[h][:], start=True, stop=True)
             arg = held([P, R], F32, "arg%d_%d" % (h, ib))
-            nc.vector.tensor_tensor(out=arg[:], in0=score[:], in1=us_half[:], op=ALU.mult)
+            nc.vector.tensor_tensor(out=arg[:], in0=us_half[:], in1=score[:], op=ALU.mult)
             nc.scalar.activation(out=arg[:], in_=arg[:], func=ACT.Tanh, scale=ts_col[:, ib:ib + 1])
-            if squares:
-                nc.scalar.activation(out=squares[-1][:], in_=squares[-1][:], func=ACT.Square)
             squares.append(arg)
-        nc.scalar.activation(out=squares[-1][:], in_=squares[-1][:], func=ACT.Square)
-        scaled = {}
-
-        def scale_dp(h, half, tag):
-            scaled[h, half] = held([P, HALF * PACK], F32, "scaled%d_%d" % (h, half), tag=tag)
-            nc.gpsimd.tensor_tensor(
-                out=scaled[h, half][:].rearrange("p (i t) -> p i t", t=PACK),
-                in0=dp_part[h, half].rearrange("p t i -> p i t"),
-                in1=factor[h][:, :, half * HALF:(half + 1) * HALF].rearrange("p t i -> p i t"), op=ALU.mult)
-
-        scale_dp(0, 0, "qr1_grouped")
-        scale_dp(1, 0, None)
-        scale_dp(0, 1, "dp_second0")
+            if len(squares) > 1:
+                square(len(squares) - 2)
+        square(len(squares) - 1)
+        scaled = []
+        for h, tag in enumerate(("qr1_grouped", "dp_raw0")):
+            scaled.append(held([P, PACK, SLOTS], F32, "scaled%d" % h, tag=tag))
+            for b in range(PACK):
+                nc.gpsimd.tensor_scalar(out=scaled[h][:, b, :], in0=dp_raw[h][:, b, :], scalar1=gate[h][:, b:b + 1], scalar2=0.0,
+                                        op0=ALU.mult, op1=ALU.add)
         g_grouped = {(h, half): held([P, HALF * PACK], BF16, "g%d_%d" % (h, half), tag="us_half" if h + half == 0 else None)
                      for h in range(2) for half in range(2)}
 
@@ -232,6 +224,11 @@ def tile_attend_ggqa_sig_k_pl_kernel(tc, q1, q2, kT, dp1, dp2, us, ts, w1, w2, o
         slopes = {}
 
         def turn(n):
+            if MODES[n] != "S":
+                ib = order[n][1]
+                engine = nc.gpsimd if MODES[n] == "G" else nc.vector
+                engine.tensor_scalar(out=squares[n][:], in0=squares[n][:], scalar1=ts_neg[:, ib:ib + 1], scalar2=ts_pos[:, ib:ib + 1],
+                                     op0=ALU.mult, op1=ALU.add)
             slopes[n] = bank("c", 4)
             for t in range(PACK):
                 nc.tensor.transpose(slopes[n][:, t * P:(t + 1) * P], squares[n][:, t * P:(t + 1) * P], ident[:])
@@ -239,10 +236,10 @@ def tile_attend_ggqa_sig_k_pl_kernel(tc, q1, q2, kT, dp1, dp2, us, ts, w1, w2, o
         def gradient(n):
             h, ib = order[n]
             span = slice(PACK * P * (ib % 2), PACK * P * (ib % 2 + 1))
-            nc.vector.scalar_tensor_tensor(
-                out=g_grouped[h, ib // 2][:, span].rearrange("p (i t) -> p i t", t=PACK),
-                in0=slopes[n][:].rearrange("p (t i) -> p i t", t=PACK), scalar=-1.0,
-                in1=scaled[h, ib // 2][:, PACK * P * (ib % 2):PACK * P * (ib % 2 + 1)].rearrange("p (i t) -> p i t", t=PACK), op0=ALU.add, op1=ALU.mult)
+            nc.vector.tensor_tensor(
+                out=g_grouped[h, ib // 2][:, span].rearrange("p (c i t) -> p c t i", i=4, t=PACK),
+                in0=scaled[h][:, :, ib * P:(ib + 1) * P].rearrange("p t (c i) -> p c t i", i=4),
+                in1=slopes[n][:].rearrange("p (t c i) -> p c t i", i=4, t=PACK), op=ALU.mult)
 
         def quantize_half(half):
             for h in range(2):
@@ -258,18 +255,17 @@ def tile_attend_ggqa_sig_k_pl_kernel(tc, q1, q2, kT, dp1, dp2, us, ts, w1, w2, o
         turn(4)
         turn(5)
         quantize_half(0)
-        scale_dp(1, 1, "g1_0")
         early = [products(j) for j in range(SPLIT_PLANES)]
         gradient(4)
-        gradient(5)
-        parts[0, 0] = held([P, HALF], F32, "low0", tag="arg0_3")
+        parts[0, 0] = held([P, HALF], F32, "low0", tag="arg0_2")
         nc.vector.tensor_copy(out=parts[0, 0][:], in_=early[0][:, 0:HALF])
         scatter_half(0, 0)
+        gradient(5)
         for n in (6, 7):
             turn(n)
             gradient(n)
         quantize_half(1)
-        parts[1, 0] = held([P, HALF], F32, "low1", tag="g1_0")
+        parts[1, 0] = held([P, HALF], F32, "low1", tag="dp_raw0")
         nc.scalar.copy(out=parts[1, 0][:], in_=early[1][:, 0:HALF])
 
         out_planes = out_0.rearrange("(p j) c -> p j c", j=PACK)
@@ -295,33 +291,60 @@ def tile_attend_ggqa_sig_k_pl_kernel(tc, q1, q2, kT, dp1, dp2, us, ts, w1, w2, o
         for j, tag in ((2, "g0_1"), (3, "g1_1")):
             windows.append(held([P, TOKENS], F32, "window%d" % j, tag=tag))
             nc.gpsimd.memset(windows[j][:], 0.0)
+        direct = held([P, DIRECT * PACK], BF16, "direct")
+        direct_view = direct[:].rearrange("p (c t) -> p c t", t=PACK)
+
+        def round_on_gpsimd(out, in_):
+            nc.gpsimd.tensor_scalar(out=out, in0=in_, scalar1=1.0, scalar2=-0.0, op0=ALU.mult, op1=ALU.add)
+
+        def twice(ap, n):
+            return ap.unsqueeze(2).to_broadcast([P, n, 2])
+
+        shared = TOKENS - GPSIMD_COLUMNS
         for j in range(PACK):
             if j < SPLIT_PLANES:
                 scatter_half(j, HALF)
             else:
                 nc.vector.tensor_copy(out=windows[j][:].indirect(offsets[:]), in_=listed[j][:])
             nc.sync.dma_start(out=out_planes[:, j, :], in_=windows[j][:])
-            scalar_end = TOKENS - GPSIMD_COLUMNS if j < 2 else TOKENS
-            for span in (spans if j == PACK - 1 else [slice(0, scalar_end)]):
-                nc.scalar.copy(out=pair_view[:, j // 2, span, j % 2], in_=windows[j][:, span])
             if j < 2:
-                nc.gpsimd.tensor_scalar(out=pair_view[:, 0, scalar_end:TOKENS, j], in0=windows[j][:, scalar_end:TOKENS],
-                                        scalar1=1.0, scalar2=-0.0, op0=ALU.mult, op1=ALU.add)
-        y_grouped = []
+                nc.scalar.copy(out=pair_view[:, 0, DIRECT:TOKENS, j], in_=windows[j][:, DIRECT:TOKENS])
+                if j == 0:
+                    round_on_gpsimd(direct_view[:, :, 0], windows[j][:, 0:DIRECT])
+                else:
+                    round_on_gpsimd(direct_view[:, :, 1:3], twice(windows[j][:, 0:DIRECT], DIRECT))
+            elif j == 2:
+                nc.scalar.copy(out=direct_view[:, :, 2:4], in_=twice(windows[j][:, 0:DIRECT], DIRECT))
+                nc.scalar.copy(out=pair_view[:, 1, DIRECT:shared, 0], in_=windows[j][:, DIRECT:shared])
+                round_on_gpsimd(pair_view[:, 1, shared:TOKENS, :], twice(windows[j][:, shared:TOKENS], GPSIMD_COLUMNS))
+            else:
+                nc.vector.tensor_copy(out=direct_view[:, :, 3], in_=windows[j][:, 0:DIRECT])
+                for span in spans[DIRECT // PIECE:]:
+                    nc.scalar.copy(out=pair_view[:, 1, span, 1], in_=windows[j][:, span])
+        y_grouped = {c: direct[:, c * PIECE * PACK:(c + 1) * PIECE * PACK] for c in range(DIRECT // PIECE)}
 
         def quantize_piece(c):
-            nc.vector.quantize_mx(out=y_codes[:, spans[c]].bitcast(E4M3), scales=y_scales[4 * (c // 2):P, (c % 2) * PIECE:(c % 2 + 1) * PIECE], in_=y_grouped[c][:])
+            nc.vector.quantize_mx(out=y_codes[:, spans[c]].bitcast(E4M3), scales=y_scales[4 * (c // 2):P, (c % 2) * PIECE:(c % 2 + 1) * PIECE], in_=y_grouped[c])
             if c in STORE_AFTER:
                 done = [-1] + [e for e in STORE_AFTER if e < c]
                 part = slice(PIECE * (done[-1] + 1), spans[c].stop)
                 nc.sync.dma_start(out=words_out[:, part], in_=y_codes[:, part].bitcast(I32))
 
-        for c, span in enumerate(spans):
-            mover = nc.vector.tensor_copy if c < VECTOR_PIECES else nc.scalar.copy
-            y_grouped.append(held([P, PIECE * PACK], BF16, "y_grouped%d" % c))
-            mover(out=y_grouped[c][:].bitcast(F32).rearrange("p (c u) -> p c u", u=2), in_=pair_words[:, span, :])
-            if c > 0:
-                quantize_piece(c - 1)
+        def interleave(c):
+            if c < VECTOR_PIECES:
+                t_ = keep.tile([P, PIECE * PACK], BF16, name="y_vector", tag="y_vector", bufs=3, align_bytes=64)
+                mover = nc.vector.tensor_copy
+            else:
+                t_ = held([P, PIECE * PACK], BF16, "y_scalar%d" % c)
+                mover = nc.scalar.copy
+            y_grouped[c] = t_[:]
+            mover(out=t_[:].bitcast(F32).rearrange("p (c u) -> p c u", u=2), in_=pair_words[:, spans[c], :])
+
+        interleave(2)
+        nc.vector.quantize_mx(out=y_codes[:, 0:DIRECT].bitcast(E4M3), scales=y_scales[:, 0:DIRECT], in_=direct[:])
+        for c in range(3, len(spans)):
+            interleave(c)
+            quantize_piece(c - 1)
         quantize_piece(len(spans) - 1)
         scales_out = out_2.rearrange("a f c -> (a f) c").bitcast(I32).rearrange("f (a c) -> a f c", a=PACK)
         for quad in range(4):

@@ -23,7 +23,7 @@ PACK = 4
 BLOCKS = SLOTS // P
 PIECE = 256
 VECTOR_PIECES = 5
-MODES = "SVVVGGGG"
+MODES = "SSTTGGGG"
 STORE_AFTER = (3, 6, 7)
 SPLIT_PLANES = 2
 GPSIMD_COLUMNS = 896
@@ -180,6 +180,8 @@ def tile_attend_ggqa_sig_k_pl_kernel(tc, q1, q2, kT, dp1, dp2, us, ts, w1, w2, o
         squares = []
 
         def square(n):
+            if MODES[n] == "T":
+                return
             nc.scalar.activation(out=squares[n][:], in_=squares[n][:], func=ACT.Square)
             if MODES[n] == "S":
                 ib = order[n][1]
@@ -224,14 +226,22 @@ def tile_attend_ggqa_sig_k_pl_kernel(tc, q1, q2, kT, dp1, dp2, us, ts, w1, w2, o
         slopes = {}
 
         def turn(n):
-            if MODES[n] != "S":
-                ib = order[n][1]
+            ib = order[n][1]
+            if MODES[n] == "T":
+                nc.vector.scalar_tensor_tensor(out=squares[n][:], in0=squares[n][:], scalar=ts_neg[:, ib:ib + 1], in1=squares[n][:],
+                                               op0=ALU.mult, op1=ALU.mult)
+            elif MODES[n] != "S":
                 engine = nc.gpsimd if MODES[n] == "G" else nc.vector
                 engine.tensor_scalar(out=squares[n][:], in0=squares[n][:], scalar1=ts_neg[:, ib:ib + 1], scalar2=ts_pos[:, ib:ib + 1],
                                      op0=ALU.mult, op1=ALU.add)
             slopes[n] = bank("c", 4)
             for t in range(PACK):
-                nc.tensor.transpose(slopes[n][:, t * P:(t + 1) * P], squares[n][:, t * P:(t + 1) * P], ident[:])
+                out = slopes[n][:, t * P:(t + 1) * P]
+                if MODES[n] == "T":
+                    nc.tensor.matmul(out, lhsT=ts_pos[:, ib:ib + 1].to_broadcast([P, P]), rhs=ident[:], start=True, stop=False, is_transpose=True)
+                    nc.tensor.matmul(out, lhsT=squares[n][:, t * P:(t + 1) * P], rhs=ident[:], start=False, stop=True, is_transpose=True)
+                else:
+                    nc.tensor.transpose(out, squares[n][:, t * P:(t + 1) * P], ident[:])
 
         def gradient(n):
             h, ib = order[n]

@@ -18,16 +18,15 @@ P = 128
 D = 512
 R = 512
 SLOTS = 512
+HALF = SLOTS // 2
 TOKENS = 2048
 PACK = 4
 BLOCKS = SLOTS // P
-PIECE = 256
-VECTOR_PIECES = 5
-MODES = "SSTTGGGG"
-STORE_AFTER = (3, 6, 7)
-SPLIT_PLANES = 2
-GPSIMD_COLUMNS = 896
-DIRECT = 512
+PIECE = 512
+PIECES = TOKENS // PIECE
+SLOPE_ENGINES = "VVGGGGGV"
+GPSIMD_TOKENS = 1664
+SCALAR_ROW_SETS = 0
 FLOPS = 4 * 2 * D * R * SLOTS
 
 
@@ -37,90 +36,80 @@ def tile_attend_ggqa_sig_k_pl_kernel(tc, q1, q2, kT, dp1, dp2, us, ts, w1, w2, o
         keep = ctx.enter_context(tc.tile_pool(name="keep", bufs=1))
         psum = ctx.enter_context(tc.psum_pool(name="psum", bufs=1))
 
-        def held(shape, dtype, name, tag=None):
-            return keep.tile(shape, dtype, name=name, tag=tag or name, align_bytes=64)
+        def held(shape, dtype, name, tag=None, bufs=1):
+            return keep.tile(shape, dtype, name=name, tag=tag or name, bufs=bufs, align_bytes=64)
 
-        def bank(tag, bufs):
-            return psum.tile([P, 512], F32, name=tag, tag=tag, bufs=bufs)
+        def bank(tag):
+            return psum.tile([P, 512], F32, name=tag, tag=tag, bufs=1)
 
         offsets = keep.tile([P, SLOTS // 16], U16, name="offsets")
         ts_row = held([P, TOKENS], F32, "ts_row")
 
-        def zero_beside_gpsimd(t_):
-            nc.vector.memset(t_[:, 0:1025], 0.0)
-            nc.vector.memset(t_[:, 1025:TOKENS], 0.0)
+        def clear_on_vector(t_, lo, hi):
+            odd = (lo + hi) // 2 + 1
+            nc.vector.memset(t_[:, lo:odd], 0.0)
+            nc.vector.memset(t_[:, odd:hi], 0.0)
 
-        zero_beside_gpsimd(ts_row)
+        clear_on_vector(ts_row, 0, TOKENS)
 
         def load_column(name, vec):
             t_ = held([P, PACK], F32, name)
             nc.sync.dma_start(out=t_[:], in_=vec.rearrange("(p b) o -> p (b o)", b=PACK))
             return t_
 
+        def load_rows(name, mat):
+            t_ = held([P, PACK, 512], F32, name)
+            nc.sync.dma_start(out=t_[:].rearrange("p j r -> p (j r)"), in_=mat.rearrange("(p j) r -> p (j r)", j=PACK))
+            return t_
+
         nc.sync.dma_start(offsets[:], offs)
         us_col = load_column("us_col", us)
-        q_raw = []
-        for h, q in enumerate((q1, q2)):
-            t_ = held([P, PACK, R], F32, "q_raw%d" % h)
-            nc.sync.dma_start(out=t_[:].rearrange("p j r -> p (j r)"), in_=q.rearrange("(p j) r -> p (j r)", j=PACK))
-            q_raw.append(t_)
-            if h == 0:
-                nc.sync.dma_start(out=ts_row[0:1, :], in_=ts[0:1, :])
-
+        q_raw = [load_rows("q_raw0", q1)]
+        nc.sync.dma_start(out=ts_row[0:1, :], in_=ts[0:1, :])
+        q_raw.append(load_rows("q_raw1", q2))
         k_planes = kT.rearrange("(p j) c -> p j c", j=PACK)
         k_raw = []
         for j in range(PACK):
             t_ = held([P, TOKENS], F32, "k_raw%d" % j)
             nc.sync.dma_start(out=t_[:], in_=k_planes[:, j, :])
             k_raw.append(t_)
-        HALF = SLOTS // 2
-        cols = [us_col, load_column("w1_col", w1), load_column("w2_col", w2)]
-        dp_raw = []
-        for h, dp in enumerate((dp1, dp2)):
-            t_ = held([P, PACK, SLOTS], F32, "dp_raw%d" % h)
-            nc.sync.dma_start(out=t_[:].rearrange("p b i -> p (b i)"), in_=dp.rearrange("(p b) i -> p (b i)", b=PACK))
-            dp_raw.append(t_)
+        w_col = [load_column("w1_col", w1), load_column("w2_col", w2)]
+        dp_raw = [load_rows("dp_raw0", dp1), load_rows("dp_raw1", dp2)]
 
         ident = held([P, P], F32, "ident")
         make_identity(nc, ident[:])
-        windows = [held([P, TOKENS], F32, "window%d" % j) for j in range(2)]
-        nc.vector.memset(windows[0][:, 0:513], 0.0)
-        nc.vector.memset(windows[0][:, 513:1024], 0.0)
-        nc.gpsimd.memset(windows[1][:], 0.0)
-        nc.gpsimd.memset(windows[0][:, 1024:TOKENS], 0.0)
-        g_all_codes = held([P, 2 * SLOTS], U32, "g_codes")
-        g_all_scales = held([P, 2 * SLOTS], U8, "g_scales")
-        nc.vector.memset(g_all_codes[:].bitcast(I32).rearrange("p (h u c) -> p h u c", h=2, u=2)[:, :, 1, :], 0)
-        nc.vector.memset(g_all_scales[:].bitcast(I32), 0)
+        windows = [held([P, TOKENS], F32, "window%d" % j) for j in range(PACK)]
+        clear_on_vector(windows[0], 0, TOKENS)
+        clear_on_vector(windows[1], 0, TOKENS // 2)
+        nc.gpsimd.memset(windows[1][:, TOKENS // 2:TOKENS], 0.0)
+        for j in (2, 3):
+            nc.gpsimd.memset(windows[j][:], 0.0)
 
         def quantize(grouped, codes, scales, fmt, lo, hi):
             nc.vector.quantize_mx(out=codes[:, lo:hi].bitcast(fmt), scales=scales[:, lo:hi],
                                   in_=grouped[:, PACK * lo:PACK * hi])
 
-        def mx_tiles(width, name):
-            return (held([P, width * PACK], BF16, name + "_grouped"), held([P, width], U32, name + "_codes"),
+        def mx_tiles(width, name, tag=None):
+            return (held([P, width * PACK], BF16, name + "_grouped", tag=tag), held([P, width], U32, name + "_codes"),
                     held([P, width], U8, name + "_scales"))
 
         qd = [mx_tiles(R, "qd%d" % h) for h in range(2)]
         qr = [mx_tiles(D, "qr%d" % h) for h in range(2)]
-        qd_codes, qd_scales = [t_[1] for t_ in qd], [t_[2] for t_ in qd]
-        qr_codes, qr_scales = [t_[1] for t_ in qr], [t_[2] for t_ in qr]
 
-        def group_along_d(h, mover, lo=0, hi=P):
-            mover(out=qd[h][0][:].rearrange("p (i m t) -> p m t i", i=PACK, t=PACK)[:, lo:hi],
-                  in_=q_raw[h][:].rearrange("p t (m i) -> p m t i", i=PACK)[:, lo:hi])
+        def group_along_d(h):
+            nc.vector.tensor_copy(out=qd[h][0][:].rearrange("p (i m t) -> p m t i", i=PACK, t=PACK),
+                                  in_=q_raw[h][:].rearrange("p t (m i) -> p m t i", i=PACK))
 
-        rounded = []
-        for h in range(2):
-            t_ = held([P, PACK * R], BF16, "q_rounded%d" % h)
-            nc.scalar.copy(out=t_[:], in_=q_raw[h][:].rearrange("p j r -> p (j r)"))
-            rounded.append(t_)
+        rounded = [held([P, PACK * R], BF16, "q_rounded%d" % h) for h in range(2)]
+
+        def round_queries(h):
+            nc.scalar.copy(out=rounded[h][:], in_=q_raw[h][:].rearrange("p j r -> p (j r)"))
 
         def group_along_r(h):
             words = rounded[h][:].bitcast(F32)
             turned_words = qr[h][0][:].bitcast(F32)
             for half in range(2):
-                ps = bank("a", 4)
+                ps = bank("a%d" % (2 * h + half))
                 for jj in range(2):
                     j = 2 * half + jj
                     for u in range(2):
@@ -130,41 +119,25 @@ def tile_attend_ggqa_sig_k_pl_kernel(tc, q1, q2, kT, dp1, dp2, us, ts, w1, w2, o
                     out=turned_words[:, 512 * half:512 * (half + 1)].rearrange("p (j m u) -> p j m u", j=2, u=2),
                     in_=ps[:].rearrange("p (j u m) -> p j m u", j=2, u=2))
 
-        def gather_keys(j, lo, hi):
-            nc.vector.tensor_copy(out=k_view[:, lo:hi, j], in_=k_raw[j][:].indirect(offsets[:, lo // 16:hi // 16]))
-
-        ps = bank("c", 4)
+        ps = bank("c0")
         for b in range(PACK):
             nc.tensor.transpose(ps[:, b * P:(b + 1) * P], us_col[:, b:b + 1].to_broadcast([P, P]), ident[:])
         us_half = held([P, R], F32, "us_half")
         nc.scalar.activation(out=us_half[:], in_=ps[:], func=ACT.Copy, scale=0.5)
 
-        group_along_d(0, nc.vector.tensor_copy)
+        round_queries(0)
+        round_queries(1)
+        group_along_d(0)
         group_along_r(0)
         quantize(*qd[0], E4M3, 0, R)
-
-        ts_listed = held([P, SLOTS], F32, "ts_listed")
-        nc.vector.tensor_copy(out=ts_listed[:], in_=ts_row[:].indirect(offsets[:]))
-        gate = []
-        for h in range(2):
-            t_ = held([P, PACK], F32, "gate%d" % h)
-            nc.gpsimd.tensor_tensor(out=t_[:], in0=cols[1 + h][:], in1=us_col[:], op=ALU.mult)
-            gate.append(t_)
-
-        group_along_d(1, nc.vector.tensor_copy)
+        group_along_d(1)
         group_along_r(1)
         quantize(*qd[1], E4M3, 0, R)
         quantize(*qr[0], E4M3, 0, D)
-        k_pair = held([P, 2, SLOTS], BF16, "k_pair", tag="ts_row")
-        for j in range(2):
-            nc.vector.tensor_copy(out=k_pair[:, j, :], in_=k_raw[j][:].indirect(offsets[:]))
         quantize(*qr[1], E4M3, 0, D)
-        k_grouped = held([P, SLOTS * PACK], BF16, "k_grouped", tag="qr1_grouped")
-        k_codes = held([P, SLOTS], U32, "k_codes")
-        k_scales = held([P, SLOTS], U8, "k_scales")
-        keys = (k_grouped, k_codes, k_scales)
-        k_view = k_grouped[:].rearrange("p (c t) -> p c t", t=PACK)
-        ps = bank("c", 4)
+        ts_listed = held([P, SLOTS], F32, "ts_listed")
+        nc.scalar.activation(out=ts_listed[:], in_=ts_row[:].indirect(offsets[:]), func=ACT.Copy)
+        ps = bank("c1")
         for b in range(BLOCKS):
             nc.tensor.transpose(ps[:, b * P:(b + 1) * P], ts_listed[:, b * P:(b + 1) * P], ident[:])
         ts_col = held([P, BLOCKS], F32, "ts_col")
@@ -173,189 +146,208 @@ def tile_attend_ggqa_sig_k_pl_kernel(tc, q1, q2, kT, dp1, dp2, us, ts, w1, w2, o
         nc.scalar.activation(out=ts_neg[:], in_=ps[:, 0:512:P], func=ACT.Copy, scale=-0.25)
         ts_pos = held([P, BLOCKS], F32, "ts_pos")
         nc.scalar.activation(out=ts_pos[:], in_=ps[:, 0:512:P], func=ACT.Copy, scale=0.25)
-        nc.scalar.copy(out=k_view[:, :, 0:2], in_=k_pair[:].rearrange("p e c -> p c e"))
-        gather_keys(2, 0, SLOTS)
+
+        keys = [mx_tiles(HALF, "k0", tag="qr1_grouped"), mx_tiles(HALF, "k1")]
+        k_view = [t_[0][:].rearrange("p (c t) -> p c t", t=PACK) for t_ in keys]
+
+        def listed(lo, hi):
+            return offsets[:, lo // 16:hi // 16]
+
+        def gather_keys(j, half):
+            nc.vector.tensor_copy(out=k_view[half][:, :, j], in_=k_raw[j][:].indirect(listed(half * HALF, (half + 1) * HALF)))
+
+        for j in range(2):
+            gather_keys(j, 1)
+        for j in range(PACK):
+            gather_keys(j, 0)
+        k_late = held([P, 2, HALF], BF16, "k_late", tag="q_rounded1")
+        for j in (2, 3):
+            nc.scalar.activation(out=k_late[:, j - 2, :], in_=k_raw[j][:].indirect(listed(HALF, SLOTS)), func=ACT.Copy)
+        nc.scalar.copy(out=k_view[1][:, :, 2:4], in_=k_late[:].rearrange("p e c -> p c e"))
+
+        gate = []
+        for h in range(2):
+            t_ = held([P, PACK], F32, "gate%d" % h)
+            nc.gpsimd.tensor_tensor(out=t_[:], in0=w_col[h][:], in1=us_col[:], op=ALU.mult)
+            gate.append(t_)
+
+        scaled = [held([P, PACK, SLOTS], F32, "scaled%d" % h, tag=tag) for h, tag in enumerate(("k_raw2", "k_raw3"))]
+        for h in range(2):
+            for b in range(PACK):
+                if h == 0 and b < SCALAR_ROW_SETS:
+                    nc.scalar.activation(out=scaled[h][:, b, :], in_=dp_raw[h][:, b, :], func=ACT.Copy, scale=gate[h][:, b:b + 1])
+                else:
+                    nc.gpsimd.tensor_scalar(out=scaled[h][:, b, :], in0=dp_raw[h][:, b, :],
+                                            scalar1=gate[h][:, b:b + 1], scalar2=0.0, op0=ALU.mult, op1=ALU.add)
 
         order = [(h, 2 * half + b) for half in range(2) for h in range(2) for b in range(2)]
         squares = []
 
         def square(n):
-            if MODES[n] == "T":
+            if SLOPE_ENGINES[n] == "T":
                 return
             nc.scalar.activation(out=squares[n][:], in_=squares[n][:], func=ACT.Square)
-            if MODES[n] == "S":
-                ib = order[n][1]
-                nc.scalar.activation(out=squares[n][:], in_=squares[n][:], func=ACT.Identity,
-                                     scale=ts_neg[:, ib:ib + 1], bias=ts_pos[:, ib:ib + 1])
 
-        for h, ib in order:
-            blk = slice(ib * P, (ib + 1) * P)
-            if h == 0 and ib % 2 == 0:
-                gather_keys(3, ib * P, (ib + 2) * P)
-                quantize(*keys, E4M3, ib * P, (ib + 2) * P)
-            score = bank("a", 4)
-            nc.tensor.matmul_mx(out=score[:], lhsT=k_codes[:, blk].bitcast(E4M3), lhsT_scale=k_scales[:, blk],
-                                rhs=qd_codes[h][:].bitcast(E4M3), rhs_scale=qd_scales[h][:], start=True, stop=True)
-            arg = held([P, R], F32, "arg%d_%d" % (h, ib))
+        for half in range(2):
+            quantize(*keys[half], E4M3, 0, HALF)
+        for n, (h, ib) in enumerate(order):
+            blk = slice(ib % 2 * P, (ib % 2 + 1) * P)
+            score = bank("a%d" % (n % 4))
+            nc.tensor.matmul_mx(out=score[:], lhsT=keys[ib // 2][1][:, blk].bitcast(E4M3), lhsT_scale=keys[ib // 2][2][:, blk],
+                                rhs=qd[h][1][:].bitcast(E4M3), rhs_scale=qd[h][2][:], start=True, stop=True)
+            arg = held([P, R], F32, "arg%d" % n)
             nc.vector.tensor_tensor(out=arg[:], in0=us_half[:], in1=score[:], op=ALU.mult)
             nc.scalar.activation(out=arg[:], in_=arg[:], func=ACT.Tanh, scale=ts_col[:, ib:ib + 1])
             squares.append(arg)
-            if len(squares) > 1:
-                square(len(squares) - 2)
-        square(len(squares) - 1)
-        scaled = []
-        for h, tag in enumerate(("qr1_grouped", "dp_raw0")):
-            scaled.append(held([P, PACK, SLOTS], F32, "scaled%d" % h, tag=tag))
-            for b in range(PACK):
-                nc.gpsimd.tensor_scalar(out=scaled[h][:, b, :], in0=dp_raw[h][:, b, :], scalar1=gate[h][:, b:b + 1], scalar2=0.0,
-                                        op0=ALU.mult, op1=ALU.add)
-        g_grouped = {(h, half): held([P, HALF * PACK], BF16, "g%d_%d" % (h, half), tag="us_half" if h + half == 0 else None)
-                     for h in range(2) for half in range(2)}
+            if n > 0:
+                square(n - 1)
+        square(len(order) - 1)
 
-        def products(j):
-            ps = bank("a", 4)
-            blk = slice(j * P, (j + 1) * P)
-            for h in range(2):
-                lo = h * SLOTS
-                nc.tensor.matmul_mx(out=ps[:], lhsT=qr_codes[h][:, blk].bitcast(E4M3), lhsT_scale=qr_scales[h][:, blk],
-                                    rhs=g_all_codes[:, lo:lo + SLOTS].bitcast(E5M2), rhs_scale=g_all_scales[:, lo:lo + SLOTS],
-                                    start=h == 0, stop=h == 1)
-            return ps
-
-        parts = {}
-        slopes = {}
+        g = {(h, half): mx_tiles(HALF, "g%d_%d" % (h, half), tag="us_half" if h + half == 0 else None) for h in range(2) for half in range(2)}
+        turned = {}
+        slopes = {"G": held([P, sum(e == "G" for e in SLOPE_ENGINES), R], F32, "slopes_g", tag="dp_raw1"),
+                  "V": held([P, sum(e == "V" for e in SLOPE_ENGINES), R], F32, "slopes_v")}
 
         def turn(n):
             ib = order[n][1]
-            if MODES[n] == "T":
-                nc.vector.scalar_tensor_tensor(out=squares[n][:], in0=squares[n][:], scalar=ts_neg[:, ib:ib + 1], in1=squares[n][:],
+            slope = slopes[SLOPE_ENGINES[n]][:, sum(e == SLOPE_ENGINES[n] for e in SLOPE_ENGINES[:n]), :]
+            if SLOPE_ENGINES[n] == "T":
+                nc.vector.scalar_tensor_tensor(out=slope, in0=squares[n][:], scalar=ts_neg[:, ib:ib + 1], in1=squares[n][:],
                                                op0=ALU.mult, op1=ALU.mult)
-            elif MODES[n] != "S":
-                engine = nc.gpsimd if MODES[n] == "G" else nc.vector
-                engine.tensor_scalar(out=squares[n][:], in0=squares[n][:], scalar1=ts_neg[:, ib:ib + 1], scalar2=ts_pos[:, ib:ib + 1],
+            elif SLOPE_ENGINES[n] == "S":
+                nc.scalar.activation(out=slope, in_=squares[n][:], func=ACT.Identity,
+                                     scale=ts_neg[:, ib:ib + 1], bias=ts_pos[:, ib:ib + 1])
+            else:
+                engine = nc.gpsimd if SLOPE_ENGINES[n] == "G" else nc.vector
+                engine.tensor_scalar(out=slope, in0=squares[n][:], scalar1=ts_neg[:, ib:ib + 1], scalar2=ts_pos[:, ib:ib + 1],
                                      op0=ALU.mult, op1=ALU.add)
-            slopes[n] = bank("c", 4)
+            turned[n] = bank("c%d" % (n % 4))
             for t in range(PACK):
-                out = slopes[n][:, t * P:(t + 1) * P]
-                if MODES[n] == "T":
+                out = turned[n][:, t * P:(t + 1) * P]
+                if SLOPE_ENGINES[n] == "T":
                     nc.tensor.matmul(out, lhsT=ts_pos[:, ib:ib + 1].to_broadcast([P, P]), rhs=ident[:], start=True, stop=False, is_transpose=True)
-                    nc.tensor.matmul(out, lhsT=squares[n][:, t * P:(t + 1) * P], rhs=ident[:], start=False, stop=True, is_transpose=True)
+                    nc.tensor.matmul(out, lhsT=slope[:, t * P:(t + 1) * P], rhs=ident[:], start=False, stop=True, is_transpose=True)
                 else:
-                    nc.tensor.transpose(out, squares[n][:, t * P:(t + 1) * P], ident[:])
+                    nc.tensor.transpose(out, slope[:, t * P:(t + 1) * P], ident[:])
 
         def gradient(n):
             h, ib = order[n]
-            span = slice(PACK * P * (ib % 2), PACK * P * (ib % 2 + 1))
+            b = ib % 2
             nc.vector.tensor_tensor(
-                out=g_grouped[h, ib // 2][:, span].rearrange("p (c i t) -> p c t i", i=4, t=PACK),
+                out=g[h, ib // 2][0][:, PACK * P * b:PACK * P * (b + 1)].rearrange("p (c i t) -> p c t i", i=4, t=PACK),
                 in0=scaled[h][:, :, ib * P:(ib + 1) * P].rearrange("p t (c i) -> p c t i", i=4),
-                in1=slopes[n][:].rearrange("p (t c i) -> p c t i", i=4, t=PACK), op=ALU.mult)
+                in1=turned[n][:].rearrange("p (t c i) -> p c t i", i=4, t=PACK), op=ALU.mult)
 
-        def quantize_half(half):
-            for h in range(2):
-                lo = h * SLOTS + half * HALF
-                quantize(g_grouped[h, half], g_all_codes[:, lo:lo + HALF], g_all_scales[:, lo:lo + HALF], E5M2, 0, HALF)
+        def products(j, half, out, heads=(0, 1)):
+            blk = slice(j * P, (j + 1) * P)
+            for h in heads:
+                nc.tensor.matmul_mx(out=out, lhsT=qr[h][1][:, blk].bitcast(E4M3), lhsT_scale=qr[h][2][:, blk],
+                                    rhs=g[h, half][1][:].bitcast(E5M2), rhs_scale=g[h, half][2][:],
+                                    start=h == 0, stop=h == 1)
 
-        def scatter_half(j, lo):
-            nc.vector.tensor_copy(out=windows[j][:].indirect(offsets[:, lo // 16:(lo + HALF) // 16]), in_=parts[j, lo][:])
-
-        for n in range(4):
-            turn(n)
+        sums = [bank("a%d" % j) for j in range(2)]
+        turn(0)
+        for n, (h, ib) in enumerate(order):
+            if n + 1 < len(order):
+                turn(n + 1)
+            else:
+                quantize(*g[1, 1], E5M2, 0, P)
             gradient(n)
-        turn(4)
-        turn(5)
-        quantize_half(0)
-        early = [products(j) for j in range(SPLIT_PLANES)]
-        gradient(4)
-        parts[0, 0] = held([P, HALF], F32, "low0", tag="arg0_2")
-        nc.vector.tensor_copy(out=parts[0, 0][:], in_=early[0][:, 0:HALF])
-        scatter_half(0, 0)
-        gradient(5)
-        for n in (6, 7):
-            turn(n)
-            gradient(n)
-        quantize_half(1)
-        parts[1, 0] = held([P, HALF], F32, "low1", tag="dp_raw0")
-        nc.scalar.copy(out=parts[1, 0][:], in_=early[1][:, 0:HALF])
+            if n in (1, 3, 5):
+                quantize(*g[h, ib // 2], E5M2, 0, HALF)
+            if n == 6:
+                for head in range(2):
+                    for j in range(2):
+                        products(j, 0, sums[j][:, 0:HALF], heads=(head,))
+        first1 = held([P, HALF], F32, "first1", tag="k_raw3")
+        nc.vector.tensor_copy(out=first1[:], in_=sums[1][:, 0:HALF])
+        quantize(*g[1, 1], E5M2, P, HALF)
 
         out_planes = out_0.rearrange("(p j) c -> p j c", j=PACK)
-        spans = [slice(lo, lo + PIECE) for lo in range(0, TOKENS, PIECE)]
-        pairs = held([P, PACK * TOKENS], BF16, "pairs", tag="g_codes")
+
+        def scatter(on_scalar, j, values, lo, hi):
+            target = windows[j][:].indirect(listed(lo, hi))
+            if on_scalar:
+                nc.scalar.activation(out=target, in_=values, func=ACT.Copy)
+            else:
+                nc.vector.tensor_copy(out=target, in_=values)
+
+        def store_plane(j):
+            queue = nc.scalar if j == 0 else nc.sync
+            queue.dma_start(out=out_planes[:, j, :], in_=windows[j][:])
+
+        first0 = held([P, HALF], F32, "first0", tag="arg6")
+        nc.scalar.copy(out=first0[:], in_=sums[0][:, 0:HALF])
+        scatter(True, 0, first0[:], 0, HALF)
+        products(0, 1, sums[0][:, HALF:SLOTS])
+        shared = bank("a3")
+        products(3, 0, shared[:, HALF:SLOTS])
+        products(1, 1, shared[:, 0:HALF])
+        sum2 = bank("a2")
+        for half in range(2):
+            products(2, half, sum2[:, half * HALF:(half + 1) * HALF])
+        products(3, 1, sums[1][:, HALF:SLOTS])
+        scatter(False, 1, first1[:], 0, HALF)
+        second0 = held([P, HALF], F32, "second0", tag="q_raw0")
+        nc.scalar.copy(out=second0[:], in_=sums[0][:, HALF:SLOTS])
+        scatter(True, 0, second0[:], HALF, SLOTS)
+        store_plane(0)
+        rest = held([P, 3 * HALF], F32, "rest")
+        nc.vector.tensor_copy(out=rest[:, 0:SLOTS], in_=shared[:])
+        nc.vector.tensor_copy(out=rest[:, SLOTS:3 * HALF], in_=sums[1][:, HALF:SLOTS])
+        scatter(False, 1, rest[:, 0:HALF], HALF, SLOTS)
+        store_plane(1)
+        whole2 = held([P, SLOTS], F32, "whole2")
+        nc.scalar.copy(out=whole2[:], in_=sum2[:])
+        for half in range(2):
+            scatter(True, 2, whole2[:, half * HALF:(half + 1) * HALF], half * HALF, (half + 1) * HALF)
+        store_plane(2)
+        scatter(False, 3, rest[:, HALF:3 * HALF], 0, SLOTS)
+        store_plane(3)
+
+        pairs = held([P, PACK * TOKENS], BF16, "pairs", tag="q_raw0")
         pair_view = pairs[:].rearrange("p (u c e) -> p u c e", u=2, e=2)
         pair_words = pairs[:].bitcast(F32).rearrange("p (u c) -> p c u", u=2)
-        for j in range(SPLIT_PLANES):
-            ps = products(j)
-            parts[j, HALF] = held([P, HALF], F32, "high%d" % j)
-            nc.scalar.copy(out=parts[j, HALF][:], in_=ps[:, HALF:SLOTS])
-        listed = [None] * SPLIT_PLANES
-        for j in range(SPLIT_PLANES, PACK):
-            dk = products(j)
-            t_ = held([P, SLOTS], F32, "dk%d" % j)
-            nc.scalar.copy(out=t_[:], in_=dk[:])
-            listed.append(t_)
         y_codes = held([P, TOKENS], U32, "y_codes")
         y_scales = held([P, TOKENS // PACK], U8, "y_scales")
         words_out = out_1.rearrange("a p c t -> p (a c t)").bitcast(I32)
+        spans = [slice(c * PIECE, (c + 1) * PIECE) for c in range(PIECES)]
 
-        scatter_half(1, 0)
-        for j, tag in ((2, "g0_1"), (3, "g1_1")):
-            windows.append(held([P, TOKENS], F32, "window%d" % j, tag=tag))
-            nc.gpsimd.memset(windows[j][:], 0.0)
-        direct = held([P, DIRECT * PACK], BF16, "direct")
-        direct_view = direct[:].rearrange("p (c t) -> p c t", t=PACK)
-
-        def round_on_gpsimd(out, in_):
-            nc.gpsimd.tensor_scalar(out=out, in0=in_, scalar1=1.0, scalar2=-0.0, op0=ALU.mult, op1=ALU.add)
-
-        def twice(ap, n):
-            return ap.unsqueeze(2).to_broadcast([P, n, 2])
-
-        shared = TOKENS - GPSIMD_COLUMNS
-        for j in range(PACK):
-            if j < SPLIT_PLANES:
-                scatter_half(j, HALF)
+        def round_into_pairs(engine, j, span):
+            out, in_ = pair_view[:, j // 2, span, j % 2], windows[j][:, span]
+            if engine == "G":
+                nc.gpsimd.tensor_scalar(out=out, in0=in_, scalar1=1.0, scalar2=-0.0, op0=ALU.mult, op1=ALU.add)
+            elif engine == "S":
+                nc.scalar.copy(out=out, in_=in_)
             else:
-                nc.vector.tensor_copy(out=windows[j][:].indirect(offsets[:]), in_=listed[j][:])
-            nc.sync.dma_start(out=out_planes[:, j, :], in_=windows[j][:])
-            if j < 2:
-                nc.scalar.copy(out=pair_view[:, 0, DIRECT:TOKENS, j], in_=windows[j][:, DIRECT:TOKENS])
-                if j == 0:
-                    round_on_gpsimd(direct_view[:, :, 0], windows[j][:, 0:DIRECT])
-                else:
-                    round_on_gpsimd(direct_view[:, :, 1:3], twice(windows[j][:, 0:DIRECT], DIRECT))
-            elif j == 2:
-                nc.scalar.copy(out=direct_view[:, :, 2:4], in_=twice(windows[j][:, 0:DIRECT], DIRECT))
-                nc.scalar.copy(out=pair_view[:, 1, DIRECT:shared, 0], in_=windows[j][:, DIRECT:shared])
-                round_on_gpsimd(pair_view[:, 1, shared:TOKENS, :], twice(windows[j][:, shared:TOKENS], GPSIMD_COLUMNS))
-            else:
-                nc.vector.tensor_copy(out=direct_view[:, :, 3], in_=windows[j][:, 0:DIRECT])
-                for span in spans[DIRECT // PIECE:]:
-                    nc.scalar.copy(out=pair_view[:, 1, span, 1], in_=windows[j][:, span])
-        y_grouped = {c: direct[:, c * PIECE * PACK:(c + 1) * PIECE * PACK] for c in range(DIRECT // PIECE)}
+                nc.vector.tensor_copy(out=out, in_=in_)
+
+        split = TOKENS - GPSIMD_TOKENS
+        last = PIECES - 1
+        round_into_pairs("G", 0, slice(split, TOKENS))
+        round_into_pairs("G", 1, slice(split, 2 * PIECE))
+        round_into_pairs("G", 1, slice(2 * PIECE, TOKENS))
+        for j in range(2):
+            round_into_pairs("S", j, slice(0, split))
+        for j in (2, 3):
+            round_into_pairs("S", j, spans[last])
+        grouped = {}
+
+        def interleave(c, mover):
+            grouped[c] = held([P, PIECE * PACK], BF16, "y_grouped%d" % c, tag="k_raw%d" % c)
+            mover(out=grouped[c][:].bitcast(F32).rearrange("p (c u) -> p c u", u=2), in_=pair_words[:, spans[c], :])
 
         def quantize_piece(c):
-            nc.vector.quantize_mx(out=y_codes[:, spans[c]].bitcast(E4M3), scales=y_scales[4 * (c // 2):P, (c % 2) * PIECE:(c % 2 + 1) * PIECE], in_=y_grouped[c])
-            if c in STORE_AFTER:
-                done = [-1] + [e for e in STORE_AFTER if e < c]
-                part = slice(PIECE * (done[-1] + 1), spans[c].stop)
-                nc.sync.dma_start(out=words_out[:, part], in_=y_codes[:, part].bitcast(I32))
+            nc.vector.quantize_mx(out=y_codes[:, spans[c]].bitcast(E4M3), scales=y_scales[4 * c:P, :], in_=grouped[c][:])
+            nc.sync.dma_start(out=words_out[:, spans[c]], in_=y_codes[:, spans[c]].bitcast(I32))
 
-        def interleave(c):
-            if c < VECTOR_PIECES:
-                t_ = keep.tile([P, PIECE * PACK], BF16, name="y_vector", tag="y_vector", bufs=3, align_bytes=64)
-                mover = nc.vector.tensor_copy
-            else:
-                t_ = held([P, PIECE * PACK], BF16, "y_scalar%d" % c)
-                mover = nc.scalar.copy
-            y_grouped[c] = t_[:]
-            mover(out=t_[:].bitcast(F32).rearrange("p (c u) -> p c u", u=2), in_=pair_words[:, spans[c], :])
-
-        interleave(2)
-        nc.vector.quantize_mx(out=y_codes[:, 0:DIRECT].bitcast(E4M3), scales=y_scales[:, 0:DIRECT], in_=direct[:])
-        for c in range(3, len(spans)):
-            interleave(c)
-            quantize_piece(c - 1)
-        quantize_piece(len(spans) - 1)
+        for c in range(last):
+            for j in (2, 3):
+                round_into_pairs("V", j, spans[c])
+            interleave(c, nc.scalar.copy)
+        interleave(last, nc.vector.tensor_copy)
+        for c in (0, last, 1, 2):
+            quantize_piece(c)
         scales_out = out_2.rearrange("a f c -> (a f) c").bitcast(I32).rearrange("f (a c) -> a f c", a=PACK)
         for quad in range(4):
             queue = nc.sync if quad % 2 == 0 else nc.scalar

@@ -24,9 +24,9 @@ PACK = 4
 BLOCKS = SLOTS // P
 PIECE = 512
 PIECES = TOKENS // PIECE
-SLOPE_ENGINES = "VVGGGGGV"
-GPSIMD_TOKENS = 1664
+SLOPE_ENGINES = "VVGGGGSS"
 SCALAR_ROW_SETS = 0
+LOW_TOKENS = 768
 FLOPS = 4 * 2 * D * R * SLOTS
 
 
@@ -78,11 +78,9 @@ def tile_attend_ggqa_sig_k_pl_kernel(tc, q1, q2, kT, dp1, dp2, us, ts, w1, w2, o
 
         ident = held([P, P], F32, "ident")
         make_identity(nc, ident[:])
-        windows = [held([P, TOKENS], F32, "window%d" % j) for j in range(PACK)]
+        windows = [held([P, TOKENS], F32, "window%d" % j) for j in range(3)]
         clear_on_vector(windows[0], 0, TOKENS)
-        clear_on_vector(windows[1], 0, TOKENS // 2)
-        nc.gpsimd.memset(windows[1][:, TOKENS // 2:TOKENS], 0.0)
-        for j in (2, 3):
+        for j in (1, 2):
             nc.gpsimd.memset(windows[j][:], 0.0)
 
         def quantize(grouped, codes, scales, fmt, lo, hi):
@@ -165,6 +163,8 @@ def tile_attend_ggqa_sig_k_pl_kernel(tc, q1, q2, kT, dp1, dp2, us, ts, w1, w2, o
             nc.scalar.activation(out=k_late[:, j - 2, :], in_=k_raw[j][:].indirect(listed(HALF, SLOTS)), func=ACT.Copy)
         nc.scalar.copy(out=k_view[1][:, :, 2:4], in_=k_late[:].rearrange("p e c -> p c e"))
 
+        windows.append(held([P, TOKENS], F32, "window3", tag="k_raw0"))
+        nc.gpsimd.memset(windows[3][:], 0.0)
         gate = []
         for h in range(2):
             t_ = held([P, PACK], F32, "gate%d" % h)
@@ -203,10 +203,15 @@ def tile_attend_ggqa_sig_k_pl_kernel(tc, q1, q2, kT, dp1, dp2, us, ts, w1, w2, o
                 square(n - 1)
         square(len(order) - 1)
 
-        g = {(h, half): mx_tiles(HALF, "g%d_%d" % (h, half), tag="us_half" if h + half == 0 else None) for h in range(2) for half in range(2)}
+        g_halves = [(held([P, 2 * HALF * PACK], BF16, "g%d_grouped" % half, tag=("us_half", None)[half]),
+                     held([P, 2 * HALF], U32, "g%d_codes" % half, tag=("arg5", None)[half]),
+                     held([P, 2 * HALF], U8, "g%d_scales" % half)) for half in range(2)]
+        g = {(h, half): (g_halves[half][0][:, PACK * HALF * h:PACK * HALF * (h + 1)], g_halves[half][1][:, HALF * h:HALF * (h + 1)],
+                         g_halves[half][2][:, HALF * h:HALF * (h + 1)]) for h in range(2) for half in range(2)}
         turned = {}
         slopes = {"G": held([P, sum(e == "G" for e in SLOPE_ENGINES), R], F32, "slopes_g", tag="dp_raw1"),
-                  "V": held([P, sum(e == "V" for e in SLOPE_ENGINES), R], F32, "slopes_v")}
+                  "V": held([P, sum(e == "V" for e in SLOPE_ENGINES), R], F32, "slopes_v"),
+                  "S": held([P, sum(e == "S" for e in SLOPE_ENGINES), R], F32, "slopes_s")}
 
         def turn(n):
             ib = order[n][1]
@@ -242,7 +247,7 @@ def tile_attend_ggqa_sig_k_pl_kernel(tc, q1, q2, kT, dp1, dp2, us, ts, w1, w2, o
             blk = slice(j * P, (j + 1) * P)
             for h in heads:
                 nc.tensor.matmul_mx(out=out, lhsT=qr[h][1][:, blk].bitcast(E4M3), lhsT_scale=qr[h][2][:, blk],
-                                    rhs=g[h, half][1][:].bitcast(E5M2), rhs_scale=g[h, half][2][:],
+                                    rhs=g[h, half][1].bitcast(E5M2), rhs_scale=g[h, half][2],
                                     start=h == 0, stop=h == 1)
 
         sums = [bank("a%d" % j) for j in range(2)]
@@ -253,8 +258,10 @@ def tile_attend_ggqa_sig_k_pl_kernel(tc, q1, q2, kT, dp1, dp2, us, ts, w1, w2, o
             else:
                 quantize(*g[1, 1], E5M2, 0, P)
             gradient(n)
-            if n in (1, 3, 5):
-                quantize(*g[h, ib // 2], E5M2, 0, HALF)
+            if n == 4:
+                quantize(*g_halves[0], E5M2, 0, 2 * HALF)
+            if n == 5:
+                quantize(*g[0, 1], E5M2, 0, HALF)
             if n == 6:
                 for head in range(2):
                     for j in range(2):
@@ -276,14 +283,14 @@ def tile_attend_ggqa_sig_k_pl_kernel(tc, q1, q2, kT, dp1, dp2, us, ts, w1, w2, o
             queue = nc.scalar if j == 0 else nc.sync
             queue.dma_start(out=out_planes[:, j, :], in_=windows[j][:])
 
-        first0 = held([P, HALF], F32, "first0", tag="arg6")
+        first0 = held([P, HALF], F32, "first0", tag="arg7")
         nc.scalar.copy(out=first0[:], in_=sums[0][:, 0:HALF])
         scatter(True, 0, first0[:], 0, HALF)
         products(0, 1, sums[0][:, HALF:SLOTS])
-        shared = bank("a3")
+        shared = bank("c1")
         products(3, 0, shared[:, HALF:SLOTS])
         products(1, 1, shared[:, 0:HALF])
-        sum2 = bank("a2")
+        sum2 = bank("c2")
         for half in range(2):
             products(2, half, sum2[:, half * HALF:(half + 1) * HALF])
         products(3, 1, sums[1][:, HALF:SLOTS])
@@ -305,48 +312,46 @@ def tile_attend_ggqa_sig_k_pl_kernel(tc, q1, q2, kT, dp1, dp2, us, ts, w1, w2, o
         scatter(False, 3, rest[:, HALF:3 * HALF], 0, SLOTS)
         store_plane(3)
 
-        pairs = held([P, PACK * TOKENS], BF16, "pairs", tag="q_raw0")
-        pair_view = pairs[:].rearrange("p (u c e) -> p u c e", u=2, e=2)
-        pair_words = pairs[:].bitcast(F32).rearrange("p (u c) -> p c u", u=2)
+        sides = [slice(0, LOW_TOKENS), slice(LOW_TOKENS, TOKENS)]
+        pairs = {1: held([P, PACK * (TOKENS - LOW_TOKENS)], BF16, "pairs1", tag="q_raw0"),
+                 0: held([P, PACK * LOW_TOKENS], BF16, "pairs0", tag="whole2")}
         y_codes = held([P, TOKENS], U32, "y_codes")
         y_scales = held([P, TOKENS // PACK], U8, "y_scales")
         words_out = out_1.rearrange("a p c t -> p (a c t)").bitcast(I32)
         spans = [slice(c * PIECE, (c + 1) * PIECE) for c in range(PIECES)]
 
-        def round_into_pairs(engine, j, span):
-            out, in_ = pair_view[:, j // 2, span, j % 2], windows[j][:, span]
-            if engine == "G":
-                nc.gpsimd.tensor_scalar(out=out, in0=in_, scalar1=1.0, scalar2=-0.0, op0=ALU.mult, op1=ALU.add)
-            elif engine == "S":
-                nc.scalar.copy(out=out, in_=in_)
-            else:
-                nc.vector.tensor_copy(out=out, in_=in_)
+        def round_on_gpsimd(out, in_):
+            nc.gpsimd.tensor_scalar(out=out, in0=in_, scalar1=1.0, scalar2=-0.0, op0=ALU.mult, op1=ALU.add)
 
-        split = TOKENS - GPSIMD_TOKENS
-        last = PIECES - 1
-        round_into_pairs("G", 0, slice(split, TOKENS))
-        round_into_pairs("G", 1, slice(split, 2 * PIECE))
-        round_into_pairs("G", 1, slice(2 * PIECE, TOKENS))
-        for j in range(2):
-            round_into_pairs("S", j, slice(0, split))
-        for j in (2, 3):
-            round_into_pairs("S", j, spans[last])
-        grouped = {}
+        def round_into_pairs(mover, j, side):
+            mover(out=pairs[side][:].rearrange("p (u c e) -> p u c e", u=2, e=2)[:, j // 2, :, j % 2],
+                  in_=windows[j][:, sides[side]])
 
-        def interleave(c, mover):
-            grouped[c] = held([P, PIECE * PACK], BF16, "y_grouped%d" % c, tag="k_raw%d" % c)
-            mover(out=grouped[c][:].bitcast(F32).rearrange("p (c u) -> p c u", u=2), in_=pair_words[:, spans[c], :])
+        grouped = [held([P, PIECE * PACK], BF16, "y_grouped%d" % c, tag=tag) for c, tag in enumerate(("dp_raw0", "k_raw1", "k_raw2", "k_raw3"))]
+
+        def interleave(mover, lo, hi):
+            side, c = int(lo >= LOW_TOKENS), lo // PIECE
+            words = pairs[side][:].bitcast(F32).rearrange("p (u c) -> p c u", u=2)
+            out = grouped[c][:].bitcast(F32).rearrange("p (c u) -> p c u", u=2)
+            mover(out=out[:, lo - c * PIECE:hi - c * PIECE, :], in_=words[:, lo - sides[side].start:hi - sides[side].start, :])
 
         def quantize_piece(c):
             nc.vector.quantize_mx(out=y_codes[:, spans[c]].bitcast(E4M3), scales=y_scales[4 * c:P, :], in_=grouped[c][:])
             nc.sync.dma_start(out=words_out[:, spans[c]], in_=y_codes[:, spans[c]].bitcast(I32))
 
-        for c in range(last):
+        for j in range(2):
+            round_into_pairs(round_on_gpsimd, j, 1)
+        for j in range(2):
+            round_into_pairs(nc.scalar.copy, j, 0)
+        for side in (1, 0):
             for j in (2, 3):
-                round_into_pairs("V", j, spans[c])
-            interleave(c, nc.scalar.copy)
-        interleave(last, nc.vector.tensor_copy)
-        for c in (0, last, 1, 2):
+                round_into_pairs(nc.vector.tensor_copy, j, side)
+        interleave(nc.scalar.copy, 2 * PIECE, 3 * PIECE)
+        interleave(nc.scalar.copy, 3 * PIECE, TOKENS)
+        interleave(nc.scalar.copy, LOW_TOKENS, 2 * PIECE)
+        interleave(nc.vector.tensor_copy, 0, PIECE)
+        interleave(nc.vector.tensor_copy, PIECE, LOW_TOKENS)
+        for c in (2, 0, 3, 1):
             quantize_piece(c)
         scales_out = out_2.rearrange("a f c -> (a f) c").bitcast(I32).rearrange("f (a c) -> a f c", a=PACK)
         for quad in range(4):

@@ -26,7 +26,6 @@ PIECE = 512
 PIECES = TOKENS // PIECE
 SLOPE_ENGINES = "VVGGGGSS"
 SCALAR_ROW_SETS = 0
-LOW_TOKENS = 768
 FLOPS = 4 * 2 * D * R * SLOTS
 
 
@@ -62,11 +61,10 @@ def tile_attend_ggqa_sig_k_pl_kernel(tc, q1, q2, kT, dp1, dp2, us, ts, w1, w2, o
             nc.sync.dma_start(out=t_[:].rearrange("p j r -> p (j r)"), in_=mat.rearrange("(p j) r -> p (j r)", j=PACK))
             return t_
 
+        q_raw = [load_rows("q_raw0", q1), load_rows("q_raw1", q2)]
         nc.sync.dma_start(offsets[:], offs)
         us_col = load_column("us_col", us)
-        q_raw = [load_rows("q_raw0", q1)]
         nc.sync.dma_start(out=ts_row[0:1, :], in_=ts[0:1, :])
-        q_raw.append(load_rows("q_raw1", q2))
         k_planes = kT.rearrange("(p j) c -> p j c", j=PACK)
         k_raw = []
         for j in range(PACK):
@@ -188,10 +186,10 @@ def tile_attend_ggqa_sig_k_pl_kernel(tc, q1, q2, kT, dp1, dp2, us, ts, w1, w2, o
                 return
             nc.scalar.activation(out=squares[n][:], in_=squares[n][:], func=ACT.Square)
 
-        for half in range(2):
-            quantize(*keys[half], E4M3, 0, HALF)
         for n, (h, ib) in enumerate(order):
             blk = slice(ib % 2 * P, (ib % 2 + 1) * P)
+            if n in (0, 2):
+                quantize(*keys[n // 2], E4M3, 0, HALF)
             score = bank("a%d" % (n % 4))
             nc.tensor.matmul_mx(out=score[:], lhsT=keys[ib // 2][1][:, blk].bitcast(E4M3), lhsT_scale=keys[ib // 2][2][:, blk],
                                 rhs=qd[h][1][:].bitcast(E4M3), rhs_scale=qd[h][2][:], start=True, stop=True)
@@ -312,48 +310,51 @@ def tile_attend_ggqa_sig_k_pl_kernel(tc, q1, q2, kT, dp1, dp2, us, ts, w1, w2, o
         scatter(False, 3, rest[:, HALF:3 * HALF], 0, SLOTS)
         store_plane(3)
 
-        sides = [slice(0, LOW_TOKENS), slice(LOW_TOKENS, TOKENS)]
-        pairs = {1: held([P, PACK * (TOKENS - LOW_TOKENS)], BF16, "pairs1", tag="q_raw0"),
-                 0: held([P, PACK * LOW_TOKENS], BF16, "pairs0", tag="whole2")}
+        rounded_first = held([P, PACK, PIECE], BF16, "rounded_first", tag="arg7")
+        rounded_rest = held([P, PACK, TOKENS - PIECE], BF16, "rounded_rest", tag="q_raw0")
         y_codes = held([P, TOKENS], U32, "y_codes")
-        y_scales = held([P, TOKENS // PACK], U8, "y_scales")
+        y_scales = held([P, 2 * PIECE], U8, "y_scales")
         words_out = out_1.rearrange("a p c t -> p (a c t)").bitcast(I32)
         spans = [slice(c * PIECE, (c + 1) * PIECE) for c in range(PIECES)]
 
         def round_on_gpsimd(out, in_):
             nc.gpsimd.tensor_scalar(out=out, in0=in_, scalar1=1.0, scalar2=-0.0, op0=ALU.mult, op1=ALU.add)
 
-        def round_into_pairs(mover, j, side):
-            mover(out=pairs[side][:].rearrange("p (u c e) -> p u c e", u=2, e=2)[:, j // 2, :, j % 2],
-                  in_=windows[j][:, sides[side]])
+        def round_first(mover, j):
+            mover(out=rounded_first[:, j, :], in_=windows[j][:, 0:PIECE])
 
-        grouped = [held([P, PIECE * PACK], BF16, "y_grouped%d" % c, tag=tag) for c, tag in enumerate(("dp_raw0", "k_raw1", "k_raw2", "k_raw3"))]
+        def round_rest(mover, j):
+            mover(out=rounded_rest[:, j, :], in_=windows[j][:, PIECE:TOKENS])
 
-        def interleave(mover, lo, hi):
-            side, c = int(lo >= LOW_TOKENS), lo // PIECE
-            words = pairs[side][:].bitcast(F32).rearrange("p (u c) -> p c u", u=2)
-            out = grouped[c][:].bitcast(F32).rearrange("p (c u) -> p c u", u=2)
-            mover(out=out[:, lo - c * PIECE:hi - c * PIECE, :], in_=words[:, lo - sides[side].start:hi - sides[side].start, :])
+        grouped_low = held([P, 2 * PIECE * PACK], BF16, "y_grouped_low", tag="dp_raw0")
+        grouped = [grouped_low[:, c * PIECE * PACK:(c + 1) * PIECE * PACK] for c in range(2)]
+        grouped += [held([P, PIECE * PACK], BF16, "y_grouped%d" % c, tag=tag)[:] for c, tag in ((2, "k_raw2"), (3, "arg7"))]
 
-        def quantize_piece(c):
-            nc.vector.quantize_mx(out=y_codes[:, spans[c]].bitcast(E4M3), scales=y_scales[4 * c:P, :], in_=grouped[c][:])
-            nc.sync.dma_start(out=words_out[:, spans[c]], in_=y_codes[:, spans[c]].bitcast(I32))
+        def interleave(mover, c):
+            planes = rounded_first[:] if c == 0 else rounded_rest[:, :, spans[c - 1]]
+            mover(out=grouped[c].rearrange("p (c i t) -> p c t i", i=4, t=PACK),
+                  in_=planes.rearrange("p t (c i) -> p c t i", i=4))
 
-        for j in range(2):
-            round_into_pairs(round_on_gpsimd, j, 1)
-        for j in range(2):
-            round_into_pairs(nc.scalar.copy, j, 0)
-        for side in (1, 0):
-            for j in (2, 3):
-                round_into_pairs(nc.vector.tensor_copy, j, side)
-        interleave(nc.scalar.copy, 2 * PIECE, 3 * PIECE)
-        interleave(nc.scalar.copy, 3 * PIECE, TOKENS)
-        interleave(nc.scalar.copy, LOW_TOKENS, 2 * PIECE)
-        interleave(nc.vector.tensor_copy, 0, PIECE)
-        interleave(nc.vector.tensor_copy, PIECE, LOW_TOKENS)
-        for c in (2, 0, 3, 1):
-            quantize_piece(c)
-        scales_out = out_2.rearrange("a f c -> (a f) c").bitcast(I32).rearrange("f (a c) -> a f c", a=PACK)
+        def quantize_tokens(span, scales, in_):
+            nc.vector.quantize_mx(out=y_codes[:, span].bitcast(E4M3), scales=scales, in_=in_)
+            nc.sync.dma_start(out=words_out[:, span], in_=y_codes[:, span].bitcast(I32))
+
+        round_rest(round_on_gpsimd, 0)
+        round_first(round_on_gpsimd, 0)
+        round_rest(round_on_gpsimd, 1)
+        for j in (1, 2):
+            round_first(nc.scalar.copy, j)
+        round_first(nc.vector.tensor_copy, 3)
+        interleave(nc.scalar.copy, 0)
+        for j in (3, 2):
+            round_rest(nc.vector.tensor_copy, j)
+        interleave(nc.vector.tensor_copy, 1)
+        interleave(nc.scalar.copy, 3)
+        interleave(nc.vector.tensor_copy, 2)
+        quantize_tokens(slice(0, 2 * PIECE), y_scales[:], grouped_low[:])
+        for c in (2, 3):
+            quantize_tokens(spans[c], y_scales[4:P, spans[c % 2]], grouped[c])
+        scales_out = out_2.rearrange("a f c -> (a f) c").bitcast(I32).rearrange("f (a c) -> a f c", a=2)
         for quad in range(4):
             queue = nc.sync if quad % 2 == 0 else nc.scalar
-            queue.dma_start(out=scales_out[:, 4 * quad:4 * quad + 4, :], in_=y_scales[32 * quad:32 * quad + 16, :].bitcast(I32))
+            queue.dma_start(out=scales_out[:, 4 * quad:4 * quad + 4, :], in_=y_scales[32 * quad:32 * quad + 8, :].bitcast(I32))

@@ -144,22 +144,18 @@ def tile_attend_ggqa_sig_k_pl_kernel(tc, q1, q2, kT, dp1, dp2, us, ts, w1, w2, o
         nc.scalar.activation(out=ts_pos[:], in_=ps[:, 0:512:P], func=ACT.Copy, scale=0.25)
 
         keys = [mx_tiles(HALF, "k0", tag="qr1_grouped"), mx_tiles(HALF, "k1")]
-        k_view = [t_[0][:].rearrange("p (c t) -> p c t", t=PACK) for t_ in keys]
+        k_view = keys[0][0][:].rearrange("p (c t) -> p c t", t=PACK)
 
         def listed(lo, hi):
             return offsets[:, lo // 16:hi // 16]
 
-        def gather_keys(j, half):
-            nc.vector.tensor_copy(out=k_view[half][:, :, j], in_=k_raw[j][:].indirect(listed(half * HALF, (half + 1) * HALF)))
-
-        for j in range(2):
-            gather_keys(j, 1)
         for j in range(PACK):
-            gather_keys(j, 0)
-        k_late = held([P, 2, HALF], BF16, "k_late", tag="q_rounded1")
-        for j in (2, 3):
-            nc.scalar.activation(out=k_late[:, j - 2, :], in_=k_raw[j][:].indirect(listed(HALF, SLOTS)), func=ACT.Copy)
-        nc.scalar.copy(out=k_view[1][:, :, 2:4], in_=k_late[:].rearrange("p e c -> p c e"))
+            nc.vector.tensor_copy(out=k_view[:, :, j], in_=k_raw[j][:].indirect(listed(0, HALF)))
+        k_late = held([P, PACK, HALF], BF16, "k_late", tag="q_rounded1")
+        for j in range(PACK):
+            nc.scalar.activation(out=k_late[:, j, :], in_=k_raw[j][:].indirect(listed(HALF, SLOTS)), func=ACT.Copy)
+        nc.scalar.copy(out=keys[1][0][:].rearrange("p (c i t) -> p c t i", i=4, t=PACK),
+                       in_=k_late[:].rearrange("p t (c i) -> p c t i", i=4))
 
         windows.append(held([P, TOKENS], F32, "window3", tag="k_raw0"))
         nc.gpsimd.memset(windows[3][:], 0.0)
@@ -284,31 +280,29 @@ def tile_attend_ggqa_sig_k_pl_kernel(tc, q1, q2, kT, dp1, dp2, us, ts, w1, w2, o
         first0 = held([P, HALF], F32, "first0", tag="arg7")
         nc.scalar.copy(out=first0[:], in_=sums[0][:, 0:HALF])
         scatter(True, 0, first0[:], 0, HALF)
-        products(0, 1, sums[0][:, HALF:SLOTS])
-        shared = bank("c1")
-        products(3, 0, shared[:, HALF:SLOTS])
-        products(1, 1, shared[:, 0:HALF])
-        sum2 = bank("c2")
+        for j in range(2):
+            products(j, 1, sums[j][:, HALF:SLOTS])
+        sums += [bank("c2"), bank("c1")]
         for half in range(2):
-            products(2, half, sum2[:, half * HALF:(half + 1) * HALF])
-        products(3, 1, sums[1][:, HALF:SLOTS])
+            for j in (2, 3):
+                products(j, half, sums[j][:, half * HALF:(half + 1) * HALF])
         scatter(False, 1, first1[:], 0, HALF)
         second0 = held([P, HALF], F32, "second0", tag="q_raw0")
         nc.scalar.copy(out=second0[:], in_=sums[0][:, HALF:SLOTS])
         scatter(True, 0, second0[:], HALF, SLOTS)
         store_plane(0)
-        rest = held([P, 3 * HALF], F32, "rest")
-        nc.vector.tensor_copy(out=rest[:, 0:SLOTS], in_=shared[:])
-        nc.vector.tensor_copy(out=rest[:, SLOTS:3 * HALF], in_=sums[1][:, HALF:SLOTS])
-        scatter(False, 1, rest[:, 0:HALF], HALF, SLOTS)
+        second1 = held([P, HALF], F32, "second1")
+        nc.vector.tensor_copy(out=second1[:], in_=sums[1][:, HALF:SLOTS])
+        scatter(False, 1, second1[:], HALF, SLOTS)
         store_plane(1)
-        whole2 = held([P, SLOTS], F32, "whole2")
-        nc.scalar.copy(out=whole2[:], in_=sum2[:])
+        whole = held([P, 2, SLOTS], F32, "whole", tag="q_raw1")
+        for j in (3, 2):
+            nc.scalar.copy(out=whole[:, j - 2, :], in_=sums[j][:])
         for half in range(2):
-            scatter(True, 2, whole2[:, half * HALF:(half + 1) * HALF], half * HALF, (half + 1) * HALF)
-        store_plane(2)
-        scatter(False, 3, rest[:, HALF:3 * HALF], 0, SLOTS)
+            scatter(True, 2, whole[:, 0, half * HALF:(half + 1) * HALF], half * HALF, (half + 1) * HALF)
+        scatter(False, 3, whole[:, 1, :], 0, SLOTS)
         store_plane(3)
+        store_plane(2)
 
         rounded_first = held([P, PACK, PIECE], BF16, "rounded_first", tag="arg7")
         rounded_rest = held([P, PACK, TOKENS - PIECE], BF16, "rounded_rest", tag="q_raw0")
@@ -352,8 +346,10 @@ def tile_attend_ggqa_sig_k_pl_kernel(tc, q1, q2, kT, dp1, dp2, us, ts, w1, w2, o
         interleave(nc.scalar.copy, 3)
         interleave(nc.vector.tensor_copy, 2)
         quantize_tokens(slice(0, 2 * PIECE), y_scales[:], grouped_low[:])
-        for c in (2, 3):
-            quantize_tokens(spans[c], y_scales[4:P, spans[c % 2]], grouped[c])
+        quantize_tokens(spans[2], y_scales[4:P, spans[0]], grouped[2])
+        for lo in range(0, PIECE, PIECE // 2):
+            hi = lo + PIECE // 2
+            quantize_tokens(slice(3 * PIECE + lo, 3 * PIECE + hi), y_scales[4:P, PIECE + lo:PIECE + hi], grouped[3][:, PACK * lo:PACK * hi])
         scales_out = out_2.rearrange("a f c -> (a f) c").bitcast(I32).rearrange("f (a c) -> a f c", a=2)
         for quad in range(4):
             queue = nc.sync if quad % 2 == 0 else nc.scalar

@@ -149,7 +149,11 @@ def tile_attend_ggqa_sig_k_pl_kernel(tc, q1, q2, kT, dp1, dp2, us, ts, w1, w2, o
         def listed(lo, hi):
             return offsets[:, lo // 16:hi // 16]
 
-        for j in range(PACK):
+        k_early = held([P, 2, HALF], BF16, "k_early")
+        for j in range(2):
+            nc.vector.tensor_copy(out=k_early[:, j, :], in_=k_raw[j][:].indirect(listed(0, HALF)))
+        nc.vector.tensor_copy(out=k_view[:, :, 0:2], in_=k_early[:].rearrange("p e c -> p c e"))
+        for j in (2, 3):
             nc.vector.tensor_copy(out=k_view[:, :, j], in_=k_raw[j][:].indirect(listed(0, HALF)))
         k_late = held([P, PACK, HALF], BF16, "k_late", tag="q_rounded1")
         for j in range(PACK):
@@ -157,8 +161,6 @@ def tile_attend_ggqa_sig_k_pl_kernel(tc, q1, q2, kT, dp1, dp2, us, ts, w1, w2, o
         nc.scalar.copy(out=keys[1][0][:].rearrange("p (c i t) -> p c t i", i=4, t=PACK),
                        in_=k_late[:].rearrange("p t (c i) -> p c t i", i=4))
 
-        windows.append(held([P, TOKENS], F32, "window3", tag="k_raw0"))
-        nc.gpsimd.memset(windows[3][:], 0.0)
         gate = []
         for h in range(2):
             t_ = held([P, PACK], F32, "gate%d" % h)
@@ -264,6 +266,9 @@ def tile_attend_ggqa_sig_k_pl_kernel(tc, q1, q2, kT, dp1, dp2, us, ts, w1, w2, o
         nc.vector.tensor_copy(out=first1[:], in_=sums[1][:, 0:HALF])
         quantize(*g[1, 1], E5M2, P, HALF)
 
+        windows.append(held([P, TOKENS], F32, "window3", tag="g1_grouped"))
+        nc.gpsimd.memset(windows[3][:], 0.0)
+
         out_planes = out_0.rearrange("(p j) c -> p j c", j=PACK)
 
         def scatter(on_scalar, j, values, lo, hi):
@@ -324,10 +329,10 @@ def tile_attend_ggqa_sig_k_pl_kernel(tc, q1, q2, kT, dp1, dp2, us, ts, w1, w2, o
         grouped = [grouped_low[:, c * PIECE * PACK:(c + 1) * PIECE * PACK] for c in range(2)]
         grouped += [held([P, PIECE * PACK], BF16, "y_grouped%d" % c, tag=tag)[:] for c, tag in ((2, "k_raw2"), (3, "arg7"))]
 
-        def interleave(mover, c):
+        def interleave(mover, c, lo=0, hi=PIECE):
             planes = rounded_first[:] if c == 0 else rounded_rest[:, :, spans[c - 1]]
-            mover(out=grouped[c].rearrange("p (c i t) -> p c t i", i=4, t=PACK),
-                  in_=planes.rearrange("p t (c i) -> p c t i", i=4))
+            mover(out=grouped[c][:, PACK * lo:PACK * hi].rearrange("p (c i t) -> p c t i", i=4, t=PACK),
+                  in_=planes[:, :, lo:hi].rearrange("p t (c i) -> p c t i", i=4))
 
         def quantize_tokens(span, scales, in_):
             nc.vector.quantize_mx(out=y_codes[:, span].bitcast(E4M3), scales=scales, in_=in_)
@@ -343,7 +348,8 @@ def tile_attend_ggqa_sig_k_pl_kernel(tc, q1, q2, kT, dp1, dp2, us, ts, w1, w2, o
         for j in (3, 2):
             round_rest(nc.vector.tensor_copy, j)
         interleave(nc.vector.tensor_copy, 1)
-        interleave(nc.scalar.copy, 3)
+        for lo in range(0, PIECE, PIECE // 2):
+            interleave(nc.scalar.copy, 3, lo, lo + PIECE // 2)
         interleave(nc.vector.tensor_copy, 2)
         quantize_tokens(slice(0, 2 * PIECE), y_scales[:], grouped_low[:])
         quantize_tokens(spans[2], y_scales[4:P, spans[0]], grouped[2])

@@ -21,11 +21,13 @@ SLOTS = 512
 HALF = SLOTS // 2
 TOKENS = 2048
 PACK = 4
-BLOCKS = SLOTS // P
+BANK = 512
+RUN = 4
 PIECE = 512
-PIECES = TOKENS // PIECE
-SLOPE_ENGINES = "VVGGGGSS"
-SCALAR_ROW_SETS = 0
+TILES = [(h, 2 * half + b) for half in range(2) for h in range(2) for b in range(2)]
+VECTOR_SLOPES = 2
+SCALAR_SLOPES = 2
+GPSIMD_SLOPES = len(TILES) - VECTOR_SLOPES - SCALAR_SLOPES
 FLOPS = 4 * 2 * D * R * SLOTS
 
 
@@ -35,222 +37,199 @@ def tile_attend_ggqa_sig_k_pl_kernel(tc, q1, q2, kT, dp1, dp2, us, ts, w1, w2, o
         keep = ctx.enter_context(tc.tile_pool(name="keep", bufs=1))
         psum = ctx.enter_context(tc.psum_pool(name="psum", bufs=1))
 
-        def held(shape, dtype, name, tag=None, bufs=1):
-            return keep.tile(shape, dtype, name=name, tag=tag or name, bufs=bufs, align_bytes=64)
+        def held(shape, dtype, name, tag=None):
+            return keep.tile(shape, dtype, name=name, tag=tag or name, align_bytes=64)
 
         def bank(tag):
-            return psum.tile([P, 512], F32, name=tag, tag=tag, bufs=1)
+            return psum.tile([P, BANK], F32, name=tag, tag=tag)
+
+        def clear_on_vector(tile):
+            odd = TOKENS // 2 + 1
+            nc.vector.memset(tile[:, 0:odd], 0.0)
+            nc.vector.memset(tile[:, odd:TOKENS], 0.0)
+
+        def load_column(name, vec):
+            tile = held([P, PACK], F32, name)
+            nc.sync.dma_start(out=tile[:], in_=vec.rearrange("(p t) o -> p (t o)", t=PACK))
+            return tile
+
+        def load_rows(name, mat):
+            tile = held([P, PACK, mat.shape[1]], F32, name)
+            nc.sync.dma_start(out=tile[:].rearrange("p t c -> p (t c)"), in_=mat.rearrange("(p t) c -> p (t c)", t=PACK))
+            return tile
 
         offsets = keep.tile([P, SLOTS // 16], U16, name="offsets")
         ts_row = held([P, TOKENS], F32, "ts_row")
-
-        def clear_on_vector(t_, lo, hi):
-            odd = (lo + hi) // 2 + 1
-            nc.vector.memset(t_[:, lo:odd], 0.0)
-            nc.vector.memset(t_[:, odd:hi], 0.0)
-
-        clear_on_vector(ts_row, 0, TOKENS)
-
-        def load_column(name, vec):
-            t_ = held([P, PACK], F32, name)
-            nc.sync.dma_start(out=t_[:], in_=vec.rearrange("(p b) o -> p (b o)", b=PACK))
-            return t_
-
-        def load_rows(name, mat):
-            t_ = held([P, PACK, 512], F32, name)
-            nc.sync.dma_start(out=t_[:].rearrange("p j r -> p (j r)"), in_=mat.rearrange("(p j) r -> p (j r)", j=PACK))
-            return t_
-
+        clear_on_vector(ts_row)
         q_raw = [load_rows("q_raw0", q1), load_rows("q_raw1", q2)]
         nc.sync.dma_start(offsets[:], offs)
         us_col = load_column("us_col", us)
         nc.sync.dma_start(out=ts_row[0:1, :], in_=ts[0:1, :])
-        k_planes = kT.rearrange("(p j) c -> p j c", j=PACK)
-        k_raw = []
-        for j in range(PACK):
-            t_ = held([P, TOKENS], F32, "k_raw%d" % j)
-            nc.sync.dma_start(out=t_[:], in_=k_planes[:, j, :])
-            k_raw.append(t_)
+        k_planes = kT.rearrange("(p t) c -> p t c", t=PACK)
+        k_raw = [held([P, TOKENS], F32, "k_raw%d" % t) for t in range(PACK)]
+        for t in range(PACK):
+            nc.sync.dma_start(out=k_raw[t][:], in_=k_planes[:, t, :])
         w_col = [load_column("w1_col", w1), load_column("w2_col", w2)]
         dp_raw = [load_rows("dp_raw0", dp1), load_rows("dp_raw1", dp2)]
 
         ident = held([P, P], F32, "ident")
         make_identity(nc, ident[:])
-        windows = [held([P, TOKENS], F32, "window%d" % j) for j in range(3)]
-        clear_on_vector(windows[0], 0, TOKENS)
-        for j in (1, 2):
-            nc.gpsimd.memset(windows[j][:], 0.0)
+        windows = [held([P, TOKENS], F32, "window%d" % t) for t in range(PACK - 1)]
+        clear_on_vector(windows[0])
+        for t in (1, 2):
+            nc.gpsimd.memset(windows[t][:], 0.0)
+
+        def listed(lo, hi):
+            return offsets[:, lo // 16:hi // 16]
+
+        def mx_tiles(width, name, grouped_tag=None, codes_tag=None):
+            return (held([P, width * PACK], BF16, name + "_grouped", tag=grouped_tag),
+                    held([P, width], U32, name + "_codes", tag=codes_tag), held([P, width], U8, name + "_scales"))
 
         def quantize(grouped, codes, scales, fmt, lo, hi):
             nc.vector.quantize_mx(out=codes[:, lo:hi].bitcast(fmt), scales=scales[:, lo:hi],
                                   in_=grouped[:, PACK * lo:PACK * hi])
 
-        def mx_tiles(width, name, tag=None):
-            return (held([P, width * PACK], BF16, name + "_grouped", tag=tag), held([P, width], U32, name + "_codes"),
-                    held([P, width], U8, name + "_scales"))
+        def interleave(mover, grouped, planes):
+            mover(out=grouped.rearrange("p (c i t) -> p c t i", i=RUN, t=PACK),
+                  in_=planes.rearrange("p t (c i) -> p c t i", i=RUN))
 
         qd = [mx_tiles(R, "qd%d" % h) for h in range(2)]
         qr = [mx_tiles(D, "qr%d" % h) for h in range(2)]
+        q_rounded = [held([P, PACK * R], BF16, "q_rounded%d" % h) for h in range(2)]
 
         def group_along_d(h):
             nc.vector.tensor_copy(out=qd[h][0][:].rearrange("p (i m t) -> p m t i", i=PACK, t=PACK),
                                   in_=q_raw[h][:].rearrange("p t (m i) -> p m t i", i=PACK))
 
-        rounded = [held([P, PACK * R], BF16, "q_rounded%d" % h) for h in range(2)]
-
-        def round_queries(h):
-            nc.scalar.copy(out=rounded[h][:], in_=q_raw[h][:].rearrange("p j r -> p (j r)"))
-
         def group_along_r(h):
-            words = rounded[h][:].bitcast(F32)
+            words = q_rounded[h][:].bitcast(F32)
             turned_words = qr[h][0][:].bitcast(F32)
-            for half in range(2):
-                ps = bank("a%d" % (2 * h + half))
+            row = R // 2
+            for pair in range(2):
+                ps = bank("a%d" % (2 * h + pair))
                 for jj in range(2):
-                    j = 2 * half + jj
+                    j = 2 * pair + jj
                     for u in range(2):
                         nc.tensor.transpose(ps[:, (2 * jj + u) * P:(2 * jj + u + 1) * P],
-                                            words[:, 256 * j + u:256 * (j + 1):2], ident[:])
+                                            words[:, row * j + u:row * (j + 1):2], ident[:])
                 nc.scalar.copy(
-                    out=turned_words[:, 512 * half:512 * (half + 1)].rearrange("p (j m u) -> p j m u", j=2, u=2),
+                    out=turned_words[:, BANK * pair:BANK * (pair + 1)].rearrange("p (j m u) -> p j m u", j=2, u=2),
                     in_=ps[:].rearrange("p (j u m) -> p j m u", j=2, u=2))
 
         ps = bank("c0")
-        for b in range(PACK):
-            nc.tensor.transpose(ps[:, b * P:(b + 1) * P], us_col[:, b:b + 1].to_broadcast([P, P]), ident[:])
+        for t in range(PACK):
+            nc.tensor.transpose(ps[:, t * P:(t + 1) * P], us_col[:, t:t + 1].to_broadcast([P, P]), ident[:])
         us_half = held([P, R], F32, "us_half")
         nc.scalar.activation(out=us_half[:], in_=ps[:], func=ACT.Copy, scale=0.5)
 
-        round_queries(0)
-        round_queries(1)
-        group_along_d(0)
-        group_along_r(0)
-        quantize(*qd[0], E4M3, 0, R)
-        group_along_d(1)
-        group_along_r(1)
-        quantize(*qd[1], E4M3, 0, R)
-        quantize(*qr[0], E4M3, 0, D)
-        quantize(*qr[1], E4M3, 0, D)
+        for h in range(2):
+            nc.scalar.copy(out=q_rounded[h][:], in_=q_raw[h][:].rearrange("p t r -> p (t r)"))
+        for h in range(2):
+            group_along_d(h)
+            group_along_r(h)
+            quantize(*qd[h], E4M3, 0, R)
+        for h in range(2):
+            quantize(*qr[h], E4M3, 0, D)
+
         ts_listed = held([P, SLOTS], F32, "ts_listed")
         nc.scalar.activation(out=ts_listed[:], in_=ts_row[:].indirect(offsets[:]), func=ACT.Copy)
         ps = bank("c1")
-        for b in range(BLOCKS):
+        for b in range(SLOTS // P):
             nc.tensor.transpose(ps[:, b * P:(b + 1) * P], ts_listed[:, b * P:(b + 1) * P], ident[:])
-        ts_col = held([P, BLOCKS], F32, "ts_col")
-        nc.scalar.copy(out=ts_col[:], in_=ps[:, 0:512:P])
-        ts_neg = held([P, BLOCKS], F32, "ts_neg")
-        nc.scalar.activation(out=ts_neg[:], in_=ps[:, 0:512:P], func=ACT.Copy, scale=-0.25)
-        ts_pos = held([P, BLOCKS], F32, "ts_pos")
-        nc.scalar.activation(out=ts_pos[:], in_=ps[:, 0:512:P], func=ACT.Copy, scale=0.25)
+        ts_col = held([P, SLOTS // P], F32, "ts_col")
+        nc.scalar.copy(out=ts_col[:], in_=ps[:, 0:SLOTS:P])
+        ts_neg = held([P, SLOTS // P], F32, "ts_neg")
+        nc.scalar.activation(out=ts_neg[:], in_=ps[:, 0:SLOTS:P], func=ACT.Copy, scale=-0.25)
+        ts_pos = held([P, SLOTS // P], F32, "ts_pos")
+        nc.scalar.activation(out=ts_pos[:], in_=ps[:, 0:SLOTS:P], func=ACT.Copy, scale=0.25)
 
-        keys = [mx_tiles(HALF, "k0", tag="qr1_grouped"), mx_tiles(HALF, "k1")]
-        k_view = keys[0][0][:].rearrange("p (c t) -> p c t", t=PACK)
-
-        def listed(lo, hi):
-            return offsets[:, lo // 16:hi // 16]
-
+        keys = [mx_tiles(HALF, "k0", grouped_tag="qr1_grouped"), mx_tiles(HALF, "k1")]
+        k_places = keys[0][0][:].rearrange("p (c t) -> p c t", t=PACK)
         k_early = held([P, 2, HALF], BF16, "k_early")
-        for j in range(2):
-            nc.vector.tensor_copy(out=k_early[:, j, :], in_=k_raw[j][:].indirect(listed(0, HALF)))
-        nc.vector.tensor_copy(out=k_view[:, :, 0:2], in_=k_early[:].rearrange("p e c -> p c e"))
-        for j in (2, 3):
-            nc.vector.tensor_copy(out=k_view[:, :, j], in_=k_raw[j][:].indirect(listed(0, HALF)))
+        for t in (0, 1):
+            nc.vector.tensor_copy(out=k_early[:, t, :], in_=k_raw[t][:].indirect(listed(0, HALF)))
+        nc.vector.tensor_copy(out=k_places[:, :, 0:2], in_=k_early[:].rearrange("p t c -> p c t"))
+        for t in (2, 3):
+            nc.vector.tensor_copy(out=k_places[:, :, t], in_=k_raw[t][:].indirect(listed(0, HALF)))
         k_late = held([P, PACK, HALF], BF16, "k_late", tag="q_rounded1")
-        for j in range(PACK):
-            nc.scalar.activation(out=k_late[:, j, :], in_=k_raw[j][:].indirect(listed(HALF, SLOTS)), func=ACT.Copy)
-        nc.scalar.copy(out=keys[1][0][:].rearrange("p (c i t) -> p c t i", i=4, t=PACK),
-                       in_=k_late[:].rearrange("p t (c i) -> p c t i", i=4))
+        for t in range(PACK):
+            nc.scalar.activation(out=k_late[:, t, :], in_=k_raw[t][:].indirect(listed(HALF, SLOTS)), func=ACT.Copy)
+        interleave(nc.scalar.copy, keys[1][0][:], k_late[:])
 
-        gate = []
+        gate = [held([P, PACK], F32, "gate%d" % h) for h in range(2)]
         for h in range(2):
-            t_ = held([P, PACK], F32, "gate%d" % h)
-            nc.gpsimd.tensor_tensor(out=t_[:], in0=w_col[h][:], in1=us_col[:], op=ALU.mult)
-            gate.append(t_)
-
-        scaled = [held([P, PACK, SLOTS], F32, "scaled%d" % h, tag=tag) for h, tag in enumerate(("k_raw2", "k_raw3"))]
+            nc.gpsimd.tensor_tensor(out=gate[h][:], in0=w_col[h][:], in1=us_col[:], op=ALU.mult)
+        scaled = [held([P, PACK, SLOTS], F32, "scaled%d" % h, tag="k_raw%d" % (2 + h)) for h in range(2)]
         for h in range(2):
-            for b in range(PACK):
-                if h == 0 and b < SCALAR_ROW_SETS:
-                    nc.scalar.activation(out=scaled[h][:, b, :], in_=dp_raw[h][:, b, :], func=ACT.Copy, scale=gate[h][:, b:b + 1])
-                else:
-                    nc.gpsimd.tensor_scalar(out=scaled[h][:, b, :], in0=dp_raw[h][:, b, :],
-                                            scalar1=gate[h][:, b:b + 1], scalar2=0.0, op0=ALU.mult, op1=ALU.add)
+            for t in range(PACK):
+                nc.gpsimd.tensor_scalar(out=scaled[h][:, t, :], in0=dp_raw[h][:, t, :],
+                                        scalar1=gate[h][:, t:t + 1], scalar2=0.0, op0=ALU.mult, op1=ALU.add)
 
-        order = [(h, 2 * half + b) for half in range(2) for h in range(2) for b in range(2)]
         squares = []
 
         def square(n):
-            if SLOPE_ENGINES[n] == "T":
-                return
             nc.scalar.activation(out=squares[n][:], in_=squares[n][:], func=ACT.Square)
 
-        for n, (h, ib) in enumerate(order):
-            blk = slice(ib % 2 * P, (ib % 2 + 1) * P)
-            if n in (0, 2):
-                quantize(*keys[n // 2], E4M3, 0, HALF)
+        for n, (h, b) in enumerate(TILES):
+            if n == 0:
+                quantize(*keys[0], E4M3, 0, HALF)
+            if n == 2:
+                quantize(*keys[1], E4M3, 0, HALF)
+            cols = slice(b % 2 * P, (b % 2 + 1) * P)
             score = bank("a%d" % (n % 4))
-            nc.tensor.matmul_mx(out=score[:], lhsT=keys[ib // 2][1][:, blk].bitcast(E4M3), lhsT_scale=keys[ib // 2][2][:, blk],
+            nc.tensor.matmul_mx(out=score[:], lhsT=keys[b // 2][1][:, cols].bitcast(E4M3), lhsT_scale=keys[b // 2][2][:, cols],
                                 rhs=qd[h][1][:].bitcast(E4M3), rhs_scale=qd[h][2][:], start=True, stop=True)
-            arg = held([P, R], F32, "arg%d" % n)
-            nc.vector.tensor_tensor(out=arg[:], in0=us_half[:], in1=score[:], op=ALU.mult)
-            nc.scalar.activation(out=arg[:], in_=arg[:], func=ACT.Tanh, scale=ts_col[:, ib:ib + 1])
-            squares.append(arg)
+            squares.append(held([P, R], F32, "square%d" % n))
+            nc.vector.tensor_tensor(out=squares[n][:], in0=us_half[:], in1=score[:], op=ALU.mult)
+            nc.scalar.activation(out=squares[n][:], in_=squares[n][:], func=ACT.Tanh, scale=ts_col[:, b:b + 1])
             if n > 0:
                 square(n - 1)
-        square(len(order) - 1)
+        last = len(TILES) - 1
+        square(last)
 
-        g_halves = [(held([P, 2 * HALF * PACK], BF16, "g%d_grouped" % half, tag=("us_half", None)[half]),
-                     held([P, 2 * HALF], U32, "g%d_codes" % half, tag=("arg5", None)[half]),
-                     held([P, 2 * HALF], U8, "g%d_scales" % half)) for half in range(2)]
-        g = {(h, half): (g_halves[half][0][:, PACK * HALF * h:PACK * HALF * (h + 1)], g_halves[half][1][:, HALF * h:HALF * (h + 1)],
-                         g_halves[half][2][:, HALF * h:HALF * (h + 1)]) for h in range(2) for half in range(2)}
+        last_on_gpsimd = VECTOR_SLOPES + GPSIMD_SLOPES - 1
+        g_halves = [mx_tiles(2 * HALF, "g0", grouped_tag="us_half", codes_tag="square%d" % last_on_gpsimd),
+                    mx_tiles(2 * HALF, "g1")]
+        g = {(h, half): (g_halves[half][0][:, PACK * HALF * h:PACK * HALF * (h + 1)],
+                         g_halves[half][1][:, HALF * h:HALF * (h + 1)], g_halves[half][2][:, HALF * h:HALF * (h + 1)])
+             for h in range(2) for half in range(2)}
+        slopes_g = held([P, GPSIMD_SLOPES, R], F32, "slopes_g", tag="dp_raw1")
+        slopes_v = held([P, VECTOR_SLOPES, R], F32, "slopes_v")
+        slopes_s = held([P, SCALAR_SLOPES, R], F32, "slopes_s")
         turned = {}
-        slopes = {"G": held([P, sum(e == "G" for e in SLOPE_ENGINES), R], F32, "slopes_g", tag="dp_raw1"),
-                  "V": held([P, sum(e == "V" for e in SLOPE_ENGINES), R], F32, "slopes_v"),
-                  "S": held([P, sum(e == "S" for e in SLOPE_ENGINES), R], F32, "slopes_s")}
 
-        def turn(n):
-            ib = order[n][1]
-            slope = slopes[SLOPE_ENGINES[n]][:, sum(e == SLOPE_ENGINES[n] for e in SLOPE_ENGINES[:n]), :]
-            if SLOPE_ENGINES[n] == "T":
-                nc.vector.scalar_tensor_tensor(out=slope, in0=squares[n][:], scalar=ts_neg[:, ib:ib + 1], in1=squares[n][:],
-                                               op0=ALU.mult, op1=ALU.mult)
-            elif SLOPE_ENGINES[n] == "S":
-                nc.scalar.activation(out=slope, in_=squares[n][:], func=ACT.Identity,
-                                     scale=ts_neg[:, ib:ib + 1], bias=ts_pos[:, ib:ib + 1])
+        def slope_and_turn(n):
+            b = TILES[n][1]
+            neg, pos = ts_neg[:, b:b + 1], ts_pos[:, b:b + 1]
+            if n > last_on_gpsimd:
+                slope = slopes_s[:, n - last_on_gpsimd - 1, :]
+                nc.scalar.activation(out=slope, in_=squares[n][:], func=ACT.Identity, scale=neg, bias=pos)
             else:
-                engine = nc.gpsimd if SLOPE_ENGINES[n] == "G" else nc.vector
-                engine.tensor_scalar(out=slope, in0=squares[n][:], scalar1=ts_neg[:, ib:ib + 1], scalar2=ts_pos[:, ib:ib + 1],
-                                     op0=ALU.mult, op1=ALU.add)
+                engine, slope = (nc.vector, slopes_v[:, n, :]) if n < VECTOR_SLOPES else (nc.gpsimd, slopes_g[:, n - VECTOR_SLOPES, :])
+                engine.tensor_scalar(out=slope, in0=squares[n][:], scalar1=neg, scalar2=pos, op0=ALU.mult, op1=ALU.add)
             turned[n] = bank("c%d" % (n % 4))
             for t in range(PACK):
-                out = turned[n][:, t * P:(t + 1) * P]
-                if SLOPE_ENGINES[n] == "T":
-                    nc.tensor.matmul(out, lhsT=ts_pos[:, ib:ib + 1].to_broadcast([P, P]), rhs=ident[:], start=True, stop=False, is_transpose=True)
-                    nc.tensor.matmul(out, lhsT=slope[:, t * P:(t + 1) * P], rhs=ident[:], start=False, stop=True, is_transpose=True)
-                else:
-                    nc.tensor.transpose(out, slope[:, t * P:(t + 1) * P], ident[:])
+                nc.tensor.transpose(turned[n][:, t * P:(t + 1) * P], slope[:, t * P:(t + 1) * P], ident[:])
 
         def gradient(n):
-            h, ib = order[n]
-            b = ib % 2
+            h, b = TILES[n]
             nc.vector.tensor_tensor(
-                out=g[h, ib // 2][0][:, PACK * P * b:PACK * P * (b + 1)].rearrange("p (c i t) -> p c t i", i=4, t=PACK),
-                in0=scaled[h][:, :, ib * P:(ib + 1) * P].rearrange("p t (c i) -> p c t i", i=4),
-                in1=turned[n][:].rearrange("p (t c i) -> p c t i", i=4, t=PACK), op=ALU.mult)
+                out=g[h, b // 2][0][:, PACK * P * (b % 2):PACK * P * (b % 2 + 1)].rearrange("p (c i t) -> p c t i", i=RUN, t=PACK),
+                in0=scaled[h][:, :, b * P:(b + 1) * P].rearrange("p t (c i) -> p c t i", i=RUN),
+                in1=turned[n][:].rearrange("p (t c i) -> p c t i", i=RUN, t=PACK), op=ALU.mult)
 
-        def products(j, half, out, heads=(0, 1)):
-            blk = slice(j * P, (j + 1) * P)
-            for h in heads:
-                nc.tensor.matmul_mx(out=out, lhsT=qr[h][1][:, blk].bitcast(E4M3), lhsT_scale=qr[h][2][:, blk],
-                                    rhs=g[h, half][1].bitcast(E5M2), rhs_scale=g[h, half][2],
-                                    start=h == 0, stop=h == 1)
+        def product(j, half, h):
+            cols = slice(j * P, (j + 1) * P)
+            nc.tensor.matmul_mx(out=sums[j][:, half * HALF:(half + 1) * HALF],
+                                lhsT=qr[h][1][:, cols].bitcast(E4M3), lhsT_scale=qr[h][2][:, cols],
+                                rhs=g[h, half][1].bitcast(E5M2), rhs_scale=g[h, half][2], start=h == 0, stop=h == 1)
 
-        sums = [bank("a%d" % j) for j in range(2)]
-        turn(0)
-        for n, (h, ib) in enumerate(order):
-            if n + 1 < len(order):
-                turn(n + 1)
+        sums = [bank("a0"), bank("a1")]
+        slope_and_turn(0)
+        for n in range(len(TILES)):
+            if n < last:
+                slope_and_turn(n + 1)
             else:
                 quantize(*g[1, 1], E5M2, 0, P)
             gradient(n)
@@ -258,10 +237,10 @@ def tile_attend_ggqa_sig_k_pl_kernel(tc, q1, q2, kT, dp1, dp2, us, ts, w1, w2, o
                 quantize(*g_halves[0], E5M2, 0, 2 * HALF)
             if n == 5:
                 quantize(*g[0, 1], E5M2, 0, HALF)
-            if n == 6:
-                for head in range(2):
+            if n == last - 1:
+                for h in range(2):
                     for j in range(2):
-                        products(j, 0, sums[j][:, 0:HALF], heads=(head,))
+                        product(j, 0, h)
         first1 = held([P, HALF], F32, "first1", tag="k_raw3")
         nc.vector.tensor_copy(out=first1[:], in_=sums[1][:, 0:HALF])
         quantize(*g[1, 1], E5M2, P, HALF)
@@ -269,52 +248,51 @@ def tile_attend_ggqa_sig_k_pl_kernel(tc, q1, q2, kT, dp1, dp2, us, ts, w1, w2, o
         windows.append(held([P, TOKENS], F32, "window3", tag="g1_grouped"))
         nc.gpsimd.memset(windows[3][:], 0.0)
 
-        out_planes = out_0.rearrange("(p j) c -> p j c", j=PACK)
+        out_planes = out_0.rearrange("(p t) c -> p t c", t=PACK)
 
-        def scatter(on_scalar, j, values, lo, hi):
-            target = windows[j][:].indirect(listed(lo, hi))
-            if on_scalar:
-                nc.scalar.activation(out=target, in_=values, func=ACT.Copy)
-            else:
-                nc.vector.tensor_copy(out=target, in_=values)
+        def scatter_on_scalar(j, values, half):
+            nc.scalar.activation(out=windows[j][:].indirect(listed(half * HALF, (half + 1) * HALF)), in_=values, func=ACT.Copy)
 
-        def store_plane(j):
-            queue = nc.scalar if j == 0 else nc.sync
+        def scatter_on_vector(j, values, lo, hi):
+            nc.vector.tensor_copy(out=windows[j][:].indirect(listed(lo, hi)), in_=values)
+
+        def store_plane(queue, j):
             queue.dma_start(out=out_planes[:, j, :], in_=windows[j][:])
 
-        first0 = held([P, HALF], F32, "first0", tag="arg7")
+        first0 = held([P, HALF], F32, "first0", tag="square%d" % last)
         nc.scalar.copy(out=first0[:], in_=sums[0][:, 0:HALF])
-        scatter(True, 0, first0[:], 0, HALF)
+        scatter_on_scalar(0, first0[:], 0)
         for j in range(2):
-            products(j, 1, sums[j][:, HALF:SLOTS])
+            for h in range(2):
+                product(j, 1, h)
         sums += [bank("c2"), bank("c1")]
         for half in range(2):
             for j in (2, 3):
-                products(j, half, sums[j][:, half * HALF:(half + 1) * HALF])
-        scatter(False, 1, first1[:], 0, HALF)
+                for h in range(2):
+                    product(j, half, h)
+        scatter_on_vector(1, first1[:], 0, HALF)
         second0 = held([P, HALF], F32, "second0", tag="q_raw0")
         nc.scalar.copy(out=second0[:], in_=sums[0][:, HALF:SLOTS])
-        scatter(True, 0, second0[:], HALF, SLOTS)
-        store_plane(0)
+        scatter_on_scalar(0, second0[:], 1)
+        store_plane(nc.scalar, 0)
         second1 = held([P, HALF], F32, "second1")
         nc.vector.tensor_copy(out=second1[:], in_=sums[1][:, HALF:SLOTS])
-        scatter(False, 1, second1[:], HALF, SLOTS)
-        store_plane(1)
-        whole = held([P, 2, SLOTS], F32, "whole", tag="q_raw1")
+        scatter_on_vector(1, second1[:], HALF, SLOTS)
+        store_plane(nc.sync, 1)
+        late = held([P, 2, SLOTS], F32, "late", tag="q_raw1")
         for j in (3, 2):
-            nc.scalar.copy(out=whole[:, j - 2, :], in_=sums[j][:])
+            nc.scalar.copy(out=late[:, j - 2, :], in_=sums[j][:])
         for half in range(2):
-            scatter(True, 2, whole[:, 0, half * HALF:(half + 1) * HALF], half * HALF, (half + 1) * HALF)
-        scatter(False, 3, whole[:, 1, :], 0, SLOTS)
-        store_plane(3)
-        store_plane(2)
+            scatter_on_scalar(2, late[:, 0, half * HALF:(half + 1) * HALF], half)
+        scatter_on_vector(3, late[:, 1, :], 0, SLOTS)
+        store_plane(nc.sync, 3)
+        store_plane(nc.sync, 2)
 
-        rounded_first = held([P, PACK, PIECE], BF16, "rounded_first", tag="arg7")
+        rounded_first = held([P, PACK, PIECE], BF16, "rounded_first", tag="square%d" % last)
         rounded_rest = held([P, PACK, TOKENS - PIECE], BF16, "rounded_rest", tag="q_raw0")
         y_codes = held([P, TOKENS], U32, "y_codes")
-        y_scales = held([P, 2 * PIECE], U8, "y_scales")
+        y_scales = held([P, TOKENS // 2], U8, "y_scales")
         words_out = out_1.rearrange("a p c t -> p (a c t)").bitcast(I32)
-        spans = [slice(c * PIECE, (c + 1) * PIECE) for c in range(PIECES)]
 
         def round_on_gpsimd(out, in_):
             nc.gpsimd.tensor_scalar(out=out, in0=in_, scalar1=1.0, scalar2=-0.0, op0=ALU.mult, op1=ALU.add)
@@ -325,17 +303,19 @@ def tile_attend_ggqa_sig_k_pl_kernel(tc, q1, q2, kT, dp1, dp2, us, ts, w1, w2, o
         def round_rest(mover, j):
             mover(out=rounded_rest[:, j, :], in_=windows[j][:, PIECE:TOKENS])
 
-        grouped_low = held([P, 2 * PIECE * PACK], BF16, "y_grouped_low", tag="dp_raw0")
-        grouped = [grouped_low[:, c * PIECE * PACK:(c + 1) * PIECE * PACK] for c in range(2)]
-        grouped += [held([P, PIECE * PACK], BF16, "y_grouped%d" % c, tag=tag)[:] for c, tag in ((2, "k_raw2"), (3, "arg7"))]
+        y_low = held([P, 2 * PIECE * PACK], BF16, "y_low", tag="dp_raw0")
+        y_grouped = [y_low[:, c * PIECE * PACK:(c + 1) * PIECE * PACK] for c in range(2)]
+        y_grouped += [held([P, PIECE * PACK], BF16, "y_grouped%d" % c, tag=tag)[:] for c, tag in ((2, "k_raw2"), (3, "square%d" % last))]
 
-        def interleave(mover, c, lo=0, hi=PIECE):
-            planes = rounded_first[:] if c == 0 else rounded_rest[:, :, spans[c - 1]]
-            mover(out=grouped[c][:, PACK * lo:PACK * hi].rearrange("p (c i t) -> p c t i", i=4, t=PACK),
-                  in_=planes[:, :, lo:hi].rearrange("p t (c i) -> p c t i", i=4))
+        def interleave_tokens(mover, c, lo, hi):
+            planes = rounded_first[:] if c == 0 else rounded_rest[:, :, (c - 1) * PIECE:c * PIECE]
+            interleave(mover, y_grouped[c][:, PACK * lo:PACK * hi], planes[:, :, lo:hi])
 
-        def quantize_tokens(span, scales, in_):
-            nc.vector.quantize_mx(out=y_codes[:, span].bitcast(E4M3), scales=scales, in_=in_)
+        def quantize_and_store(c, lo, hi):
+            span = slice(c * PIECE + lo, c * PIECE + hi)
+            nc.vector.quantize_mx(out=y_codes[:, span].bitcast(E4M3),
+                                  scales=y_scales[4 * (c // 2):P, c % 2 * PIECE + lo:c % 2 * PIECE + hi],
+                                  in_=y_grouped[c][:, PACK * lo:PACK * hi])
             nc.sync.dma_start(out=words_out[:, span], in_=y_codes[:, span].bitcast(I32))
 
         round_rest(round_on_gpsimd, 0)
@@ -344,18 +324,18 @@ def tile_attend_ggqa_sig_k_pl_kernel(tc, q1, q2, kT, dp1, dp2, us, ts, w1, w2, o
         for j in (1, 2):
             round_first(nc.scalar.copy, j)
         round_first(nc.vector.tensor_copy, 3)
-        interleave(nc.scalar.copy, 0)
+        interleave_tokens(nc.scalar.copy, 0, 0, PIECE)
         for j in (3, 2):
             round_rest(nc.vector.tensor_copy, j)
-        interleave(nc.vector.tensor_copy, 1)
-        for lo in range(0, PIECE, PIECE // 2):
-            interleave(nc.scalar.copy, 3, lo, lo + PIECE // 2)
-        interleave(nc.vector.tensor_copy, 2)
-        quantize_tokens(slice(0, 2 * PIECE), y_scales[:], grouped_low[:])
-        quantize_tokens(spans[2], y_scales[4:P, spans[0]], grouped[2])
-        for lo in range(0, PIECE, PIECE // 2):
-            hi = lo + PIECE // 2
-            quantize_tokens(slice(3 * PIECE + lo, 3 * PIECE + hi), y_scales[4:P, PIECE + lo:PIECE + hi], grouped[3][:, PACK * lo:PACK * hi])
+        halves = [(0, PIECE // 2), (PIECE // 2, PIECE)]
+        interleave_tokens(nc.vector.tensor_copy, 1, 0, PIECE)
+        for lo, hi in halves:
+            interleave_tokens(nc.scalar.copy, 3, lo, hi)
+        interleave_tokens(nc.vector.tensor_copy, 2, 0, PIECE)
+        for c in range(3):
+            quantize_and_store(c, 0, PIECE)
+        for lo, hi in halves:
+            quantize_and_store(3, lo, hi)
         scales_out = out_2.rearrange("a f c -> (a f) c").bitcast(I32).rearrange("f (a c) -> a f c", a=2)
         for quad in range(4):
             queue = nc.sync if quad % 2 == 0 else nc.scalar

@@ -25,9 +25,7 @@ BANK = 512
 RUN = 4
 PIECE = 512
 TILES = [(h, 2 * half + b) for half in range(2) for h in range(2) for b in range(2)]
-VECTOR_SLOPES = 2
-SCALAR_SLOPES = 2
-GPSIMD_SLOPES = len(TILES) - VECTOR_SLOPES - SCALAR_SLOPES
+ORDER = (0, 2, 1, 3)
 FLOPS = 4 * 2 * D * R * SLOTS
 
 
@@ -50,7 +48,7 @@ def tile_attend_ggqa_sig_k_pl_kernel(tc, q1, q2, kT, dp1, dp2, us, ts, w1, w2, o
 
         def load_column(name, vec):
             tile = held([P, PACK], F32, name)
-            nc.sync.dma_start(out=tile[:], in_=vec.rearrange("(p t) o -> p (t o)", t=PACK))
+            nc.scalar.dma_start(out=tile[:], in_=vec.rearrange("(p t) o -> p (t o)", t=PACK))
             return tile
 
         def load_rows(name, mat):
@@ -61,88 +59,99 @@ def tile_attend_ggqa_sig_k_pl_kernel(tc, q1, q2, kT, dp1, dp2, us, ts, w1, w2, o
         offsets = keep.tile([P, SLOTS // 16], U16, name="offsets")
         ts_row = held([P, TOKENS], F32, "ts_row")
         clear_on_vector(ts_row)
-        q_raw = [load_rows("q_raw0", q1), load_rows("q_raw1", q2)]
+        q_raw = [load_rows("q_raw0", q1)]
         nc.sync.dma_start(offsets[:], offs)
-        us_col = load_column("us_col", us)
         nc.sync.dma_start(out=ts_row[0:1, :], in_=ts[0:1, :])
+        q_raw.append(load_rows("q_raw1", q2))
+        us_col = load_column("us_col", us)
+        w_col = [load_column("w1_col", w1), load_column("w2_col", w2)]
         k_planes = kT.rearrange("(p t) c -> p t c", t=PACK)
         k_raw = [held([P, TOKENS], F32, "k_raw%d" % t) for t in range(PACK)]
         for t in range(PACK):
             nc.sync.dma_start(out=k_raw[t][:], in_=k_planes[:, t, :])
-        w_col = [load_column("w1_col", w1), load_column("w2_col", w2)]
         dp_raw = [load_rows("dp_raw0", dp1), load_rows("dp_raw1", dp2)]
 
         ident = held([P, P], F32, "ident")
         make_identity(nc, ident[:])
-        windows = [held([P, TOKENS], F32, "window%d" % t) for t in range(PACK - 1)]
-        clear_on_vector(windows[0])
-        for t in (1, 2):
+        windows = {t: held([P, TOKENS], F32, "window%d" % t) for t in (0, 2)}
+        for t in (0, 2):
             nc.gpsimd.memset(windows[t][:], 0.0)
 
         def listed(lo, hi):
             return offsets[:, lo // 16:hi // 16]
 
-        def mx_tiles(width, name, grouped_tag=None, codes_tag=None):
+        def mx_tiles(width, name, grouped_tag=None):
             return (held([P, width * PACK], BF16, name + "_grouped", tag=grouped_tag),
-                    held([P, width], U32, name + "_codes", tag=codes_tag), held([P, width], U8, name + "_scales"))
+                    held([P, width], U32, name + "_codes"), held([P, width], U8, name + "_scales"))
 
         def quantize(grouped, codes, scales, fmt, lo, hi):
             nc.vector.quantize_mx(out=codes[:, lo:hi].bitcast(fmt), scales=scales[:, lo:hi],
                                   in_=grouped[:, PACK * lo:PACK * hi])
 
+        def in_runs(planes):
+            return planes.rearrange("p t (c i) -> p c t i", i=RUN)
+
+        def in_places(grouped):
+            return grouped.rearrange("p (c i t) -> p c t i", i=RUN, t=PACK)
+
         def interleave(mover, grouped, planes):
-            mover(out=grouped.rearrange("p (c i t) -> p c t i", i=RUN, t=PACK),
-                  in_=planes.rearrange("p t (c i) -> p c t i", i=RUN))
+            mover(out=in_places(grouped), in_=in_runs(planes))
+
+        w_quarter = [held([P, PACK], F32, "w_quarter%d" % h) for h in range(2)]
+        for h in range(2):
+            nc.scalar.activation(out=w_quarter[h][:], in_=w_col[h][:], func=ACT.Copy, scale=-0.25)
+
+        ts_listed = held([P, SLOTS], F32, "ts_listed")
+        nc.scalar.activation(out=ts_listed[:], in_=ts_row[:].indirect(offsets[:]), func=ACT.Copy)
+        ps = bank("a0")
+        for b in range(SLOTS // P):
+            nc.tensor.transpose(ps[:, b * P:(b + 1) * P], ts_listed[:, b * P:(b + 1) * P], ident[:])
+        ts_col = held([P, SLOTS // P], F32, "ts_col")
+        nc.scalar.copy(out=ts_col[:], in_=ps[:, 0:SLOTS:P])
+        ts_spread = bank("a1")
+        for b in range(SLOTS // P):
+            nc.tensor.transpose(ts_spread[:, b * P:(b + 1) * P], ts_col[:, b:b + 1].to_broadcast([P, P]), ident[:])
+        ts_rows = held([P, SLOTS], F32, "ts_rows")
+        nc.scalar.copy(out=ts_rows[:], in_=ts_spread[:])
 
         qd = [mx_tiles(R, "qd%d" % h) for h in range(2)]
         qr = [mx_tiles(D, "qr%d" % h) for h in range(2)]
-        q_rounded = [held([P, PACK * R], BF16, "q_rounded%d" % h) for h in range(2)]
 
         def group_along_d(h):
             nc.vector.tensor_copy(out=qd[h][0][:].rearrange("p (i m t) -> p m t i", i=PACK, t=PACK),
                                   in_=q_raw[h][:].rearrange("p t (m i) -> p m t i", i=PACK))
 
         def group_along_r(h):
-            words = q_rounded[h][:].bitcast(F32)
-            turned_words = qr[h][0][:].bitcast(F32)
-            row = R // 2
-            for pair in range(2):
-                ps = bank("a%d" % (2 * h + pair))
-                for jj in range(2):
-                    j = 2 * pair + jj
-                    for u in range(2):
-                        nc.tensor.transpose(ps[:, (2 * jj + u) * P:(2 * jj + u + 1) * P],
-                                            words[:, row * j + u:row * (j + 1):2], ident[:])
+            words = qd[h][0][:].bitcast(F32)
+            for u in range(2):
+                ps = bank("c%d" % (2 * h + u))
+                for i in range(PACK):
+                    nc.tensor.transpose(ps[:, i * P:(i + 1) * P], words[:, 2 * P * i + u:2 * P * (i + 1):2], ident[:])
                 nc.scalar.copy(
-                    out=turned_words[:, BANK * pair:BANK * (pair + 1)].rearrange("p (j m u) -> p j m u", j=2, u=2),
-                    in_=ps[:].rearrange("p (j u m) -> p j m u", j=2, u=2))
+                    out=qr[h][0][:, 2 * BANK * u:2 * BANK * (u + 1)].rearrange("m (e p i) -> m e p i", e=2, i=PACK),
+                    in_=ps[:].bitcast(BF16).rearrange("m (i p e) -> m e p i", i=PACK, e=2))
 
-        ps = bank("c0")
-        for t in range(PACK):
-            nc.tensor.transpose(ps[:, t * P:(t + 1) * P], us_col[:, t:t + 1].to_broadcast([P, P]), ident[:])
-        us_half = held([P, R], F32, "us_half")
-        nc.scalar.activation(out=us_half[:], in_=ps[:], func=ACT.Copy, scale=0.5)
-
-        for h in range(2):
-            nc.scalar.copy(out=q_rounded[h][:], in_=q_raw[h][:].rearrange("p t r -> p (t r)"))
         for h in range(2):
             group_along_d(h)
             group_along_r(h)
+        for h in range(2):
             quantize(*qd[h], E4M3, 0, R)
+
+        scale = [held([P, P, PACK], F32, "scale%d" % b) for b in range(SLOTS // P)]
+        for b in range(SLOTS // P):
+            nc.vector.tensor_tensor(out=scale[b][:], in0=us_col[:].unsqueeze(1).to_broadcast([P, P, PACK]),
+                                    in1=ts_spread[:, b * P:(b + 1) * P].unsqueeze(2).to_broadcast([P, P, PACK]), op=ALU.mult)
         for h in range(2):
             quantize(*qr[h], E4M3, 0, D)
 
-        ts_listed = held([P, SLOTS], F32, "ts_listed")
-        nc.scalar.activation(out=ts_listed[:], in_=ts_row[:].indirect(offsets[:]), func=ACT.Copy)
-        ps = bank("c1")
-        for b in range(SLOTS // P):
-            nc.tensor.transpose(ps[:, b * P:(b + 1) * P], ts_listed[:, b * P:(b + 1) * P], ident[:])
-        ts_col = held([P, SLOTS // P], F32, "ts_col")
-        nc.scalar.copy(out=ts_col[:], in_=ps[:, 0:SLOTS:P])
-        ts_neg = held([P, SLOTS // P], F32, "ts_neg")
-        nc.scalar.activation(out=ts_neg[:], in_=ps[:, 0:SLOTS:P], func=ACT.Copy, scale=-0.25)
-        ts_pos = held([P, SLOTS // P], F32, "ts_pos")
-        nc.scalar.activation(out=ts_pos[:], in_=ps[:, 0:SLOTS:P], func=ACT.Copy, scale=0.25)
+        gate = [held([P, PACK], F32, "gate%d" % h) for h in range(2)]
+        for h in range(2):
+            nc.gpsimd.tensor_tensor(out=gate[h][:], in0=w_quarter[h][:], in1=us_col[:], op=ALU.mult)
+        factor = [held([P, PACK, SLOTS], F32, "factor%d" % h) for h in range(2)]
+        for h in range(2):
+            for t in range(PACK):
+                nc.gpsimd.tensor_scalar(out=factor[h][:, t, :], in0=ts_rows[:],
+                                        scalar1=gate[h][:, t:t + 1], scalar2=0.0, op0=ALU.mult, op1=ALU.add)
 
         keys = [mx_tiles(HALF, "k0", grouped_tag="qr1_grouped"), mx_tiles(HALF, "k1")]
         k_places = keys[0][0][:].rearrange("p (c t) -> p c t", t=PACK)
@@ -152,24 +161,27 @@ def tile_attend_ggqa_sig_k_pl_kernel(tc, q1, q2, kT, dp1, dp2, us, ts, w1, w2, o
         nc.vector.tensor_copy(out=k_places[:, :, 0:2], in_=k_early[:].rearrange("p t c -> p c t"))
         for t in (2, 3):
             nc.vector.tensor_copy(out=k_places[:, :, t], in_=k_raw[t][:].indirect(listed(0, HALF)))
-        k_late = held([P, PACK, HALF], BF16, "k_late", tag="q_rounded1")
+        k_late = held([P, PACK, HALF], BF16, "k_late")
         for t in range(PACK):
             nc.scalar.activation(out=k_late[:, t, :], in_=k_raw[t][:].indirect(listed(HALF, SLOTS)), func=ACT.Copy)
         interleave(nc.scalar.copy, keys[1][0][:], k_late[:])
 
-        gate = [held([P, PACK], F32, "gate%d" % h) for h in range(2)]
-        for h in range(2):
-            nc.gpsimd.tensor_tensor(out=gate[h][:], in0=w_col[h][:], in1=us_col[:], op=ALU.mult)
-        scaled = [held([P, PACK, SLOTS], F32, "scaled%d" % h, tag="k_raw%d" % (2 + h)) for h in range(2)]
-        for h in range(2):
-            for t in range(PACK):
-                nc.gpsimd.tensor_scalar(out=scaled[h][:, t, :], in0=dp_raw[h][:, t, :],
-                                        scalar1=gate[h][:, t:t + 1], scalar2=0.0, op0=ALU.mult, op1=ALU.add)
+        def weigh(engine, out, h, half):
+            cols = slice(half * HALF, (half + 1) * HALF)
+            engine.tensor_tensor(out=in_places(out), in0=in_runs(dp_raw[h][:, :, cols]), in1=in_runs(factor[h][:, :, cols]), op=ALU.mult)
 
-        squares = []
+        weight = {(0, half): held([P, PACK * HALF], F32, "weight0%d" % half) for half in range(2)}
+        for half in range(2):
+            weigh(nc.gpsimd, weight[0, half][:], 0, half)
 
-        def square(n):
-            nc.scalar.activation(out=squares[n][:], in_=squares[n][:], func=ACT.Square)
+        squares = {(h, half): held([P, PACK * HALF], F32, "squares%d%d" % (h, half)) for h in range(2) for half in range(2)}
+
+        def part(tiles, n):
+            h, b = TILES[n]
+            return tiles[h, b // 2][:, b % 2 * BANK:(b % 2 + 1) * BANK]
+
+        def square(h, half):
+            nc.scalar.activation(out=squares[h, half][:], in_=squares[h, half][:], func=ACT.Square)
 
         for n, (h, b) in enumerate(TILES):
             if n == 0:
@@ -178,118 +190,99 @@ def tile_attend_ggqa_sig_k_pl_kernel(tc, q1, q2, kT, dp1, dp2, us, ts, w1, w2, o
                 quantize(*keys[1], E4M3, 0, HALF)
             cols = slice(b % 2 * P, (b % 2 + 1) * P)
             score = bank("a%d" % (n % 4))
-            nc.tensor.matmul_mx(out=score[:], lhsT=keys[b // 2][1][:, cols].bitcast(E4M3), lhsT_scale=keys[b // 2][2][:, cols],
-                                rhs=qd[h][1][:].bitcast(E4M3), rhs_scale=qd[h][2][:], start=True, stop=True)
-            squares.append(held([P, R], F32, "square%d" % n))
-            nc.vector.tensor_tensor(out=squares[n][:], in0=us_half[:], in1=score[:], op=ALU.mult)
-            nc.scalar.activation(out=squares[n][:], in_=squares[n][:], func=ACT.Tanh, scale=ts_col[:, b:b + 1])
-            if n > 0:
-                square(n - 1)
-        last = len(TILES) - 1
-        square(last)
+            for i in range(PACK):
+                rows = slice(i * P, (i + 1) * P)
+                nc.tensor.matmul_mx(out=score[:, rows], lhsT=qd[h][1][:, rows].bitcast(E4M3), lhsT_scale=qd[h][2][:, rows],
+                                    rhs=keys[b // 2][1][:, cols].bitcast(E4M3), rhs_scale=keys[b // 2][2][:, cols],
+                                    start=True, stop=True)
+            nc.vector.tensor_tensor(out=part(squares, n).rearrange("p (c t) -> p c t", t=PACK), in0=scale[b][:],
+                                    in1=score[:].rearrange("p (t c) -> p c t", t=PACK), op=ALU.mult)
+            nc.scalar.activation(out=part(squares, n), in_=part(squares, n), func=ACT.Tanh, scale=0.5)
+            if n % 2 == 0 and n > 0:
+                square(TILES[n - 1][0], TILES[n - 1][1] // 2)
+        square(1, 1)
 
-        last_on_gpsimd = VECTOR_SLOPES + GPSIMD_SLOPES - 1
-        g_halves = [mx_tiles(2 * HALF, "g0", grouped_tag="us_half", codes_tag="square%d" % last_on_gpsimd),
-                    mx_tiles(2 * HALF, "g1")]
-        g = {(h, half): (g_halves[half][0][:, PACK * HALF * h:PACK * HALF * (h + 1)],
-                         g_halves[half][1][:, HALF * h:HALF * (h + 1)], g_halves[half][2][:, HALF * h:HALF * (h + 1)])
-             for h in range(2) for half in range(2)}
-        slopes_g = held([P, GPSIMD_SLOPES, R], F32, "slopes_g", tag="dp_raw1")
-        slopes_v = held([P, VECTOR_SLOPES, R], F32, "slopes_v")
-        slopes_s = held([P, SCALAR_SLOPES, R], F32, "slopes_s")
-        turned = {}
+        windows[1] = held([P, TOKENS], F32, "window1", tag="factor0")
+        windows[3] = held([P, TOKENS], F32, "window3", tag="dp_raw0")
+        for t in (1, 3):
+            nc.gpsimd.memset(windows[t][:], 0.0)
 
-        def slope_and_turn(n):
-            b = TILES[n][1]
-            neg, pos = ts_neg[:, b:b + 1], ts_pos[:, b:b + 1]
-            if n > last_on_gpsimd:
-                slope = slopes_s[:, n - last_on_gpsimd - 1, :]
-                nc.scalar.activation(out=slope, in_=squares[n][:], func=ACT.Identity, scale=neg, bias=pos)
-            else:
-                engine, slope = (nc.vector, slopes_v[:, n, :]) if n < VECTOR_SLOPES else (nc.gpsimd, slopes_g[:, n - VECTOR_SLOPES, :])
-                engine.tensor_scalar(out=slope, in0=squares[n][:], scalar1=neg, scalar2=pos, op0=ALU.mult, op1=ALU.add)
-            turned[n] = bank("c%d" % (n % 4))
-            for t in range(PACK):
-                nc.tensor.transpose(turned[n][:, t * P:(t + 1) * P], slope[:, t * P:(t + 1) * P], ident[:])
+        g_halves = [mx_tiles(2 * HALF, "g0", grouped_tag="scale2"), mx_tiles(2 * HALF, "g1")]
+        weight[1, 0] = held([P, PACK * HALF], F32, "weight10", tag="scale3")
 
-        def gradient(n):
-            h, b = TILES[n]
-            nc.vector.tensor_tensor(
-                out=g[h, b // 2][0][:, PACK * P * (b % 2):PACK * P * (b % 2 + 1)].rearrange("p (c i t) -> p c t i", i=RUN, t=PACK),
-                in0=scaled[h][:, :, b * P:(b + 1) * P].rearrange("p t (c i) -> p c t i", i=RUN),
-                in1=turned[n][:].rearrange("p (t c i) -> p c t i", i=RUN, t=PACK), op=ALU.mult)
+        def gradient(h, half, lo, hi):
+            cols = slice(PACK * lo, PACK * hi)
+            nc.vector.scalar_tensor_tensor(out=g_halves[half][0][:, PACK * (HALF * h + lo):PACK * (HALF * h + hi)],
+                                           in0=squares[h, half][:, cols], scalar=1.0, in1=weight[h, half][:, cols],
+                                           op0=ALU.subtract, op1=ALU.mult)
 
-        def product(j, half, h):
+        def product(out, j, half, h):
             cols = slice(j * P, (j + 1) * P)
-            nc.tensor.matmul_mx(out=sums[j][:, half * HALF:(half + 1) * HALF],
-                                lhsT=qr[h][1][:, cols].bitcast(E4M3), lhsT_scale=qr[h][2][:, cols],
-                                rhs=g[h, half][1].bitcast(E5M2), rhs_scale=g[h, half][2], start=h == 0, stop=h == 1)
+            slots = slice(h * HALF, (h + 1) * HALF)
+            nc.tensor.matmul_mx(out=out, lhsT=qr[h][1][:, cols].bitcast(E4M3), lhsT_scale=qr[h][2][:, cols],
+                                rhs=g_halves[half][1][:, slots].bitcast(E5M2), rhs_scale=g_halves[half][2][:, slots],
+                                start=h == 0, stop=h == 1)
 
-        sums = [bank("a0"), bank("a1")]
-        slope_and_turn(0)
-        for n in range(len(TILES)):
-            if n < last:
-                slope_and_turn(n + 1)
-            else:
-                quantize(*g[1, 1], E5M2, 0, P)
-            gradient(n)
-            if n == 4:
-                quantize(*g_halves[0], E5M2, 0, 2 * HALF)
-            if n == 5:
-                quantize(*g[0, 1], E5M2, 0, HALF)
-            if n == last - 1:
-                for h in range(2):
-                    for j in range(2):
-                        product(j, 0, h)
-        first1 = held([P, HALF], F32, "first1", tag="k_raw3")
-        nc.vector.tensor_copy(out=first1[:], in_=sums[1][:, 0:HALF])
-        quantize(*g[1, 1], E5M2, P, HALF)
-
-        windows.append(held([P, TOKENS], F32, "window3", tag="g1_grouped"))
-        nc.gpsimd.memset(windows[3][:], 0.0)
+        weigh(nc.vector, weight[1, 0][:], 1, 0)
+        gradient(0, 0, 0, HALF)
+        gradient(1, 0, 0, HALF)
+        for h in range(2):
+            quantize(*g_halves[0], E5M2, h * HALF, (h + 1) * HALF)
+        weight[1, 1] = held([P, PACK * HALF], F32, "weight11", tag="scale2")
+        weigh(nc.vector, weight[1, 1][:], 1, 1)
+        odd_firsts = bank("c1")
+        firsts = {0: bank("c0")[:, 0:HALF], 2: bank("c2")[:, 0:HALF], 1: odd_firsts[:, 0:HALF], 3: odd_firsts[:, HALF:2 * HALF]}
+        for j in ORDER:
+            for h in range(2):
+                product(firsts[j], j, 0, h)
+        gradient(0, 1, 0, HALF)
+        gradient(1, 1, 0, P)
+        quantize(*g_halves[1], E5M2, 0, HALF)
+        gradient(1, 1, P, HALF)
+        quantize(*g_halves[1], E5M2, HALF, HALF + P)
+        quantize(*g_halves[1], E5M2, HALF + P, 2 * HALF)
+        dk_odd = held([P, 2, HALF], F32, "dk_odd", tag="g1_grouped")
+        nc.vector.tensor_copy(out=dk_odd[:].rearrange("p j c -> p (j c)"), in_=odd_firsts[:])
+        seconds = [bank("a%d" % j) for j in range(PACK)]
+        for h in range(2):
+            for j in ORDER:
+                product(seconds[j][:, 0:HALF], j, 1, h)
 
         out_planes = out_0.rearrange("(p t) c -> p t c", t=PACK)
+        dk = {(1, 0): dk_odd[:, 0, :], (3, 0): dk_odd[:, 1, :]}
 
-        def scatter_on_scalar(j, values, half):
-            nc.scalar.activation(out=windows[j][:].indirect(listed(half * HALF, (half + 1) * HALF)), in_=values, func=ACT.Copy)
+        def empty(mover, j, half, tag=None):
+            dk[j, half] = held([P, HALF], F32, "dk%d%d" % (j, half), tag=tag)[:]
+            mover(out=dk[j, half], in_=seconds[j][:, 0:HALF] if half else firsts[j])
 
-        def scatter_on_vector(j, values, lo, hi):
-            nc.vector.tensor_copy(out=windows[j][:].indirect(listed(lo, hi)), in_=values)
+        def scatter(on_scalar, j, half):
+            window = windows[j][:].indirect(listed(half * HALF, (half + 1) * HALF))
+            if on_scalar:
+                nc.scalar.activation(out=window, in_=dk[j, half], func=ACT.Copy)
+            else:
+                nc.vector.tensor_copy(out=window, in_=dk[j, half])
 
         def store_plane(queue, j):
             queue.dma_start(out=out_planes[:, j, :], in_=windows[j][:])
 
-        first0 = held([P, HALF], F32, "first0", tag="square%d" % last)
-        nc.scalar.copy(out=first0[:], in_=sums[0][:, 0:HALF])
-        scatter_on_scalar(0, first0[:], 0)
-        for j in range(2):
-            for h in range(2):
-                product(j, 1, h)
-        sums += [bank("c2"), bank("c1")]
         for half in range(2):
-            for j in (2, 3):
-                for h in range(2):
-                    product(j, half, h)
-        scatter_on_vector(1, first1[:], 0, HALF)
-        second0 = held([P, HALF], F32, "second0", tag="q_raw0")
-        nc.scalar.copy(out=second0[:], in_=sums[0][:, HALF:SLOTS])
-        scatter_on_scalar(0, second0[:], 1)
-        store_plane(nc.scalar, 0)
-        second1 = held([P, HALF], F32, "second1")
-        nc.vector.tensor_copy(out=second1[:], in_=sums[1][:, HALF:SLOTS])
-        scatter_on_vector(1, second1[:], HALF, SLOTS)
+            for j in (0, 2):
+                empty(nc.scalar.copy, j, half)
+            for j in (0, 2):
+                scatter(True, j, half)
+                if half:
+                    store_plane(nc.sync if j else nc.scalar, j)
+        for j in (1, 3):
+            scatter(False, j, 0)
+        empty(nc.vector.tensor_copy, 1, 1, tag="dk01")
+        scatter(False, 1, 1)
         store_plane(nc.sync, 1)
-        late = held([P, 2, SLOTS], F32, "late", tag="q_raw1")
-        for j in (3, 2):
-            nc.scalar.copy(out=late[:, j - 2, :], in_=sums[j][:])
-        for half in range(2):
-            scatter_on_scalar(2, late[:, 0, half * HALF:(half + 1) * HALF], half)
-        scatter_on_vector(3, late[:, 1, :], 0, SLOTS)
+        empty(nc.scalar.copy, 3, 1)
+        scatter(True, 3, 1)
         store_plane(nc.sync, 3)
-        store_plane(nc.sync, 2)
 
-        rounded_first = held([P, PACK, PIECE], BF16, "rounded_first", tag="square%d" % last)
-        rounded_rest = held([P, PACK, TOKENS - PIECE], BF16, "rounded_rest", tag="q_raw0")
+        rounded_first = held([P, PACK, PIECE], BF16, "rounded_first")
+        rounded_rest = held([P, PACK, TOKENS - PIECE], BF16, "rounded_rest", tag="dp_raw1")
         y_codes = held([P, TOKENS], U32, "y_codes")
         y_scales = held([P, TOKENS // 2], U8, "y_scales")
         words_out = out_1.rearrange("a p c t -> p (a c t)").bitcast(I32)
@@ -303,9 +296,8 @@ def tile_attend_ggqa_sig_k_pl_kernel(tc, q1, q2, kT, dp1, dp2, us, ts, w1, w2, o
         def round_rest(mover, j):
             mover(out=rounded_rest[:, j, :], in_=windows[j][:, PIECE:TOKENS])
 
-        y_low = held([P, 2 * PIECE * PACK], BF16, "y_low", tag="dp_raw0")
-        y_grouped = [y_low[:, c * PIECE * PACK:(c + 1) * PIECE * PACK] for c in range(2)]
-        y_grouped += [held([P, PIECE * PACK], BF16, "y_grouped%d" % c, tag=tag)[:] for c, tag in ((2, "k_raw2"), (3, "square%d" % last))]
+        y_grouped = [held([P, PIECE * PACK], BF16, "y_grouped%d" % c, tag=tag)[:]
+                     for c, tag in enumerate(("k_raw0", "k_raw1", "k_raw2", "rounded_first"))]
 
         def interleave_tokens(mover, c, lo, hi):
             planes = rounded_first[:] if c == 0 else rounded_rest[:, :, (c - 1) * PIECE:c * PIECE]
@@ -320,13 +312,13 @@ def tile_attend_ggqa_sig_k_pl_kernel(tc, q1, q2, kT, dp1, dp2, us, ts, w1, w2, o
 
         round_rest(round_on_gpsimd, 0)
         round_first(round_on_gpsimd, 0)
-        round_rest(round_on_gpsimd, 1)
-        for j in (1, 2):
-            round_first(nc.scalar.copy, j)
-        round_first(nc.vector.tensor_copy, 3)
-        interleave_tokens(nc.scalar.copy, 0, 0, PIECE)
-        for j in (3, 2):
+        for j in (2, 1):
+            round_first(nc.vector.tensor_copy, j)
+        for j in (2, 1):
             round_rest(nc.vector.tensor_copy, j)
+        round_first(nc.scalar.copy, 3)
+        interleave_tokens(nc.scalar.copy, 0, 0, PIECE)
+        round_rest(nc.vector.tensor_copy, 3)
         halves = [(0, PIECE // 2), (PIECE // 2, PIECE)]
         interleave_tokens(nc.vector.tensor_copy, 1, 0, PIECE)
         for lo, hi in halves:

@@ -73,16 +73,17 @@ def tile_attend_ggqa_sig_k_pl_kernel(tc, q1, q2, kT, dp1, dp2, us, ts, w1, w2, o
 
         ident = held([P, P], F32, "ident")
         make_identity(nc, ident[:])
-        windows = {t: held([P, TOKENS], F32, "window%d" % t) for t in (0, 2)}
+        windows = {t: held([P, TOKENS], F32, "window%d" % t) for t in (0, 1, 2)}
+        clear_on_vector(windows[1])
         for t in (0, 2):
             nc.gpsimd.memset(windows[t][:], 0.0)
 
         def listed(lo, hi):
             return offsets[:, lo // 16:hi // 16]
 
-        def mx_tiles(width, name, grouped_tag=None):
+        def mx_tiles(width, name, grouped_tag=None, codes_tag=None):
             return (held([P, width * PACK], BF16, name + "_grouped", tag=grouped_tag),
-                    held([P, width], U32, name + "_codes"), held([P, width], U8, name + "_scales"))
+                    held([P, width], U32, name + "_codes", tag=codes_tag), held([P, width], U8, name + "_scales"))
 
         def quantize(grouped, codes, scales, fmt, lo, hi):
             nc.vector.quantize_mx(out=codes[:, lo:hi].bitcast(fmt), scales=scales[:, lo:hi],
@@ -114,6 +115,12 @@ def tile_attend_ggqa_sig_k_pl_kernel(tc, q1, q2, kT, dp1, dp2, us, ts, w1, w2, o
         ts_rows = held([P, SLOTS], F32, "ts_rows")
         nc.scalar.copy(out=ts_rows[:], in_=ts_spread[:])
 
+        ps = bank("a2")
+        for t in range(PACK):
+            nc.tensor.transpose(ps[:, t * P:(t + 1) * P], us_col[:, t:t + 1].to_broadcast([P, P]), ident[:])
+        us_half = held([P, R], F32, "us_half")
+        nc.scalar.activation(out=us_half[:], in_=ps[:], func=ACT.Copy, scale=0.5)
+
         qd = [mx_tiles(R, "qd%d" % h) for h in range(2)]
         qr = [mx_tiles(D, "qr%d" % h) for h in range(2)]
 
@@ -137,10 +144,6 @@ def tile_attend_ggqa_sig_k_pl_kernel(tc, q1, q2, kT, dp1, dp2, us, ts, w1, w2, o
         for h in range(2):
             quantize(*qd[h], E4M3, 0, R)
 
-        scale = [held([P, P, PACK], F32, "scale%d" % b) for b in range(SLOTS // P)]
-        for b in range(SLOTS // P):
-            nc.vector.tensor_tensor(out=scale[b][:], in0=us_col[:].unsqueeze(1).to_broadcast([P, P, PACK]),
-                                    in1=ts_spread[:, b * P:(b + 1) * P].unsqueeze(2).to_broadcast([P, P, PACK]), op=ALU.mult)
         for h in range(2):
             quantize(*qr[h], E4M3, 0, D)
 
@@ -148,10 +151,10 @@ def tile_attend_ggqa_sig_k_pl_kernel(tc, q1, q2, kT, dp1, dp2, us, ts, w1, w2, o
         for h in range(2):
             nc.gpsimd.tensor_tensor(out=gate[h][:], in0=w_quarter[h][:], in1=us_col[:], op=ALU.mult)
         factor = [held([P, PACK, SLOTS], F32, "factor%d" % h) for h in range(2)]
-        for h in range(2):
+        for h, engine in enumerate((nc.gpsimd, nc.vector)):
             for t in range(PACK):
-                nc.gpsimd.tensor_scalar(out=factor[h][:, t, :], in0=ts_rows[:],
-                                        scalar1=gate[h][:, t:t + 1], scalar2=0.0, op0=ALU.mult, op1=ALU.add)
+                engine.tensor_scalar(out=factor[h][:, t, :], in0=ts_rows[:],
+                                     scalar1=gate[h][:, t:t + 1], scalar2=0.0, op0=ALU.mult, op1=ALU.add)
 
         keys = [mx_tiles(HALF, "k0", grouped_tag="qr1_grouped"), mx_tiles(HALF, "k1")]
         k_places = keys[0][0][:].rearrange("p (c t) -> p c t", t=PACK)
@@ -166,55 +169,53 @@ def tile_attend_ggqa_sig_k_pl_kernel(tc, q1, q2, kT, dp1, dp2, us, ts, w1, w2, o
             nc.scalar.activation(out=k_late[:, t, :], in_=k_raw[t][:].indirect(listed(HALF, SLOTS)), func=ACT.Copy)
         interleave(nc.scalar.copy, keys[1][0][:], k_late[:])
 
-        def weigh(engine, out, h, half):
-            cols = slice(half * HALF, (half + 1) * HALF)
-            engine.tensor_tensor(out=in_places(out), in0=in_runs(dp_raw[h][:, :, cols]), in1=in_runs(factor[h][:, :, cols]), op=ALU.mult)
+        squares = [held([P, R], F32, "square%d" % n) for n in range(len(TILES))]
 
-        weight = {(0, half): held([P, PACK * HALF], F32, "weight0%d" % half) for half in range(2)}
-        for half in range(2):
-            weigh(nc.gpsimd, weight[0, half][:], 0, half)
-
-        squares = {(h, half): held([P, PACK * HALF], F32, "squares%d%d" % (h, half)) for h in range(2) for half in range(2)}
-
-        def part(tiles, n):
-            h, b = TILES[n]
-            return tiles[h, b // 2][:, b % 2 * BANK:(b % 2 + 1) * BANK]
-
-        def square(h, half):
-            nc.scalar.activation(out=squares[h, half][:], in_=squares[h, half][:], func=ACT.Square)
+        def square(n):
+            nc.scalar.activation(out=squares[n][:], in_=squares[n][:], func=ACT.Square)
 
         for n, (h, b) in enumerate(TILES):
-            if n == 0:
-                quantize(*keys[0], E4M3, 0, HALF)
-            if n == 2:
-                quantize(*keys[1], E4M3, 0, HALF)
+            if n < 2:
+                quantize(*keys[n], E4M3, 0, HALF)
             cols = slice(b % 2 * P, (b % 2 + 1) * P)
             score = bank("a%d" % (n % 4))
-            for i in range(PACK):
-                rows = slice(i * P, (i + 1) * P)
-                nc.tensor.matmul_mx(out=score[:, rows], lhsT=qd[h][1][:, rows].bitcast(E4M3), lhsT_scale=qd[h][2][:, rows],
-                                    rhs=keys[b // 2][1][:, cols].bitcast(E4M3), rhs_scale=keys[b // 2][2][:, cols],
-                                    start=True, stop=True)
-            nc.vector.tensor_tensor(out=part(squares, n).rearrange("p (c t) -> p c t", t=PACK), in0=scale[b][:],
-                                    in1=score[:].rearrange("p (t c) -> p c t", t=PACK), op=ALU.mult)
-            nc.scalar.activation(out=part(squares, n), in_=part(squares, n), func=ACT.Tanh, scale=0.5)
-            if n % 2 == 0 and n > 0:
-                square(TILES[n - 1][0], TILES[n - 1][1] // 2)
-        square(1, 1)
+            nc.tensor.matmul_mx(out=score[:], lhsT=keys[b // 2][1][:, cols].bitcast(E4M3), lhsT_scale=keys[b // 2][2][:, cols],
+                                rhs=qd[h][1][:].bitcast(E4M3), rhs_scale=qd[h][2][:], start=True, stop=True)
+            nc.vector.tensor_tensor(out=squares[n][:], in0=us_half[:], in1=score[:], op=ALU.mult)
+            nc.scalar.activation(out=squares[n][:], in_=squares[n][:], func=ACT.Tanh, scale=ts_col[:, b:b + 1])
+            if n > 0:
+                square(n - 1)
+        last = len(TILES) - 1
+        square(last)
 
-        windows[1] = held([P, TOKENS], F32, "window1", tag="factor0")
-        windows[3] = held([P, TOKENS], F32, "window3", tag="dp_raw0")
-        for t in (1, 3):
-            nc.gpsimd.memset(windows[t][:], 0.0)
+        g_halves = [mx_tiles(2 * HALF, "g0", grouped_tag="us_half", codes_tag="factor0")]
+        weight = {}
 
-        g_halves = [mx_tiles(2 * HALF, "g0", grouped_tag="scale2"), mx_tiles(2 * HALF, "g1")]
-        weight[1, 0] = held([P, PACK * HALF], F32, "weight10", tag="scale3")
+        def weigh(engine, n, count, tag=None):
+            h, b = TILES[n]
+            tile = held([P, PACK, count * P], F32, "weight%d" % n, tag=tag)
+            cols = slice(b * P, (b + count) * P)
+            engine.tensor_tensor(out=tile[:], in0=dp_raw[h][:, :, cols], in1=factor[h][:, :, cols], op=ALU.mult)
+            for m in range(count):
+                weight[n + m] = tile[:, :, m * P:(m + 1) * P]
 
-        def gradient(h, half, lo, hi):
-            cols = slice(PACK * lo, PACK * hi)
-            nc.vector.scalar_tensor_tensor(out=g_halves[half][0][:, PACK * (HALF * h + lo):PACK * (HALF * h + hi)],
-                                           in0=squares[h, half][:, cols], scalar=1.0, in1=weight[h, half][:, cols],
-                                           op0=ALU.subtract, op1=ALU.mult)
+        weigh(nc.gpsimd, 0, 2, tag="k1_grouped")
+        weigh(nc.gpsimd, 2, 2)
+        weigh(nc.gpsimd, 4, 2)
+
+        turned = {}
+
+        def turn(n):
+            turned[n] = bank("c%d" % (n % 4))
+            for t in range(PACK):
+                nc.tensor.transpose(turned[n][:, t * P:(t + 1) * P], squares[n][:, t * P:(t + 1) * P], ident[:])
+
+        def gradient(n):
+            half = n // 4
+            nc.vector.scalar_tensor_tensor(
+                out=g_halves[half][0][:, BANK * (n % 4):BANK * (n % 4 + 1)].rearrange("p (c t) -> p c t", t=PACK),
+                in0=turned[n][:].rearrange("p (t c) -> p c t", t=PACK), scalar=1.0,
+                in1=weight[n].rearrange("p t c -> p c t"), op0=ALU.subtract, op1=ALU.mult)
 
         def product(out, j, half, h):
             cols = slice(j * P, (j + 1) * P)
@@ -223,27 +224,32 @@ def tile_attend_ggqa_sig_k_pl_kernel(tc, q1, q2, kT, dp1, dp2, us, ts, w1, w2, o
                                 rhs=g_halves[half][1][:, slots].bitcast(E5M2), rhs_scale=g_halves[half][2][:, slots],
                                 start=h == 0, stop=h == 1)
 
-        weigh(nc.vector, weight[1, 0][:], 1, 0)
-        gradient(0, 0, 0, HALF)
-        gradient(1, 0, 0, HALF)
-        for h in range(2):
-            quantize(*g_halves[0], E5M2, h * HALF, (h + 1) * HALF)
-        weight[1, 1] = held([P, PACK * HALF], F32, "weight11", tag="scale2")
-        weigh(nc.vector, weight[1, 1][:], 1, 1)
-        odd_firsts = bank("c1")
-        firsts = {0: bank("c0")[:, 0:HALF], 2: bank("c2")[:, 0:HALF], 1: odd_firsts[:, 0:HALF], 3: odd_firsts[:, HALF:2 * HALF]}
+        for n in range(4):
+            turn(n)
+        for n in range(4):
+            gradient(n)
+            turn(n + 4)
+        quantize(*g_halves[0], E5M2, 0, 2 * HALF)
+        weigh(nc.gpsimd, 6, 1, tag="us_half")
+        odd_firsts = bank("a2")
+        firsts = {0: bank("a0")[:, 0:HALF], 2: bank("a1")[:, 0:HALF], 1: odd_firsts[:, 0:HALF], 3: odd_firsts[:, HALF:2 * HALF]}
         for j in ORDER:
             for h in range(2):
                 product(firsts[j], j, 0, h)
-        gradient(0, 1, 0, HALF)
-        gradient(1, 1, 0, P)
+        g_halves.append(mx_tiles(2 * HALF, "g1", codes_tag="dp_raw1"))
+        gradient(4)
+        gradient(5)
+        weigh(nc.vector, last, 1, tag="weight4")
+        gradient(6)
         quantize(*g_halves[1], E5M2, 0, HALF)
-        gradient(1, 1, P, HALF)
+        gradient(last)
         quantize(*g_halves[1], E5M2, HALF, HALF + P)
         quantize(*g_halves[1], E5M2, HALF + P, 2 * HALF)
-        dk_odd = held([P, 2, HALF], F32, "dk_odd", tag="g1_grouped")
+        dk_odd = held([P, 2, HALF], F32, "dk_odd", tag="weight4")
         nc.vector.tensor_copy(out=dk_odd[:].rearrange("p j c -> p (j c)"), in_=odd_firsts[:])
-        seconds = [bank("a%d" % j) for j in range(PACK)]
+        windows[3] = held([P, TOKENS], F32, "window3", tag="g1_grouped")
+        nc.gpsimd.memset(windows[3][:], 0.0)
+        seconds = {j: bank(tag) for j, tag in zip(ORDER, ("a3", "c0", "c2", "c3"))}
         for h in range(2):
             for j in ORDER:
                 product(seconds[j][:, 0:HALF], j, 1, h)
@@ -274,15 +280,15 @@ def tile_attend_ggqa_sig_k_pl_kernel(tc, q1, q2, kT, dp1, dp2, us, ts, w1, w2, o
                     store_plane(nc.sync if j else nc.scalar, j)
         for j in (1, 3):
             scatter(False, j, 0)
-        empty(nc.vector.tensor_copy, 1, 1, tag="dk01")
+        empty(nc.vector.tensor_copy, 1, 1, tag="weight4")
         scatter(False, 1, 1)
         store_plane(nc.sync, 1)
         empty(nc.scalar.copy, 3, 1)
         scatter(True, 3, 1)
         store_plane(nc.sync, 3)
 
-        rounded_first = held([P, PACK, PIECE], BF16, "rounded_first")
-        rounded_rest = held([P, PACK, TOKENS - PIECE], BF16, "rounded_rest", tag="dp_raw1")
+        rounded_first = held([P, PACK, PIECE], BF16, "rounded_first", tag="dk31")
+        rounded_rest = held([P, PACK, TOKENS - PIECE], BF16, "rounded_rest", tag="dp_raw0")
         y_codes = held([P, TOKENS], U32, "y_codes")
         y_scales = held([P, TOKENS // 2], U8, "y_scales")
         words_out = out_1.rearrange("a p c t -> p (a c t)").bitcast(I32)
@@ -297,7 +303,7 @@ def tile_attend_ggqa_sig_k_pl_kernel(tc, q1, q2, kT, dp1, dp2, us, ts, w1, w2, o
             mover(out=rounded_rest[:, j, :], in_=windows[j][:, PIECE:TOKENS])
 
         y_grouped = [held([P, PIECE * PACK], BF16, "y_grouped%d" % c, tag=tag)[:]
-                     for c, tag in enumerate(("k_raw0", "k_raw1", "k_raw2", "rounded_first"))]
+                     for c, tag in enumerate(("k_raw0", "k_raw1", "k_raw2", "dk31"))]
 
         def interleave_tokens(mover, c, lo, hi):
             planes = rounded_first[:] if c == 0 else rounded_rest[:, :, (c - 1) * PIECE:c * PIECE]
@@ -310,15 +316,15 @@ def tile_attend_ggqa_sig_k_pl_kernel(tc, q1, q2, kT, dp1, dp2, us, ts, w1, w2, o
                                   in_=y_grouped[c][:, PACK * lo:PACK * hi])
             nc.sync.dma_start(out=words_out[:, span], in_=y_codes[:, span].bitcast(I32))
 
-        round_rest(round_on_gpsimd, 0)
-        round_first(round_on_gpsimd, 0)
-        for j in (2, 1):
+        for j in (0, 2):
+            round_rest(round_on_gpsimd, j)
+        for j in (0, 1):
             round_first(nc.vector.tensor_copy, j)
-        for j in (2, 1):
-            round_rest(nc.vector.tensor_copy, j)
-        round_first(nc.scalar.copy, 3)
+        for j in (2, 3):
+            round_first(nc.scalar.copy, j)
         interleave_tokens(nc.scalar.copy, 0, 0, PIECE)
-        round_rest(nc.vector.tensor_copy, 3)
+        for j in (1, 3):
+            round_rest(nc.vector.tensor_copy, j)
         halves = [(0, PIECE // 2), (PIECE // 2, PIECE)]
         interleave_tokens(nc.vector.tensor_copy, 1, 0, PIECE)
         for lo, hi in halves:

@@ -151,10 +151,10 @@ def tile_attend_ggqa_sig_k_pl_kernel(tc, q1, q2, kT, dp1, dp2, us, ts, w1, w2, o
         for h in range(2):
             nc.gpsimd.tensor_tensor(out=gate[h][:], in0=w_quarter[h][:], in1=us_col[:], op=ALU.mult)
         factor = [held([P, PACK, SLOTS], F32, "factor%d" % h) for h in range(2)]
-        for h, engine in enumerate((nc.gpsimd, nc.vector)):
+        for h in range(2):
             for t in range(PACK):
-                engine.tensor_scalar(out=factor[h][:, t, :], in0=ts_rows[:],
-                                     scalar1=gate[h][:, t:t + 1], scalar2=0.0, op0=ALU.mult, op1=ALU.add)
+                nc.gpsimd.tensor_scalar(out=factor[h][:, t, :], in0=ts_rows[:],
+                                        scalar1=gate[h][:, t:t + 1], scalar2=0.0, op0=ALU.mult, op1=ALU.add)
 
         keys = [mx_tiles(HALF, "k0", grouped_tag="qr1_grouped"), mx_tiles(HALF, "k1")]
         k_places = keys[0][0][:].rearrange("p (c t) -> p c t", t=PACK)
@@ -193,11 +193,12 @@ def tile_attend_ggqa_sig_k_pl_kernel(tc, q1, q2, kT, dp1, dp2, us, ts, w1, w2, o
 
         def weigh(engine, n, count, tag=None):
             h, b = TILES[n]
-            tile = held([P, PACK, count * P], F32, "weight%d" % n, tag=tag)
+            tile = held([P, count * BANK], F32, "weight%d" % n, tag=tag)
             cols = slice(b * P, (b + count) * P)
-            engine.tensor_tensor(out=tile[:], in0=dp_raw[h][:, :, cols], in1=factor[h][:, :, cols], op=ALU.mult)
+            engine.tensor_tensor(out=in_places(tile[:]), in0=in_runs(dp_raw[h][:, :, cols]),
+                                 in1=in_runs(factor[h][:, :, cols]), op=ALU.mult)
             for m in range(count):
-                weight[n + m] = tile[:, :, m * P:(m + 1) * P]
+                weight[n + m] = tile[:, m * BANK:(m + 1) * BANK]
 
         weigh(nc.gpsimd, 0, 2, tag="k1_grouped")
         weigh(nc.gpsimd, 2, 2)
@@ -215,7 +216,7 @@ def tile_attend_ggqa_sig_k_pl_kernel(tc, q1, q2, kT, dp1, dp2, us, ts, w1, w2, o
             nc.vector.scalar_tensor_tensor(
                 out=g_halves[half][0][:, BANK * (n % 4):BANK * (n % 4 + 1)].rearrange("p (c t) -> p c t", t=PACK),
                 in0=turned[n][:].rearrange("p (t c) -> p c t", t=PACK), scalar=1.0,
-                in1=weight[n].rearrange("p t c -> p c t"), op0=ALU.subtract, op1=ALU.mult)
+                in1=weight[n].rearrange("p (c t) -> p c t", t=PACK), op0=ALU.subtract, op1=ALU.mult)
 
         def product(out, j, half, h):
             cols = slice(j * P, (j + 1) * P)

@@ -73,6 +73,8 @@ def tile_attend_ggqa_sig_k_pl_kernel(tc, q1, q2, kT, dp1, dp2, us, ts, w1, w2, o
 
         ident = held([P, P], F32, "ident")
         make_identity(nc, ident[:])
+        minus_one = held([P, 1], F32, "minus_one")
+        nc.gpsimd.memset(minus_one[:], -1.0)
         windows = {t: held([P, TOKENS], F32, "window%d" % t) for t in (0, 1, 2)}
         clear_on_vector(windows[1])
         for t in (0, 2):
@@ -193,12 +195,11 @@ def tile_attend_ggqa_sig_k_pl_kernel(tc, q1, q2, kT, dp1, dp2, us, ts, w1, w2, o
 
         def weigh(engine, n, count, tag=None):
             h, b = TILES[n]
-            tile = held([P, count * BANK], F32, "weight%d" % n, tag=tag)
+            tile = held([P, PACK, count * P], F32, "weight%d" % n, tag=tag)
             cols = slice(b * P, (b + count) * P)
-            engine.tensor_tensor(out=in_places(tile[:]), in0=in_runs(dp_raw[h][:, :, cols]),
-                                 in1=in_runs(factor[h][:, :, cols]), op=ALU.mult)
+            engine.tensor_tensor(out=tile[:], in0=dp_raw[h][:, :, cols], in1=factor[h][:, :, cols], op=ALU.mult)
             for m in range(count):
-                weight[n + m] = tile[:, m * BANK:(m + 1) * BANK]
+                weight[n + m] = tile[:, :, m * P:(m + 1) * P]
 
         weigh(nc.gpsimd, 0, 2, tag="k1_grouped")
         weigh(nc.gpsimd, 2, 2)
@@ -207,16 +208,17 @@ def tile_attend_ggqa_sig_k_pl_kernel(tc, q1, q2, kT, dp1, dp2, us, ts, w1, w2, o
         turned = {}
 
         def turn(n):
-            turned[n] = bank("c%d" % (n % 4))
+            turned[n] = bank("%s%d" % ("ca"[n // 4], n % 4))
             for t in range(PACK):
-                nc.tensor.transpose(turned[n][:, t * P:(t + 1) * P], squares[n][:, t * P:(t + 1) * P], ident[:])
+                nc.tensor.matmul(turned[n][:, t * P:(t + 1) * P], lhsT=minus_one[:].to_broadcast([P, P]), rhs=ident[:],
+                                 is_transpose=True, start=t == 0, stop=False)
+            for t in range(PACK):
+                nc.tensor.matmul(turned[n][:, t * P:(t + 1) * P], lhsT=squares[n][:, t * P:(t + 1) * P], rhs=ident[:],
+                                 is_transpose=True, start=False, stop=t == PACK - 1)
 
         def gradient(n):
-            half = n // 4
-            nc.vector.scalar_tensor_tensor(
-                out=g_halves[half][0][:, BANK * (n % 4):BANK * (n % 4 + 1)].rearrange("p (c t) -> p c t", t=PACK),
-                in0=turned[n][:].rearrange("p (t c) -> p c t", t=PACK), scalar=1.0,
-                in1=weight[n].rearrange("p (c t) -> p c t", t=PACK), op0=ALU.subtract, op1=ALU.mult)
+            nc.vector.tensor_tensor(out=in_places(g_halves[n // 4][0][:, BANK * (n % 4):BANK * (n % 4 + 1)]), in0=in_runs(weight[n]),
+                                    in1=in_runs(turned[n][:].rearrange("p (t c) -> p t c", t=PACK)), op=ALU.mult)
 
         def product(out, j, half, h):
             cols = slice(j * P, (j + 1) * P)
@@ -229,19 +231,25 @@ def tile_attend_ggqa_sig_k_pl_kernel(tc, q1, q2, kT, dp1, dp2, us, ts, w1, w2, o
             turn(n)
         for n in range(4):
             gradient(n)
-            turn(n + 4)
+        turn(4)
+        turn(5)
         quantize(*g_halves[0], E5M2, 0, 2 * HALF)
         weigh(nc.gpsimd, 6, 1, tag="us_half")
-        odd_firsts = bank("a2")
-        firsts = {0: bank("a0")[:, 0:HALF], 2: bank("a1")[:, 0:HALF], 1: odd_firsts[:, 0:HALF], 3: odd_firsts[:, HALF:2 * HALF]}
-        for j in ORDER:
+        firsts = {0: bank("c0")[:, 0:HALF], 2: bank("c1")[:, 0:HALF]}
+        for j in firsts:
             for h in range(2):
                 product(firsts[j], j, 0, h)
+        turn(6)
+        turn(last)
         g_halves.append(mx_tiles(2 * HALF, "g1", codes_tag="dp_raw1"))
         gradient(4)
         gradient(5)
         weigh(nc.vector, last, 1, tag="weight4")
         gradient(6)
+        odd_firsts = bank("a2")
+        for j in (1, 3):
+            for h in range(2):
+                product(odd_firsts[:, j // 2 * HALF:(j // 2 + 1) * HALF], j, 0, h)
         quantize(*g_halves[1], E5M2, 0, HALF)
         gradient(last)
         quantize(*g_halves[1], E5M2, HALF, HALF + P)
@@ -250,7 +258,7 @@ def tile_attend_ggqa_sig_k_pl_kernel(tc, q1, q2, kT, dp1, dp2, us, ts, w1, w2, o
         nc.vector.tensor_copy(out=dk_odd[:].rearrange("p j c -> p (j c)"), in_=odd_firsts[:])
         windows[3] = held([P, TOKENS], F32, "window3", tag="g1_grouped")
         nc.gpsimd.memset(windows[3][:], 0.0)
-        seconds = {j: bank(tag) for j, tag in zip(ORDER, ("a3", "c0", "c2", "c3"))}
+        seconds = {j: bank(tag) for j, tag in zip(ORDER, ("c2", "c3", "a0", "a3"))}
         for h in range(2):
             for j in ORDER:
                 product(seconds[j][:, 0:HALF], j, 1, h)

@@ -73,7 +73,7 @@ def tile_attend_ggqa_sig_k_pl_kernel(tc, q1, q2, kT, dp1, dp2, us, ts, w1, w2, o
 
         ident = held([P, P], F32, "ident")
         make_identity(nc, ident[:])
-        minus_one = held([P, 1], F32, "minus_one")
+        minus_one = held([P, P], F32, "minus_one")
         nc.gpsimd.memset(minus_one[:], -1.0)
         windows = {t: held([P, TOKENS], F32, "window%d" % t) for t in (0, 1, 2)}
         clear_on_vector(windows[1])
@@ -155,7 +155,7 @@ def tile_attend_ggqa_sig_k_pl_kernel(tc, q1, q2, kT, dp1, dp2, us, ts, w1, w2, o
         factor = [held([P, PACK, SLOTS], F32, "factor%d" % h) for h in range(2)]
         for h in range(2):
             for t in range(PACK):
-                nc.gpsimd.tensor_scalar(out=factor[h][:, t, :], in0=ts_rows[:],
+                nc.vector.tensor_scalar(out=factor[h][:, t, :], in0=ts_rows[:],
                                         scalar1=gate[h][:, t:t + 1], scalar2=0.0, op0=ALU.mult, op1=ALU.add)
 
         keys = [mx_tiles(HALF, "k0", grouped_tag="qr1_grouped"), mx_tiles(HALF, "k1")]
@@ -210,7 +210,7 @@ def tile_attend_ggqa_sig_k_pl_kernel(tc, q1, q2, kT, dp1, dp2, us, ts, w1, w2, o
         def turn(n):
             turned[n] = bank("%s%d" % ("ca"[n // 4], n % 4))
             for t in range(PACK):
-                nc.tensor.matmul(turned[n][:, t * P:(t + 1) * P], lhsT=minus_one[:].to_broadcast([P, P]), rhs=ident[:],
+                nc.tensor.matmul(turned[n][:, t * P:(t + 1) * P], lhsT=minus_one[:], rhs=ident[:],
                                  is_transpose=True, start=t == 0, stop=False)
             for t in range(PACK):
                 nc.tensor.matmul(turned[n][:, t * P:(t + 1) * P], lhsT=squares[n][:, t * P:(t + 1) * P], rhs=ident[:],

@@ -41,10 +41,13 @@ def tile_attend_ggqa_sig_k_pl_kernel(tc, q1, q2, kT, dp1, dp2, us, ts, w1, w2, o
         def bank(tag):
             return psum.tile([P, BANK], F32, name=tag, tag=tag)
 
-        def clear_on_vector(tile):
-            odd = TOKENS // 2 + 1
-            nc.vector.memset(tile[:, 0:odd], 0.0)
-            nc.vector.memset(tile[:, odd:TOKENS], 0.0)
+        def clear_on_vector(tile, lo, hi):
+            nc.vector.memset(tile[:, lo:lo + 1], 0.0)
+            nc.vector.memset(tile[:, lo + 1:hi], 0.0)
+
+        def clear_together(tile):
+            clear_on_vector(tile, 0, TOKENS // 2)
+            nc.gpsimd.memset(tile[:, TOKENS // 2:TOKENS], 0.0)
 
         def load_column(name, vec):
             tile = held([P, PACK], F32, name)
@@ -58,7 +61,7 @@ def tile_attend_ggqa_sig_k_pl_kernel(tc, q1, q2, kT, dp1, dp2, us, ts, w1, w2, o
 
         offsets = keep.tile([P, SLOTS // 16], U16, name="offsets")
         ts_row = held([P, TOKENS], F32, "ts_row")
-        clear_on_vector(ts_row)
+        clear_together(ts_row)
         q_raw = [load_rows("q_raw0", q1)]
         nc.sync.dma_start(offsets[:], offs)
         nc.sync.dma_start(out=ts_row[0:1, :], in_=ts[0:1, :])
@@ -76,9 +79,9 @@ def tile_attend_ggqa_sig_k_pl_kernel(tc, q1, q2, kT, dp1, dp2, us, ts, w1, w2, o
         minus_one = held([P, P], F32, "minus_one")
         nc.gpsimd.memset(minus_one[:], -1.0)
         windows = {t: held([P, TOKENS], F32, "window%d" % t) for t in (0, 1, 2)}
-        clear_on_vector(windows[1])
-        for t in (0, 2):
-            nc.gpsimd.memset(windows[t][:], 0.0)
+        clear_on_vector(windows[1], 0, TOKENS)
+        nc.gpsimd.memset(windows[0][:], 0.0)
+        clear_together(windows[2])
 
         def listed(lo, hi):
             return offsets[:, lo // 16:hi // 16]
@@ -115,7 +118,7 @@ def tile_attend_ggqa_sig_k_pl_kernel(tc, q1, q2, kT, dp1, dp2, us, ts, w1, w2, o
         for b in range(SLOTS // P):
             nc.tensor.transpose(ts_spread[:, b * P:(b + 1) * P], ts_col[:, b:b + 1].to_broadcast([P, P]), ident[:])
         ts_rows = held([P, SLOTS], F32, "ts_rows")
-        nc.scalar.copy(out=ts_rows[:], in_=ts_spread[:])
+        nc.vector.tensor_copy(out=ts_rows[:], in_=ts_spread[:])
 
         ps = bank("a2")
         for t in range(PACK):
@@ -125,27 +128,33 @@ def tile_attend_ggqa_sig_k_pl_kernel(tc, q1, q2, kT, dp1, dp2, us, ts, w1, w2, o
 
         qd = [mx_tiles(R, "qd%d" % h) for h in range(2)]
         qr = [mx_tiles(D, "qr%d" % h) for h in range(2)]
+        q_rounded = [held([P, PACK * R], BF16, "q_rounded%d" % h, tag=tag) for h, tag in enumerate(("ts_listed", None))]
 
         def group_along_d(h):
             nc.vector.tensor_copy(out=qd[h][0][:].rearrange("p (i m t) -> p m t i", i=PACK, t=PACK),
                                   in_=q_raw[h][:].rearrange("p t (m i) -> p m t i", i=PACK))
 
         def group_along_r(h):
-            words = qd[h][0][:].bitcast(F32)
-            for u in range(2):
-                ps = bank("c%d" % (2 * h + u))
-                for i in range(PACK):
-                    nc.tensor.transpose(ps[:, i * P:(i + 1) * P], words[:, 2 * P * i + u:2 * P * (i + 1):2], ident[:])
+            words = q_rounded[h][:].bitcast(F32)
+            turned_words = qr[h][0][:].bitcast(F32)
+            row = R // 2
+            for pair in range(2):
+                ps = bank("c%d" % (2 * h + pair))
+                for jj in range(2):
+                    j = 2 * pair + jj
+                    for u in range(2):
+                        nc.tensor.transpose(ps[:, (2 * jj + u) * P:(2 * jj + u + 1) * P],
+                                            words[:, row * j + u:row * (j + 1):2], ident[:])
                 nc.scalar.copy(
-                    out=qr[h][0][:, 2 * BANK * u:2 * BANK * (u + 1)].rearrange("m (e p i) -> m e p i", e=2, i=PACK),
-                    in_=ps[:].bitcast(BF16).rearrange("m (i p e) -> m e p i", i=PACK, e=2))
+                    out=turned_words[:, BANK * pair:BANK * (pair + 1)].rearrange("p (j m u) -> p j m u", j=2, u=2),
+                    in_=ps[:].rearrange("p (j u m) -> p j m u", j=2, u=2))
 
+        for h in range(2):
+            nc.scalar.copy(out=q_rounded[h][:], in_=q_raw[h][:].rearrange("p t r -> p (t r)"))
         for h in range(2):
             group_along_d(h)
             group_along_r(h)
-        for h in range(2):
             quantize(*qd[h], E4M3, 0, R)
-
         for h in range(2):
             quantize(*qr[h], E4M3, 0, D)
 

@@ -26,6 +26,7 @@ RUN = 4
 PIECE = 512
 TILES = [(h, 2 * half + b) for half in range(2) for h in range(2) for b in range(2)]
 ORDER = (0, 2, 1, 3)
+VECTOR_CLEARS = 1408
 FLOPS = 4 * 2 * D * R * SLOTS
 
 
@@ -45,9 +46,9 @@ def tile_attend_ggqa_sig_k_pl_kernel(tc, q1, q2, kT, dp1, dp2, us, ts, w1, w2, o
             nc.vector.memset(tile[:, lo:lo + 1], 0.0)
             nc.vector.memset(tile[:, lo + 1:hi], 0.0)
 
-        def clear_together(tile):
-            clear_on_vector(tile, 0, TOKENS // 2)
-            nc.gpsimd.memset(tile[:, TOKENS // 2:TOKENS], 0.0)
+        def clear_together(tile, split):
+            clear_on_vector(tile, 0, split)
+            nc.gpsimd.memset(tile[:, split:TOKENS], 0.0)
 
         def load_column(name, vec):
             tile = held([P, PACK], F32, name)
@@ -61,7 +62,7 @@ def tile_attend_ggqa_sig_k_pl_kernel(tc, q1, q2, kT, dp1, dp2, us, ts, w1, w2, o
 
         offsets = keep.tile([P, SLOTS // 16], U16, name="offsets")
         ts_row = held([P, TOKENS], F32, "ts_row")
-        clear_together(ts_row)
+        clear_together(ts_row, TOKENS // 2)
         q_raw = [load_rows("q_raw0", q1)]
         nc.sync.dma_start(offsets[:], offs)
         nc.sync.dma_start(out=ts_row[0:1, :], in_=ts[0:1, :])
@@ -81,7 +82,7 @@ def tile_attend_ggqa_sig_k_pl_kernel(tc, q1, q2, kT, dp1, dp2, us, ts, w1, w2, o
         windows = {t: held([P, TOKENS], F32, "window%d" % t) for t in (0, 1, 2)}
         clear_on_vector(windows[1], 0, TOKENS)
         nc.gpsimd.memset(windows[0][:], 0.0)
-        clear_together(windows[2])
+        clear_together(windows[2], VECTOR_CLEARS)
 
         def listed(lo, hi):
             return offsets[:, lo // 16:hi // 16]
@@ -114,11 +115,9 @@ def tile_attend_ggqa_sig_k_pl_kernel(tc, q1, q2, kT, dp1, dp2, us, ts, w1, w2, o
             nc.tensor.transpose(ps[:, b * P:(b + 1) * P], ts_listed[:, b * P:(b + 1) * P], ident[:])
         ts_col = held([P, SLOTS // P], F32, "ts_col")
         nc.scalar.copy(out=ts_col[:], in_=ps[:, 0:SLOTS:P])
-        ts_spread = bank("a1")
+        ts_spread = bank("a3")
         for b in range(SLOTS // P):
             nc.tensor.transpose(ts_spread[:, b * P:(b + 1) * P], ts_col[:, b:b + 1].to_broadcast([P, P]), ident[:])
-        ts_rows = held([P, SLOTS], F32, "ts_rows")
-        nc.vector.tensor_copy(out=ts_rows[:], in_=ts_spread[:])
 
         ps = bank("a2")
         for t in range(PACK):
@@ -128,7 +127,7 @@ def tile_attend_ggqa_sig_k_pl_kernel(tc, q1, q2, kT, dp1, dp2, us, ts, w1, w2, o
 
         qd = [mx_tiles(R, "qd%d" % h) for h in range(2)]
         qr = [mx_tiles(D, "qr%d" % h) for h in range(2)]
-        q_rounded = [held([P, PACK * R], BF16, "q_rounded%d" % h, tag=tag) for h, tag in enumerate(("ts_listed", None))]
+        q_rounded = [held([P, PACK * R], BF16, "q_rounded%d" % h) for h in range(2)]
 
         def group_along_d(h):
             nc.vector.tensor_copy(out=qd[h][0][:].rearrange("p (i m t) -> p m t i", i=PACK, t=PACK),
@@ -150,8 +149,7 @@ def tile_attend_ggqa_sig_k_pl_kernel(tc, q1, q2, kT, dp1, dp2, us, ts, w1, w2, o
                     in_=ps[:].rearrange("p (j u m) -> p j m u", j=2, u=2))
 
         for h in range(2):
-            nc.scalar.copy(out=q_rounded[h][:], in_=q_raw[h][:].rearrange("p t r -> p (t r)"))
-        for h in range(2):
+            nc.vector.tensor_copy(out=q_rounded[h][:], in_=q_raw[h][:].rearrange("p t r -> p (t r)"))
             group_along_d(h)
             group_along_r(h)
             quantize(*qd[h], E4M3, 0, R)
@@ -164,8 +162,7 @@ def tile_attend_ggqa_sig_k_pl_kernel(tc, q1, q2, kT, dp1, dp2, us, ts, w1, w2, o
         factor = [held([P, PACK, SLOTS], F32, "factor%d" % h) for h in range(2)]
         for h in range(2):
             for t in range(PACK):
-                nc.vector.tensor_scalar(out=factor[h][:, t, :], in0=ts_rows[:],
-                                        scalar1=gate[h][:, t:t + 1], scalar2=0.0, op0=ALU.mult, op1=ALU.add)
+                nc.scalar.activation(out=factor[h][:, t, :], in_=ts_spread[:], func=ACT.Copy, scale=gate[h][:, t:t + 1])
 
         keys = [mx_tiles(HALF, "k0", grouped_tag="qr1_grouped"), mx_tiles(HALF, "k1")]
         k_places = keys[0][0][:].rearrange("p (c t) -> p c t", t=PACK)

@@ -25,7 +25,7 @@ BANK = 512
 RUN = 4
 PIECE = 512
 TILES = [(h, 2 * half + b) for half in range(2) for h in range(2) for b in range(2)]
-ORDER = (0, 2, 1, 3)
+DIRECT = 1152
 VECTOR_CLEARS = 1408
 FLOPS = 4 * 2 * D * R * SLOTS
 
@@ -73,7 +73,12 @@ def tile_attend_ggqa_sig_k_pl_kernel(tc, q1, q2, kT, dp1, dp2, us, ts, w1, w2, o
         k_raw = [held([P, TOKENS], F32, "k_raw%d" % t) for t in range(PACK)]
         for t in range(PACK):
             nc.sync.dma_start(out=k_raw[t][:], in_=k_planes[:, t, :])
-        dp_raw = [load_rows("dp_raw0", dp1), load_rows("dp_raw1", dp2)]
+        dp_raw = {}
+        for half in range(2):
+            for h, dp in enumerate((dp1, dp2)):
+                dp_raw[h, half] = held([P, PACK, HALF], F32, "dp_raw%d%d" % (h, half))
+                nc.sync.dma_start(out=dp_raw[h, half][:],
+                                  in_=dp.rearrange("(p t) c -> p t c", t=PACK)[:, :, half * HALF:(half + 1) * HALF])
 
         ident = held([P, P], F32, "ident")
         make_identity(nc, ident[:])
@@ -164,7 +169,7 @@ def tile_attend_ggqa_sig_k_pl_kernel(tc, q1, q2, kT, dp1, dp2, us, ts, w1, w2, o
             for t in range(PACK):
                 nc.scalar.activation(out=factor[h][:, t, :], in_=ts_spread[:], func=ACT.Copy, scale=gate[h][:, t:t + 1])
 
-        keys = [mx_tiles(HALF, "k0", grouped_tag="qr1_grouped"), mx_tiles(HALF, "k1")]
+        keys = [mx_tiles(HALF, "k0", grouped_tag="qr1_grouped"), mx_tiles(HALF, "k1", codes_tag="dp_raw00")]
         k_places = keys[0][0][:].rearrange("p (c t) -> p c t", t=PACK)
         k_early = held([P, 2, HALF], BF16, "k_early")
         for t in (0, 1):
@@ -177,14 +182,27 @@ def tile_attend_ggqa_sig_k_pl_kernel(tc, q1, q2, kT, dp1, dp2, us, ts, w1, w2, o
             nc.scalar.activation(out=k_late[:, t, :], in_=k_raw[t][:].indirect(listed(HALF, SLOTS)), func=ACT.Copy)
         interleave(nc.scalar.copy, keys[1][0][:], k_late[:])
 
+        weight = {}
+
+        def weigh(n, count, tag=None):
+            h, b = TILES[n]
+            tile = held([P, PACK, count * P], F32, "weight%d" % n, tag=tag)
+            nc.gpsimd.tensor_tensor(out=tile[:], in0=dp_raw[h, b // 2][:, :, b % 2 * P:(b % 2 + count) * P],
+                                    in1=factor[h][:, :, b * P:(b + count) * P], op=ALU.mult)
+            for m in range(count):
+                weight[n + m] = tile[:, :, m * P:(m + 1) * P]
+
         squares = [held([P, R], F32, "square%d" % n) for n in range(len(TILES))]
 
         def square(n):
             nc.scalar.activation(out=squares[n][:], in_=squares[n][:], func=ACT.Square)
 
         for n, (h, b) in enumerate(TILES):
-            if n < 2:
-                quantize(*keys[n], E4M3, 0, HALF)
+            if n == 0:
+                quantize(*keys[0], E4M3, 0, HALF)
+                weigh(0, 2, tag="qr1_grouped")
+            if n == 3:
+                quantize(*keys[1], E4M3, 0, HALF)
             cols = slice(b % 2 * P, (b % 2 + 1) * P)
             score = bank("a%d" % (n % 4))
             nc.tensor.matmul_mx(out=score[:], lhsT=keys[b // 2][1][:, cols].bitcast(E4M3), lhsT_scale=keys[b // 2][2][:, cols],
@@ -196,20 +214,9 @@ def tile_attend_ggqa_sig_k_pl_kernel(tc, q1, q2, kT, dp1, dp2, us, ts, w1, w2, o
         last = len(TILES) - 1
         square(last)
 
-        g_halves = [mx_tiles(2 * HALF, "g0", grouped_tag="us_half", codes_tag="factor0")]
-        weight = {}
-
-        def weigh(engine, n, count, tag=None):
-            h, b = TILES[n]
-            tile = held([P, PACK, count * P], F32, "weight%d" % n, tag=tag)
-            cols = slice(b * P, (b + count) * P)
-            engine.tensor_tensor(out=tile[:], in0=dp_raw[h][:, :, cols], in1=factor[h][:, :, cols], op=ALU.mult)
-            for m in range(count):
-                weight[n + m] = tile[:, :, m * P:(m + 1) * P]
-
-        weigh(nc.gpsimd, 0, 2, tag="k1_grouped")
-        weigh(nc.gpsimd, 2, 2)
-        weigh(nc.gpsimd, 4, 2)
+        weigh(2, 2, tag="k1_grouped")
+        weigh(4, 2)
+        g_halves = [mx_tiles(2 * HALF, "g0", grouped_tag="us_half", codes_tag="dp_raw01"), mx_tiles(2 * HALF, "g1")]
 
         turned = {}
 
@@ -233,6 +240,13 @@ def tile_attend_ggqa_sig_k_pl_kernel(tc, q1, q2, kT, dp1, dp2, us, ts, w1, w2, o
                                 rhs=g_halves[half][1][:, slots].bitcast(E5M2), rhs_scale=g_halves[half][2][:, slots],
                                 start=h == 0, stop=h == 1)
 
+        def two_planes(tag, j0, half):
+            ps = bank(tag)
+            for jj in range(2):
+                for h in range(2):
+                    product(ps[:, jj * HALF:(jj + 1) * HALF], j0 + jj, half, h)
+            return ps
+
         for n in range(4):
             turn(n)
         for n in range(4):
@@ -240,41 +254,40 @@ def tile_attend_ggqa_sig_k_pl_kernel(tc, q1, q2, kT, dp1, dp2, us, ts, w1, w2, o
         turn(4)
         turn(5)
         quantize(*g_halves[0], E5M2, 0, 2 * HALF)
-        weigh(nc.gpsimd, 6, 1, tag="us_half")
-        firsts = {0: bank("c0")[:, 0:HALF], 2: bank("c1")[:, 0:HALF]}
-        for j in firsts:
-            for h in range(2):
-                product(firsts[j], j, 0, h)
+        weigh(6, 1, tag="us_half")
+        weigh(last, 1)
+        gradient(4)
+        early_firsts = two_planes("c0", 0, 0)
         turn(6)
         turn(last)
-        g_halves.append(mx_tiles(2 * HALF, "g1", codes_tag="dp_raw1"))
-        gradient(4)
         gradient(5)
-        weigh(nc.vector, last, 1, tag="weight4")
-        gradient(6)
-        odd_firsts = bank("a2")
-        for j in (1, 3):
-            for h in range(2):
-                product(odd_firsts[:, j // 2 * HALF:(j // 2 + 1) * HALF], j, 0, h)
         quantize(*g_halves[1], E5M2, 0, HALF)
+        gradient(6)
+        late_firsts = two_planes("a2", 2, 0)
         gradient(last)
         quantize(*g_halves[1], E5M2, HALF, HALF + P)
         quantize(*g_halves[1], E5M2, HALF + P, 2 * HALF)
-        dk_odd = held([P, 2, HALF], F32, "dk_odd", tag="weight4")
-        nc.vector.tensor_copy(out=dk_odd[:].rearrange("p j c -> p (j c)"), in_=odd_firsts[:])
         windows[3] = held([P, TOKENS], F32, "window3", tag="g1_grouped")
         nc.gpsimd.memset(windows[3][:], 0.0)
-        seconds = {j: bank(tag) for j, tag in zip(ORDER, ("c2", "c3", "a0", "a3"))}
+        seconds = {0: bank("c2"), 1: bank("c3")}
         for h in range(2):
-            for j in ORDER:
+            for j in seconds:
                 product(seconds[j][:, 0:HALF], j, 1, h)
+        late_seconds = two_planes("a0", 2, 1)
 
         out_planes = out_0.rearrange("(p t) c -> p t c", t=PACK)
-        dk = {(1, 0): dk_odd[:, 0, :], (3, 0): dk_odd[:, 1, :]}
+        dk = {}
+        dk_seconds = held([P, 2 * HALF], F32, "dk_seconds")
 
-        def empty(mover, j, half, tag=None):
-            dk[j, half] = held([P, HALF], F32, "dk%d%d" % (j, half), tag=tag)[:]
-            mover(out=dk[j, half], in_=seconds[j][:, 0:HALF] if half else firsts[j])
+        def empty_one(j):
+            dk[j, 1] = dk_seconds[:, j * HALF:(j + 1) * HALF]
+            nc.vector.tensor_copy(out=dk[j, 1], in_=seconds[j][:, 0:HALF])
+
+        def empty_two(mover, ps, j0, half, tag=None):
+            tile = held([P, 2 * HALF], F32, "dk_pair%d%d" % (j0, half), tag=tag)
+            mover(out=tile[:], in_=ps[:])
+            for jj in range(2):
+                dk[j0 + jj, half] = tile[:, jj * HALF:(jj + 1) * HALF]
 
         def scatter(on_scalar, j, half):
             window = windows[j][:].indirect(listed(half * HALF, (half + 1) * HALF))
@@ -286,69 +299,97 @@ def tile_attend_ggqa_sig_k_pl_kernel(tc, q1, q2, kT, dp1, dp2, us, ts, w1, w2, o
         def store_plane(queue, j):
             queue.dma_start(out=out_planes[:, j, :], in_=windows[j][:])
 
-        for half in range(2):
-            for j in (0, 2):
-                empty(nc.scalar.copy, j, half)
-            for j in (0, 2):
-                scatter(True, j, half)
-                if half:
-                    store_plane(nc.sync if j else nc.scalar, j)
-        for j in (1, 3):
-            scatter(False, j, 0)
-        empty(nc.vector.tensor_copy, 1, 1, tag="weight4")
-        scatter(False, 1, 1)
+        empty_two(nc.scalar.copy, early_firsts, 0, 0)
+        for j in (0, 1):
+            scatter(True, j, 0)
+        empty_two(nc.vector.tensor_copy, late_firsts, 2, 0, tag="weight7")
+        for j in (0, 1):
+            empty_one(j)
+        scatter(False, 0, 1)
+        store_plane(nc.sync, 0)
+        scatter(True, 1, 1)
         store_plane(nc.sync, 1)
-        empty(nc.scalar.copy, 3, 1)
+        scatter(False, 2, 0)
+        scatter(True, 3, 0)
+        empty_two(nc.vector.tensor_copy, late_seconds, 2, 1, tag="dk_seconds")
+        scatter(False, 2, 1)
+        store_plane(nc.sync, 2)
         scatter(True, 3, 1)
         store_plane(nc.sync, 3)
 
-        rounded_first = held([P, PACK, PIECE], BF16, "rounded_first", tag="dk31")
-        rounded_rest = held([P, PACK, TOKENS - PIECE], BF16, "rounded_rest", tag="dp_raw0")
         y_codes = held([P, TOKENS], U32, "y_codes")
         y_scales = held([P, TOKENS // 2], U8, "y_scales")
         words_out = out_1.rearrange("a p c t -> p (a c t)").bitcast(I32)
 
+        stores = {PIECE: 0, DIRECT: PIECE, DIRECT + PIECE: DIRECT, TOKENS: DIRECT + PIECE}
+
+        def quantize_and_store(grouped, lo, hi):
+            a, col = divmod(lo, TOKENS // 2)
+            nc.vector.quantize_mx(out=y_codes[:, lo:hi].bitcast(E4M3), scales=y_scales[4 * a:P, col:col + hi - lo], in_=grouped)
+            if hi in stores:
+                nc.sync.dma_start(out=words_out[:, stores[hi]:hi], in_=y_codes[:, stores[hi]:hi].bitcast(I32))
+
         def round_on_gpsimd(out, in_):
             nc.gpsimd.tensor_scalar(out=out, in0=in_, scalar1=1.0, scalar2=-0.0, op0=ALU.mult, op1=ALU.add)
 
-        def round_first(mover, j):
-            mover(out=rounded_first[:, j, :], in_=windows[j][:, 0:PIECE])
-
-        def round_rest(mover, j):
-            mover(out=rounded_rest[:, j, :], in_=windows[j][:, PIECE:TOKENS])
-
-        y_grouped = [held([P, PIECE * PACK], BF16, "y_grouped%d" % c, tag=tag)[:]
-                     for c, tag in enumerate(("k_raw0", "k_raw1", "k_raw2", "dk31"))]
-
-        def interleave_tokens(mover, c, lo, hi):
-            planes = rounded_first[:] if c == 0 else rounded_rest[:, :, (c - 1) * PIECE:c * PIECE]
-            interleave(mover, y_grouped[c][:, PACK * lo:PACK * hi], planes[:, :, lo:hi])
-
-        def quantize_and_store(c, lo, hi):
-            span = slice(c * PIECE + lo, c * PIECE + hi)
-            nc.vector.quantize_mx(out=y_codes[:, span].bitcast(E4M3),
-                                  scales=y_scales[4 * (c // 2):P, c % 2 * PIECE + lo:c % 2 * PIECE + hi],
-                                  in_=y_grouped[c][:, PACK * lo:PACK * hi])
-            nc.sync.dma_start(out=words_out[:, span], in_=y_codes[:, span].bitcast(I32))
-
-        for j in (0, 2):
-            round_rest(round_on_gpsimd, j)
+        rounded = held([P, PACK, DIRECT], BF16, "rounded", tag="dp_raw11")
         for j in (0, 1):
-            round_first(nc.vector.tensor_copy, j)
+            round_on_gpsimd(out=rounded[:, j, :], in_=windows[j][:, 0:DIRECT])
         for j in (2, 3):
-            round_first(nc.scalar.copy, j)
-        interleave_tokens(nc.scalar.copy, 0, 0, PIECE)
-        for j in (1, 3):
-            round_rest(nc.vector.tensor_copy, j)
-        halves = [(0, PIECE // 2), (PIECE // 2, PIECE)]
-        interleave_tokens(nc.vector.tensor_copy, 1, 0, PIECE)
-        for lo, hi in halves:
-            interleave_tokens(nc.scalar.copy, 3, lo, hi)
-        interleave_tokens(nc.vector.tensor_copy, 2, 0, PIECE)
-        for c in range(3):
-            quantize_and_store(c, 0, PIECE)
-        for lo, hi in halves:
-            quantize_and_store(3, lo, hi)
+            nc.vector.tensor_copy(out=rounded[:, j, :], in_=windows[j][:, 0:DIRECT])
+
+        chunks = [(lo, min(2, (TOKENS - lo) // P)) for lo in range(DIRECT, TOKENS, 2 * P)]
+        pair_banks = [("c1", "a1", "a3", "c0"), ("c2", "c3", "a2", "a0")]
+        first_pairs = held([P, len(chunks) * BANK], BF16, "first_pairs", tag="dk_seconds")
+        pairs = {}
+
+        def turn_planes(u, k):
+            ps = bank(pair_banks[u][k])
+            lo, blocks = chunks[k]
+            for b in range(blocks):
+                for e in range(2):
+                    nc.tensor.transpose(ps[:, (2 * b + e) * P:(2 * b + e + 1) * P],
+                                        windows[2 * u + e][:, lo + b * P:lo + (b + 1) * P], ident[:])
+            return ps
+
+        def pair_up(u, k, ps):
+            blocks = chunks[k][1]
+            width = 2 * P * blocks
+            pairs[u, k] = first_pairs[:, k * BANK:k * BANK + width] if u == 0 else held([P, width], BF16, "pairs%d" % k)[:]
+            nc.scalar.copy(out=pairs[u, k].rearrange("c (b p e) -> c b p e", b=blocks, e=2),
+                           in_=ps[:, 0:width].rearrange("c (b e p) -> c b p e", b=blocks, e=2))
+
+        def turn_back(k):
+            ps = bank(pair_banks[0][k])
+            blocks = chunks[k][1]
+            for u in range(2):
+                words = pairs[u, k].bitcast(F32)
+                for b in range(blocks):
+                    nc.tensor.transpose(ps[:, (blocks * u + b) * P:(blocks * u + b + 1) * P], words[:, b * P:(b + 1) * P], ident[:])
+            grouped = held([P, blocks * P * PACK], BF16, "turned_back%d" % k)
+            nc.scalar.copy(out=grouped[:].bitcast(F32).rearrange("p (c u) -> p c u", u=2),
+                           in_=ps[:, 0:2 * P * blocks].rearrange("p (u c) -> p c u", u=2))
+            return grouped[:]
+
+        for k in range(len(chunks)):
+            pair_up(0, k, turn_planes(0, k))
+        turned_planes = [turn_planes(1, k) for k in range(len(chunks))]
+        pair_up(1, 0, turned_planes[0])
+        late = []
+        for k in range(len(chunks)):
+            if k + 1 < len(chunks):
+                pair_up(1, k + 1, turned_planes[k + 1])
+            late.append(turn_back(k))
+
+        spans = [(lo, min(lo + PIECE, DIRECT)) for lo in range(0, DIRECT, PIECE)]
+        early = [held([P, (hi - lo) * PACK], BF16, "y_grouped%d" % c, tag="k_raw%d" % c)[:] for c, (lo, hi) in enumerate(spans)]
+        for c, (lo, hi) in enumerate(spans):
+            interleave(nc.vector.tensor_copy, early[c], rounded[:, :, lo:hi])
+            if c > 0:
+                quantize_and_store(early[c - 1], *spans[c - 1])
+        quantize_and_store(early[-1], *spans[-1])
+        for k, (lo, blocks) in enumerate(chunks):
+            quantize_and_store(late[k], lo, lo + blocks * P)
         scales_out = out_2.rearrange("a f c -> (a f) c").bitcast(I32).rearrange("f (a c) -> a f c", a=2)
         for quad in range(4):
             queue = nc.sync if quad % 2 == 0 else nc.scalar

@@ -26,7 +26,7 @@ RUN = 4
 PIECE = 512
 TILES = [(h, 2 * half + b) for half in range(2) for h in range(2) for b in range(2)]
 DIRECT = 1152
-VECTOR_CLEARS = 1408
+VECTOR_CLEARS = 256
 FLOPS = 4 * 2 * D * R * SLOTS
 
 
@@ -84,10 +84,9 @@ def tile_attend_ggqa_sig_k_pl_kernel(tc, q1, q2, kT, dp1, dp2, us, ts, w1, w2, o
         make_identity(nc, ident[:])
         minus_one = held([P, P], F32, "minus_one")
         nc.gpsimd.memset(minus_one[:], -1.0)
-        windows = {t: held([P, TOKENS], F32, "window%d" % t) for t in (0, 1, 2)}
+        windows = {t: held([P, TOKENS], F32, "window%d" % t) for t in (0, 1)}
         clear_on_vector(windows[1], 0, TOKENS)
-        nc.gpsimd.memset(windows[0][:], 0.0)
-        clear_together(windows[2], VECTOR_CLEARS)
+        clear_together(windows[0], VECTOR_CLEARS)
 
         def listed(lo, hi):
             return offsets[:, lo // 16:hi // 16]
@@ -172,13 +171,16 @@ def tile_attend_ggqa_sig_k_pl_kernel(tc, q1, q2, kT, dp1, dp2, us, ts, w1, w2, o
         keys = [mx_tiles(HALF, "k0", grouped_tag="qr1_grouped"), mx_tiles(HALF, "k1", codes_tag="dp_raw00")]
         k_places = keys[0][0][:].rearrange("p (c t) -> p c t", t=PACK)
         k_early = held([P, 2, HALF], BF16, "k_early")
+        k_late = held([P, PACK, HALF], BF16, "k_late")
         for t in (0, 1):
             nc.vector.tensor_copy(out=k_early[:, t, :], in_=k_raw[t][:].indirect(listed(0, HALF)))
+            nc.vector.tensor_copy(out=k_late[:, t, :], in_=k_raw[t][:].indirect(listed(HALF, SLOTS)))
         nc.vector.tensor_copy(out=k_places[:, :, 0:2], in_=k_early[:].rearrange("p t c -> p c t"))
         for t in (2, 3):
             nc.vector.tensor_copy(out=k_places[:, :, t], in_=k_raw[t][:].indirect(listed(0, HALF)))
-        k_late = held([P, PACK, HALF], BF16, "k_late")
-        for t in range(PACK):
+        windows[2] = held([P, TOKENS], F32, "window2", tag="k_early")
+        nc.gpsimd.memset(windows[2][:], 0.0)
+        for t in (2, 3):
             nc.scalar.activation(out=k_late[:, t, :], in_=k_raw[t][:].indirect(listed(HALF, SLOTS)), func=ACT.Copy)
         interleave(nc.scalar.copy, keys[1][0][:], k_late[:])
 
@@ -194,8 +196,12 @@ def tile_attend_ggqa_sig_k_pl_kernel(tc, q1, q2, kT, dp1, dp2, us, ts, w1, w2, o
 
         squares = [held([P, R], F32, "square%d" % n) for n in range(len(TILES))]
 
+        last = len(TILES) - 1
+        halves = [slice(0, R // 2), slice(R // 2, R)]
+
         def square(n):
-            nc.scalar.activation(out=squares[n][:], in_=squares[n][:], func=ACT.Square)
+            for part in halves if n == last else [slice(0, R)]:
+                nc.scalar.activation(out=squares[n][:, part], in_=squares[n][:, part], func=ACT.Square)
 
         for n, (h, b) in enumerate(TILES):
             if n == 0:
@@ -204,14 +210,14 @@ def tile_attend_ggqa_sig_k_pl_kernel(tc, q1, q2, kT, dp1, dp2, us, ts, w1, w2, o
             if n == 3:
                 quantize(*keys[1], E4M3, 0, HALF)
             cols = slice(b % 2 * P, (b % 2 + 1) * P)
-            score = bank("a%d" % (n % 4))
-            nc.tensor.matmul_mx(out=score[:], lhsT=keys[b // 2][1][:, cols].bitcast(E4M3), lhsT_scale=keys[b // 2][2][:, cols],
-                                rhs=qd[h][1][:].bitcast(E4M3), rhs_scale=qd[h][2][:], start=True, stop=True)
-            nc.vector.tensor_tensor(out=squares[n][:], in0=us_half[:], in1=score[:], op=ALU.mult)
-            nc.scalar.activation(out=squares[n][:], in_=squares[n][:], func=ACT.Tanh, scale=ts_col[:, b:b + 1])
+            for k, part in enumerate(halves if n == 0 else [slice(0, R)]):
+                score = bank("a%d" % (k if n == 0 else (n + 1) % 4))[:, part]
+                nc.tensor.matmul_mx(out=score, lhsT=keys[b // 2][1][:, cols].bitcast(E4M3), lhsT_scale=keys[b // 2][2][:, cols],
+                                    rhs=qd[h][1][:, part].bitcast(E4M3), rhs_scale=qd[h][2][:, part], start=True, stop=True)
+                nc.vector.tensor_tensor(out=squares[n][:, part], in0=us_half[:, part], in1=score, op=ALU.mult)
+                nc.scalar.activation(out=squares[n][:, part], in_=squares[n][:, part], func=ACT.Tanh, scale=ts_col[:, b:b + 1])
             if n > 0:
                 square(n - 1)
-        last = len(TILES) - 1
         square(last)
 
         weigh(2, 2, tag="k1_grouped")
@@ -221,7 +227,7 @@ def tile_attend_ggqa_sig_k_pl_kernel(tc, q1, q2, kT, dp1, dp2, us, ts, w1, w2, o
         turned = {}
 
         def turn(n):
-            turned[n] = bank("%s%d" % ("ca"[n // 4], n % 4))
+            turned[n] = bank("c%d" % n if n < 4 else "a%d" % ((n + 1) % 4))
             for t in range(PACK):
                 nc.tensor.matmul(turned[n][:, t * P:(t + 1) * P], lhsT=minus_one[:], rhs=ident[:],
                                  is_transpose=True, start=t == 0, stop=False)
@@ -247,6 +253,14 @@ def tile_attend_ggqa_sig_k_pl_kernel(tc, q1, q2, kT, dp1, dp2, us, ts, w1, w2, o
                     product(ps[:, jj * HALF:(jj + 1) * HALF], j0 + jj, half, h)
             return ps
 
+        dk = {}
+
+        def empty_two(mover, ps, j0, half, tag=None):
+            tile = held([P, 2 * HALF], F32, "dk_pair%d%d" % (j0, half), tag=tag)
+            mover(out=tile[:], in_=ps[:])
+            for jj in range(2):
+                dk[j0 + jj, half] = tile[:, jj * HALF:(jj + 1) * HALF]
+
         for n in range(4):
             turn(n)
         for n in range(4):
@@ -263,7 +277,7 @@ def tile_attend_ggqa_sig_k_pl_kernel(tc, q1, q2, kT, dp1, dp2, us, ts, w1, w2, o
         gradient(5)
         quantize(*g_halves[1], E5M2, 0, HALF)
         gradient(6)
-        late_firsts = two_planes("a2", 2, 0)
+        late_firsts = two_planes("a3", 2, 0)
         gradient(last)
         quantize(*g_halves[1], E5M2, HALF, HALF + P)
         quantize(*g_halves[1], E5M2, HALF + P, 2 * HALF)
@@ -273,21 +287,14 @@ def tile_attend_ggqa_sig_k_pl_kernel(tc, q1, q2, kT, dp1, dp2, us, ts, w1, w2, o
         for h in range(2):
             for j in seconds:
                 product(seconds[j][:, 0:HALF], j, 1, h)
-        late_seconds = two_planes("a0", 2, 1)
+        late_seconds = two_planes("a1", 2, 1)
 
         out_planes = out_0.rearrange("(p t) c -> p t c", t=PACK)
-        dk = {}
         dk_seconds = held([P, 2 * HALF], F32, "dk_seconds")
 
         def empty_one(j):
             dk[j, 1] = dk_seconds[:, j * HALF:(j + 1) * HALF]
             nc.vector.tensor_copy(out=dk[j, 1], in_=seconds[j][:, 0:HALF])
-
-        def empty_two(mover, ps, j0, half, tag=None):
-            tile = held([P, 2 * HALF], F32, "dk_pair%d%d" % (j0, half), tag=tag)
-            mover(out=tile[:], in_=ps[:])
-            for jj in range(2):
-                dk[j0 + jj, half] = tile[:, jj * HALF:(jj + 1) * HALF]
 
         def scatter(on_scalar, j, half):
             window = windows[j][:].indirect(listed(half * HALF, (half + 1) * HALF))
@@ -309,9 +316,9 @@ def tile_attend_ggqa_sig_k_pl_kernel(tc, q1, q2, kT, dp1, dp2, us, ts, w1, w2, o
         store_plane(nc.sync, 0)
         scatter(True, 1, 1)
         store_plane(nc.sync, 1)
+        empty_two(nc.scalar.copy, late_seconds, 2, 1)
         scatter(False, 2, 0)
         scatter(True, 3, 0)
-        empty_two(nc.vector.tensor_copy, late_seconds, 2, 1, tag="dk_seconds")
         scatter(False, 2, 1)
         store_plane(nc.sync, 2)
         scatter(True, 3, 1)
@@ -339,8 +346,8 @@ def tile_attend_ggqa_sig_k_pl_kernel(tc, q1, q2, kT, dp1, dp2, us, ts, w1, w2, o
             nc.vector.tensor_copy(out=rounded[:, j, :], in_=windows[j][:, 0:DIRECT])
 
         chunks = [(lo, min(2, (TOKENS - lo) // P)) for lo in range(DIRECT, TOKENS, 2 * P)]
-        pair_banks = [("c1", "a1", "a3", "c0"), ("c2", "c3", "a2", "a0")]
-        first_pairs = held([P, len(chunks) * BANK], BF16, "first_pairs", tag="dk_seconds")
+        pair_banks = [("c1", "a2", "a0", "c0"), ("c2", "c3", "a3", "a1")]
+        first_pairs = held([P, len(chunks) * BANK], BF16, "first_pairs", tag="dk_pair21")
         pairs = {}
 
         def turn_planes(u, k):

@@ -168,7 +168,7 @@ def tile_attend_ggqa_sig_k_pl_kernel(tc, q1, q2, kT, dp1, dp2, us, ts, w1, w2, o
             for t in range(PACK):
                 nc.scalar.activation(out=factor[h][:, t, :], in_=ts_spread[:], func=ACT.Copy, scale=gate[h][:, t:t + 1])
 
-        keys = [mx_tiles(HALF, "k0", grouped_tag="qr1_grouped"), mx_tiles(HALF, "k1", codes_tag="dp_raw00")]
+        keys = [mx_tiles(HALF, "k0", grouped_tag="qr1_grouped"), mx_tiles(HALF, "k1")]
         k_places = keys[0][0][:].rearrange("p (c t) -> p c t", t=PACK)
         k_early = held([P, 2, HALF], BF16, "k_early")
         k_late = held([P, PACK, HALF], BF16, "k_late")
@@ -205,10 +205,9 @@ def tile_attend_ggqa_sig_k_pl_kernel(tc, q1, q2, kT, dp1, dp2, us, ts, w1, w2, o
 
         for n, (h, b) in enumerate(TILES):
             if n == 0:
-                quantize(*keys[0], E4M3, 0, HALF)
-                weigh(0, 2, tag="qr1_grouped")
-            if n == 3:
-                quantize(*keys[1], E4M3, 0, HALF)
+                for half in range(2):
+                    quantize(*keys[half], E4M3, 0, HALF)
+                weigh(0, 2, tag="k1_grouped")
             cols = slice(b % 2 * P, (b % 2 + 1) * P)
             for k, part in enumerate(halves if n == 0 else [slice(0, R)]):
                 score = bank("a%d" % (k if n == 0 else (n + 1) % 4))[:, part]
@@ -216,11 +215,13 @@ def tile_attend_ggqa_sig_k_pl_kernel(tc, q1, q2, kT, dp1, dp2, us, ts, w1, w2, o
                                     rhs=qd[h][1][:, part].bitcast(E4M3), rhs_scale=qd[h][2][:, part], start=True, stop=True)
                 nc.vector.tensor_tensor(out=squares[n][:, part], in0=us_half[:, part], in1=score, op=ALU.mult)
                 nc.scalar.activation(out=squares[n][:, part], in_=squares[n][:, part], func=ACT.Tanh, scale=ts_col[:, b:b + 1])
-            if n > 0:
+            if n == 0:
+                square(0)
+            if n > 1:
                 square(n - 1)
         square(last)
 
-        weigh(2, 2, tag="k1_grouped")
+        weigh(2, 2)
         weigh(4, 2)
         g_halves = [mx_tiles(2 * HALF, "g0", grouped_tag="us_half", codes_tag="dp_raw01"), mx_tiles(2 * HALF, "g1")]
 
@@ -276,6 +277,7 @@ def tile_attend_ggqa_sig_k_pl_kernel(tc, q1, q2, kT, dp1, dp2, us, ts, w1, w2, o
         turn(last)
         gradient(5)
         quantize(*g_halves[1], E5M2, 0, HALF)
+        empty_two(nc.vector.tensor_copy, early_firsts, 0, 0)
         gradient(6)
         late_firsts = two_planes("a3", 2, 0)
         gradient(last)
@@ -306,7 +308,6 @@ def tile_attend_ggqa_sig_k_pl_kernel(tc, q1, q2, kT, dp1, dp2, us, ts, w1, w2, o
         def store_plane(queue, j):
             queue.dma_start(out=out_planes[:, j, :], in_=windows[j][:])
 
-        empty_two(nc.scalar.copy, early_firsts, 0, 0)
         for j in (0, 1):
             scatter(True, j, 0)
         empty_two(nc.vector.tensor_copy, late_firsts, 2, 0, tag="weight7")
@@ -339,11 +340,14 @@ def tile_attend_ggqa_sig_k_pl_kernel(tc, q1, q2, kT, dp1, dp2, us, ts, w1, w2, o
         def round_on_gpsimd(out, in_):
             nc.gpsimd.tensor_scalar(out=out, in0=in_, scalar1=1.0, scalar2=-0.0, op0=ALU.mult, op1=ALU.add)
 
-        rounded = held([P, PACK, DIRECT], BF16, "rounded", tag="dp_raw11")
+        parts = [(0, PIECE), (PIECE, DIRECT)]
+        rounded = [held([P, PACK, hi - lo], BF16, "rounded%d" % lo) for lo, hi in parts]
         for j in (0, 1):
-            round_on_gpsimd(out=rounded[:, j, :], in_=windows[j][:, 0:DIRECT])
-        for j in (2, 3):
-            nc.vector.tensor_copy(out=rounded[:, j, :], in_=windows[j][:, 0:DIRECT])
+            for tile, (lo, hi) in zip(rounded, parts):
+                round_on_gpsimd(out=tile[:, j, :], in_=windows[j][:, lo:hi])
+        for tile, (lo, hi) in zip(rounded, parts):
+            for j in (2, 3):
+                nc.vector.tensor_copy(out=tile[:, j, :], in_=windows[j][:, lo:hi])
 
         chunks = [(lo, min(2, (TOKENS - lo) // P)) for lo in range(DIRECT, TOKENS, 2 * P)]
         pair_banks = [("c1", "a2", "a0", "c0"), ("c2", "c3", "a3", "a1")]
@@ -381,17 +385,18 @@ def tile_attend_ggqa_sig_k_pl_kernel(tc, q1, q2, kT, dp1, dp2, us, ts, w1, w2, o
         for k in range(len(chunks)):
             pair_up(0, k, turn_planes(0, k))
         turned_planes = [turn_planes(1, k) for k in range(len(chunks))]
-        pair_up(1, 0, turned_planes[0])
+        for k in (0, 1):
+            pair_up(1, k, turned_planes[k])
         late = []
         for k in range(len(chunks)):
-            if k + 1 < len(chunks):
-                pair_up(1, k + 1, turned_planes[k + 1])
+            if k + 2 < len(chunks):
+                pair_up(1, k + 2, turned_planes[k + 2])
             late.append(turn_back(k))
 
         spans = [(lo, min(lo + PIECE, DIRECT)) for lo in range(0, DIRECT, PIECE)]
         early = [held([P, (hi - lo) * PACK], BF16, "y_grouped%d" % c, tag="k_raw%d" % c)[:] for c, (lo, hi) in enumerate(spans)]
         for c, (lo, hi) in enumerate(spans):
-            interleave(nc.vector.tensor_copy, early[c], rounded[:, :, lo:hi])
+            interleave(nc.vector.tensor_copy, early[c], rounded[1][:, :, lo - PIECE:hi - PIECE] if c else rounded[0][:])
             if c > 0:
                 quantize_and_store(early[c - 1], *spans[c - 1])
         quantize_and_store(early[-1], *spans[-1])

@@ -73,12 +73,7 @@ def tile_attend_ggqa_sig_k_pl_kernel(tc, q1, q2, kT, dp1, dp2, us, ts, w1, w2, o
         k_raw = [held([P, TOKENS], F32, "k_raw%d" % t) for t in range(PACK)]
         for t in range(PACK):
             nc.sync.dma_start(out=k_raw[t][:], in_=k_planes[:, t, :])
-        dp_raw = {}
-        for half in range(2):
-            for h, dp in enumerate((dp1, dp2)):
-                dp_raw[h, half] = held([P, PACK, HALF], F32, "dp_raw%d%d" % (h, half))
-                nc.sync.dma_start(out=dp_raw[h, half][:],
-                                  in_=dp.rearrange("(p t) c -> p t c", t=PACK)[:, :, half * HALF:(half + 1) * HALF])
+        dp_raw = [load_rows("dp_raw0", dp1), load_rows("dp_raw1", dp2)]
 
         ident = held([P, P], F32, "ident")
         make_identity(nc, ident[:])
@@ -186,11 +181,11 @@ def tile_attend_ggqa_sig_k_pl_kernel(tc, q1, q2, kT, dp1, dp2, us, ts, w1, w2, o
 
         weight = {}
 
-        def weigh(n, count, tag=None):
+        def weigh(engine, n, count, tag=None):
             h, b = TILES[n]
             tile = held([P, PACK, count * P], F32, "weight%d" % n, tag=tag)
-            nc.gpsimd.tensor_tensor(out=tile[:], in0=dp_raw[h, b // 2][:, :, b % 2 * P:(b % 2 + count) * P],
-                                    in1=factor[h][:, :, b * P:(b + count) * P], op=ALU.mult)
+            cols = slice(b * P, (b + count) * P)
+            engine.tensor_tensor(out=tile[:], in0=dp_raw[h][:, :, cols], in1=factor[h][:, :, cols], op=ALU.mult)
             for m in range(count):
                 weight[n + m] = tile[:, :, m * P:(m + 1) * P]
 
@@ -207,7 +202,7 @@ def tile_attend_ggqa_sig_k_pl_kernel(tc, q1, q2, kT, dp1, dp2, us, ts, w1, w2, o
             if n == 0:
                 for half in range(2):
                     quantize(*keys[half], E4M3, 0, HALF)
-                weigh(0, 2, tag="k1_grouped")
+                weigh(nc.gpsimd, 0, 2, tag="k1_grouped")
             cols = slice(b % 2 * P, (b % 2 + 1) * P)
             for k, part in enumerate(halves if n == 0 else [slice(0, R)]):
                 score = bank("a%d" % (k if n == 0 else (n + 1) % 4))[:, part]
@@ -221,9 +216,9 @@ def tile_attend_ggqa_sig_k_pl_kernel(tc, q1, q2, kT, dp1, dp2, us, ts, w1, w2, o
                 square(n - 1)
         square(last)
 
-        weigh(2, 2)
-        weigh(4, 2)
-        g_halves = [mx_tiles(2 * HALF, "g0", grouped_tag="us_half", codes_tag="dp_raw01"), mx_tiles(2 * HALF, "g1")]
+        weigh(nc.gpsimd, 2, 2)
+        weigh(nc.gpsimd, 4, 2)
+        g_halves = [mx_tiles(2 * HALF, "g0", grouped_tag="us_half", codes_tag="factor0")]
 
         turned = {}
 
@@ -269,17 +264,17 @@ def tile_attend_ggqa_sig_k_pl_kernel(tc, q1, q2, kT, dp1, dp2, us, ts, w1, w2, o
         turn(4)
         turn(5)
         quantize(*g_halves[0], E5M2, 0, 2 * HALF)
-        weigh(6, 1, tag="us_half")
-        weigh(last, 1)
+        weigh(nc.gpsimd, 6, 1, tag="us_half")
+        g_halves.append(mx_tiles(2 * HALF, "g1", codes_tag="dp_raw1"))
         gradient(4)
         early_firsts = two_planes("c0", 0, 0)
         turn(6)
         turn(last)
         gradient(5)
-        quantize(*g_halves[1], E5M2, 0, HALF)
-        empty_two(nc.vector.tensor_copy, early_firsts, 0, 0)
+        weigh(nc.vector, last, 1, tag="weight4")
         gradient(6)
         late_firsts = two_planes("a3", 2, 0)
+        quantize(*g_halves[1], E5M2, 0, HALF)
         gradient(last)
         quantize(*g_halves[1], E5M2, HALF, HALF + P)
         quantize(*g_halves[1], E5M2, HALF + P, 2 * HALF)
@@ -308,9 +303,10 @@ def tile_attend_ggqa_sig_k_pl_kernel(tc, q1, q2, kT, dp1, dp2, us, ts, w1, w2, o
         def store_plane(queue, j):
             queue.dma_start(out=out_planes[:, j, :], in_=windows[j][:])
 
+        empty_two(nc.scalar.copy, early_firsts, 0, 0)
         for j in (0, 1):
             scatter(True, j, 0)
-        empty_two(nc.vector.tensor_copy, late_firsts, 2, 0, tag="weight7")
+        empty_two(nc.vector.tensor_copy, late_firsts, 2, 0, tag="weight4")
         for j in (0, 1):
             empty_one(j)
         scatter(False, 0, 1)

@@ -142,13 +142,14 @@ def tile_attend_ggqa_sig_k_pl_kernel(tc, q1, q2, kT, dp1, dp2, us, ts, w1, w2, o
                     j = 2 * pair + jj
                     for u in range(2):
                         nc.tensor.transpose(ps[:, (2 * jj + u) * P:(2 * jj + u + 1) * P],
-                                            words[:, row * j + u:row * (j + 1):2], ident[:])
+                                            words[:, row * j + u * P:row * j + (u + 1) * P], ident[:])
                 nc.scalar.copy(
                     out=turned_words[:, BANK * pair:BANK * (pair + 1)].rearrange("p (j m u) -> p j m u", j=2, u=2),
                     in_=ps[:].rearrange("p (j u m) -> p j m u", j=2, u=2))
 
         for h in range(2):
-            nc.vector.tensor_copy(out=q_rounded[h][:], in_=q_raw[h][:].rearrange("p t r -> p (t r)"))
+            nc.vector.tensor_copy(out=q_rounded[h][:].rearrange("p (t u m e) -> p t u m e", t=PACK, u=2, e=2),
+                                  in_=q_raw[h][:].rearrange("p t (m u e) -> p t u m e", u=2, e=2))
             group_along_d(h)
             group_along_r(h)
             quantize(*qd[h], E4M3, 0, R)
@@ -167,15 +168,15 @@ def tile_attend_ggqa_sig_k_pl_kernel(tc, q1, q2, kT, dp1, dp2, us, ts, w1, w2, o
         k_places = keys[0][0][:].rearrange("p (c t) -> p c t", t=PACK)
         k_early = held([P, 2, HALF], BF16, "k_early")
         k_late = held([P, PACK, HALF], BF16, "k_late")
+        nc.vector.tensor_copy(out=k_late[:, 0, :], in_=k_raw[0][:].indirect(listed(HALF, SLOTS)))
         for t in (0, 1):
             nc.vector.tensor_copy(out=k_early[:, t, :], in_=k_raw[t][:].indirect(listed(0, HALF)))
-            nc.vector.tensor_copy(out=k_late[:, t, :], in_=k_raw[t][:].indirect(listed(HALF, SLOTS)))
         nc.vector.tensor_copy(out=k_places[:, :, 0:2], in_=k_early[:].rearrange("p t c -> p c t"))
         for t in (2, 3):
             nc.vector.tensor_copy(out=k_places[:, :, t], in_=k_raw[t][:].indirect(listed(0, HALF)))
         windows[2] = held([P, TOKENS], F32, "window2", tag="k_early")
         nc.gpsimd.memset(windows[2][:], 0.0)
-        for t in (2, 3):
+        for t in (1, 2, 3):
             nc.scalar.activation(out=k_late[:, t, :], in_=k_raw[t][:].indirect(listed(HALF, SLOTS)), func=ACT.Copy)
         interleave(nc.scalar.copy, keys[1][0][:], k_late[:])
 

from contextlib import ExitStack

import concourse.mybir as mybir
from concourse.masks import make_identity

F32 = mybir.dt.float32
BF16 = mybir.dt.bfloat16
I32 = mybir.dt.int32
U32 = mybir.dt.uint32
U16 = mybir.dt.uint16
U8 = mybir.dt.uint8
E4M3 = mybir.dt.float8_e4m3fn_x4
E5M2 = mybir.dt.float8_e5m2_x4
ACT = mybir.ActivationFunctionType
ALU = mybir.AluOpType

P = 128
D = 512
R = 512
SLOTS = 512
HALF = SLOTS // 2
TOKENS = 2048
PACK = 4
BANK = 512
RUN = 4
PIECE = 512
TILES = [(h, 2 * half + b) for half in range(2) for h in range(2) for b in range(2)]
DIRECT = 1152
VECTOR_CLEARS = 256
FLOPS = 4 * 2 * D * R * SLOTS


def tile_attend_ggqa_sig_k_pl_kernel(tc, q1, q2, kT, dp1, dp2, us, ts, w1, w2, offs, out_0, out_1, out_2):
    nc = tc.nc
    with ExitStack() as ctx:
        keep = ctx.enter_context(tc.tile_pool(name="keep", bufs=1))
        psum = ctx.enter_context(tc.psum_pool(name="psum", bufs=1))

        def held(shape, dtype, name, tag=None):
            return keep.tile(shape, dtype, name=name, tag=tag or name, align_bytes=64)

        def bank(tag):
            return psum.tile([P, BANK], F32, name=tag, tag=tag)

        def clear_on_vector(tile, lo, hi):
            nc.vector.memset(tile[:, lo:lo + 1], 0.0)
            nc.vector.memset(tile[:, lo + 1:hi], 0.0)

        def clear_together(tile, split):
            clear_on_vector(tile, 0, split)
            nc.gpsimd.memset(tile[:, split:TOKENS], 0.0)

        def load_column(name, vec):
            tile = held([P, PACK], F32, name)
            nc.scalar.dma_start(out=tile[:], in_=vec.rearrange("(p t) o -> p (t o)", t=PACK))
            return tile

        def load_rows(name, mat):
            tile = held([P, PACK, mat.shape[1]], F32, name)
            nc.sync.dma_start(out=tile[:].rearrange("p t c -> p (t c)"), in_=mat.rearrange("(p t) c -> p (t c)", t=PACK))
            return tile

        offsets = keep.tile([P, SLOTS // 16], U16, name="offsets")
        ts_row = held([P, TOKENS], F32, "ts_row")
        clear_together(ts_row, TOKENS // 2)
        q_raw = [load_rows("q_raw0", q1)]
        nc.sync.dma_start(offsets[:], offs)
        nc.sync.dma_start(out=ts_row[0:1, :], in_=ts[0:1, :])
        q_raw.append(load_rows("q_raw1", q2))
        us_col = load_column("us_col", us)
        w_col = [load_column("w1_col", w1), load_column("w2_col", w2)]
        k_planes = kT.rearrange("(p t) c -> p t c", t=PACK)
        k_raw = [held([P, TOKENS], F32, "k_raw%d" % t) for t in range(PACK)]
        for t in range(PACK):
            nc.sync.dma_start(out=k_raw[t][:], in_=k_planes[:, t, :])
        dp_raw = [load_rows("dp_raw0", dp1), load_rows("dp_raw1", dp2)]

        ident = held([P, P], F32, "ident")
        make_identity(nc, ident[:])
        minus_one = held([P, P], F32, "minus_one")
        nc.gpsimd.memset(minus_one[:], -1.0)
        windows = {t: held([P, TOKENS], F32, "window%d" % t) for t in (0, 1)}
        clear_on_vector(windows[1], 0, TOKENS)
        clear_together(windows[0], VECTOR_CLEARS)

        def listed(lo, hi):
            return offsets[:, lo // 16:hi // 16]

        def mx_tiles(width, name, grouped_tag=None, codes_tag=None):
            return (held([P, width * PACK], BF16, name + "_grouped", tag=grouped_tag),
                    held([P, width], U32, name + "_codes", tag=codes_tag), held([P, width], U8, name + "_scales"))

        def quantize(grouped, codes, scales, fmt, lo, hi):
            nc.vector.quantize_mx(out=codes[:, lo:hi].bitcast(fmt), scales=scales[:, lo:hi],
                                  in_=grouped[:, PACK * lo:PACK * hi])

        def in_runs(planes):
            return planes.rearrange("p t (c i) -> p c t i", i=RUN)

        def in_places(grouped):
            return grouped.rearrange("p (c i t) -> p c t i", i=RUN, t=PACK)

        def interleave(mover, grouped, planes):
            mover(out=in_places(grouped), in_=in_runs(planes))

        w_quarter = [held([P, PACK], F32, "w_quarter%d" % h) for h in range(2)]
        for h in range(2):
            nc.scalar.activation(out=w_quarter[h][:], in_=w_col[h][:], func=ACT.Copy, scale=-0.25)

        ts_listed = held([P, SLOTS], F32, "ts_listed")
        nc.scalar.activation(out=ts_listed[:], in_=ts_row[:].indirect(offsets[:]), func=ACT.Copy)
        ps = bank("a0")
        for b in range(SLOTS // P):
            nc.tensor.transpose(ps[:, b * P:(b + 1) * P], ts_listed[:, b * P:(b + 1) * P], ident[:])
        ts_col = held([P, SLOTS // P], F32, "ts_col")
        nc.scalar.copy(out=ts_col[:], in_=ps[:, 0:SLOTS:P])
        ts_spread = bank("a3")
        for b in range(SLOTS // P):
            nc.tensor.transpose(ts_spread[:, b * P:(b + 1) * P], ts_col[:, b:b + 1].to_broadcast([P, P]), ident[:])

        ps = bank("a2")
        for t in range(PACK):
            nc.tensor.transpose(ps[:, t * P:(t + 1) * P], us_col[:, t:t + 1].to_broadcast([P, P]), ident[:])
        us_half = held([P, R], F32, "us_half")
        nc.scalar.activation(out=us_half[:], in_=ps[:], func=ACT.Copy, scale=0.5)

        qd = [mx_tiles(R, "qd%d" % h) for h in range(2)]
        qr = [mx_tiles(D, "qr%d" % h) for h in range(2)]
        q_rounded = [held([P, PACK * R], BF16, "q_rounded%d" % h) for h in range(2)]

        def group_along_d(h):
            nc.vector.tensor_copy(out=qd[h][0][:].rearrange("p (i m t) -> p m t i", i=PACK, t=PACK),
                                  in_=q_raw[h][:].rearrange("p t (m i) -> p m t i", i=PACK))

        def group_along_r(h):
            words = q_rounded[h][:].bitcast(F32)
            turned_words = qr[h][0][:].bitcast(F32)
            row = R // 2
            for pair in range(2):
                ps = bank("c%d" % (2 * h + pair))
                for jj in range(2):
                    j = 2 * pair + jj
                    for u in range(2):
                        nc.tensor.transpose(ps[:, (2 * jj + u) * P:(2 * jj + u + 1) * P],
                                            words[:, row * j + u * P:row * j + (u + 1) * P], ident[:])
                nc.scalar.copy(
                    out=turned_words[:, BANK * pair:BANK * (pair + 1)].rearrange("p (j m u) -> p j m u", j=2, u=2),
                    in_=ps[:].rearrange("p (j u m) -> p j m u", j=2, u=2))

        for h in range(2):
            nc.vector.tensor_copy(out=q_rounded[h][:].rearrange("p (t u m e) -> p t u m e", t=PACK, u=2, e=2),
                                  in_=q_raw[h][:].rearrange("p t (m u e) -> p t u m e", u=2, e=2))
            group_along_d(h)
            group_along_r(h)
            quantize(*qd[h], E4M3, 0, R)
        for h in range(2):
            quantize(*qr[h], E4M3, 0, D)

        gate = [held([P, PACK], F32, "gate%d" % h) for h in range(2)]
        for h in range(2):
            nc.gpsimd.tensor_tensor(out=gate[h][:], in0=w_quarter[h][:], in1=us_col[:], op=ALU.mult)
        factor = [held([P, PACK, SLOTS], F32, "factor%d" % h) for h in range(2)]
        for h in range(2):
            for t in range(PACK):
                nc.scalar.activation(out=factor[h][:, t, :], in_=ts_spread[:], func=ACT.Copy, scale=gate[h][:, t:t + 1])

        keys = [mx_tiles(HALF, "k0", grouped_tag="qr1_grouped"), mx_tiles(HALF, "k1")]
        k_places = keys[0][0][:].rearrange("p (c t) -> p c t", t=PACK)
        k_early = held([P, 2, HALF], BF16, "k_early")
        k_late = held([P, PACK, HALF], BF16, "k_late")
        nc.vector.tensor_copy(out=k_late[:, 0, :], in_=k_raw[0][:].indirect(listed(HALF, SLOTS)))
        for t in (0, 1):
            nc.vector.tensor_copy(out=k_early[:, t, :], in_=k_raw[t][:].indirect(listed(0, HALF)))
        nc.vector.tensor_copy(out=k_places[:, :, 0:2], in_=k_early[:].rearrange("p t c -> p c t"))
        for t in (2, 3):
            nc.vector.tensor_copy(out=k_places[:, :, t], in_=k_raw[t][:].indirect(listed(0, HALF)))
        windows[2] = held([P, TOKENS], F32, "window2", tag="k_early")
        nc.gpsimd.memset(windows[2][:], 0.0)
        for t in (1, 2, 3):
            nc.scalar.activation(out=k_late[:, t, :], in_=k_raw[t][:].indirect(listed(HALF, SLOTS)), func=ACT.Copy)
        interleave(nc.scalar.copy, keys[1][0][:], k_late[:])

        weight = {}

        def weigh(engine, n, count, tag=None):
            h, b = TILES[n]
            tile = held([P, PACK, count * P], F32, "weight%d" % n, tag=tag)
            cols = slice(b * P, (b + count) * P)
            engine.tensor_tensor(out=tile[:], in0=dp_raw[h][:, :, cols], in1=factor[h][:, :, cols], op=ALU.mult)
            for m in range(count):
                weight[n + m] = tile[:, :, m * P:(m + 1) * P]

        squares = [held([P, R], F32, "square%d" % n) for n in range(len(TILES))]

        last = len(TILES) - 1
        halves = [slice(0, R // 2), slice(R // 2, R)]

        def square(n):
            for part in halves if n == last else [slice(0, R)]:
                nc.scalar.activation(out=squares[n][:, part], in_=squares[n][:, part], func=ACT.Square)

        for n, (h, b) in enumerate(TILES):
            if n == 0:
                for half in range(2):
                    quantize(*keys[half], E4M3, 0, HALF)
                weigh(nc.gpsimd, 0, 2, tag="k1_grouped")
            cols = slice(b % 2 * P, (b % 2 + 1) * P)
            for k, part in enumerate(halves if n == 0 else [slice(0, R)]):
                score = bank("a%d" % (k if n == 0 else (n + 1) % 4))[:, part]
                nc.tensor.matmul_mx(out=score, lhsT=keys[b // 2][1][:, cols].bitcast(E4M3), lhsT_scale=keys[b // 2][2][:, cols],
                                    rhs=qd[h][1][:, part].bitcast(E4M3), rhs_scale=qd[h][2][:, part], start=True, stop=True)
                nc.vector.tensor_tensor(out=squares[n][:, part], in0=us_half[:, part], in1=score, op=ALU.mult)
                nc.scalar.activation(out=squares[n][:, part], in_=squares[n][:, part], func=ACT.Tanh, scale=ts_col[:, b:b + 1])
            if n == 0:
                square(0)
            if n > 1:
                square(n - 1)
        square(last)

        weigh(nc.gpsimd, 2, 2)
        weigh(nc.gpsimd, 4, 2)
        g_halves = [mx_tiles(2 * HALF, "g0", grouped_tag="us_half", codes_tag="factor0")]

        turned = {}

        def turn(n):
            turned[n] = bank("c%d" % n if n < 4 else "a%d" % ((n + 1) % 4))
            for t in range(PACK):
                nc.tensor.matmul(turned[n][:, t * P:(t + 1) * P], lhsT=minus_one[:], rhs=ident[:],
                                 is_transpose=True, start=t == 0, stop=False)
            for t in range(PACK):
                nc.tensor.matmul(turned[n][:, t * P:(t + 1) * P], lhsT=squares[n][:, t * P:(t + 1) * P], rhs=ident[:],
                                 is_transpose=True, start=False, stop=t == PACK - 1)

        def gradient(n):
            nc.vector.tensor_tensor(out=in_places(g_halves[n // 4][0][:, BANK * (n % 4):BANK * (n % 4 + 1)]), in0=in_runs(weight[n]),
                                    in1=in_runs(turned[n][:].rearrange("p (t c) -> p t c", t=PACK)), op=ALU.mult)

        def product(out, j, half, h):
            cols = slice(j * P, (j + 1) * P)
            slots = slice(h * HALF, (h + 1) * HALF)
            nc.tensor.matmul_mx(out=out, lhsT=qr[h][1][:, cols].bitcast(E4M3), lhsT_scale=qr[h][2][:, cols],
                                rhs=g_halves[half][1][:, slots].bitcast(E5M2), rhs_scale=g_halves[half][2][:, slots],
                                start=h == 0, stop=h == 1)

        def two_planes(tag, j0, half):
            ps = bank(tag)
            for jj in range(2):
                for h in range(2):
                    product(ps[:, jj * HALF:(jj + 1) * HALF], j0 + jj, half, h)
            return ps

        dk = {}

        def empty_two(mover, ps, j0, half, tag=None):
            tile = held([P, 2 * HALF], F32, "dk_pair%d%d" % (j0, half), tag=tag)
            mover(out=tile[:], in_=ps[:])
            for jj in range(2):
                dk[j0 + jj, half] = tile[:, jj * HALF:(jj + 1) * HALF]

        for n in range(4):
            turn(n)
        for n in range(4):
            gradient(n)
        turn(4)
        turn(5)
        quantize(*g_halves[0], E5M2, 0, 2 * HALF)
        weigh(nc.gpsimd, 6, 1, tag="us_half")
        g_halves.append(mx_tiles(2 * HALF, "g1", codes_tag="dp_raw1"))
        gradient(4)
        early_firsts = two_planes("c0", 0, 0)
        turn(6)
        turn(last)
        gradient(5)
        weigh(nc.vector, last, 1, tag="weight4")
        gradient(6)
        late_firsts = two_planes("a3", 2, 0)
        quantize(*g_halves[1], E5M2, 0, HALF)
        gradient(last)
        quantize(*g_halves[1], E5M2, HALF, HALF + P)
        quantize(*g_halves[1], E5M2, HALF + P, 2 * HALF)
        windows[3] = held([P, TOKENS], F32, "window3", tag="g1_grouped")
        nc.gpsimd.memset(windows[3][:], 0.0)
        seconds = {0: bank("c2"), 1: bank("c3")}
        for h in range(2):
            for j in seconds:
                product(seconds[j][:, 0:HALF], j, 1, h)
        late_seconds = two_planes("a1", 2, 1)

        out_planes = out_0.rearrange("(p t) c -> p t c", t=PACK)
        dk_seconds = held([P, 2 * HALF], F32, "dk_seconds")

        def empty_one(j):
            dk[j, 1] = dk_seconds[:, j * HALF:(j + 1) * HALF]
            nc.vector.tensor_copy(out=dk[j, 1], in_=seconds[j][:, 0:HALF])

        def scatter(on_scalar, j, half):
            window = windows[j][:].indirect(listed(half * HALF, (half + 1) * HALF))
            if on_scalar:
                nc.scalar.activation(out=window, in_=dk[j, half], func=ACT.Copy)
            else:
                nc.vector.tensor_copy(out=window, in_=dk[j, half])

        def store_plane(queue, j):
            queue.dma_start(out=out_planes[:, j, :], in_=windows[j][:])

        empty_two(nc.scalar.copy, early_firsts, 0, 0)
        for j in (0, 1):
            scatter(True, j, 0)
        empty_two(nc.vector.tensor_copy, late_firsts, 2, 0, tag="weight4")
        for j in (0, 1):
            empty_one(j)
        scatter(False, 0, 1)
        store_plane(nc.sync, 0)
        scatter(True, 1, 1)
        store_plane(nc.sync, 1)
        empty_two(nc.scalar.copy, late_seconds, 2, 1)
        scatter(False, 2, 0)
        scatter(True, 3, 0)
        scatter(False, 2, 1)
        store_plane(nc.sync, 2)
        scatter(True, 3, 1)
        store_plane(nc.sync, 3)

        y_codes = held([P, TOKENS], U32, "y_codes")
        y_scales = held([P, TOKENS // 2], U8, "y_scales")
        words_out = out_1.rearrange("a p c t -> p (a c t)").bitcast(I32)

        stores = {PIECE: 0, DIRECT: PIECE, DIRECT + PIECE: DIRECT, TOKENS: DIRECT + PIECE}

        def quantize_and_store(grouped, lo, hi):
            a, col = divmod(lo, TOKENS // 2)
            nc.vector.quantize_mx(out=y_codes[:, lo:hi].bitcast(E4M3), scales=y_scales[4 * a:P, col:col + hi - lo], in_=grouped)
            if hi in stores:
                nc.sync.dma_start(out=words_out[:, stores[hi]:hi], in_=y_codes[:, stores[hi]:hi].bitcast(I32))

        def round_on_gpsimd(out, in_):
            nc.gpsimd.tensor_scalar(out=out, in0=in_, scalar1=1.0, scalar2=-0.0, op0=ALU.mult, op1=ALU.add)

        parts = [(0, PIECE), (PIECE, DIRECT)]
        rounded = [held([P, PACK, hi - lo], BF16, "rounded%d" % lo) for lo, hi in parts]
        for j in (0, 1):
            for tile, (lo, hi) in zip(rounded, parts):
                round_on_gpsimd(out=tile[:, j, :], in_=windows[j][:, lo:hi])
        for tile, (lo, hi) in zip(rounded, parts):
            for j in (2, 3):
                nc.vector.tensor_copy(out=tile[:, j, :], in_=windows[j][:, lo:hi])

        chunks = [(lo, min(2, (TOKENS - lo) // P)) for lo in range(DIRECT, TOKENS, 2 * P)]
        pair_banks = [("c1", "a2", "a0", "c0"), ("c2", "c3", "a3", "a1")]
        first_pairs = held([P, len(chunks) * BANK], BF16, "first_pairs", tag="dk_pair21")
        pairs = {}

        def turn_planes(u, k):
            ps = bank(pair_banks[u][k])
            lo, blocks = chunks[k]
            for b in range(blocks):
                for e in range(2):
                    nc.tensor.transpose(ps[:, (2 * b + e) * P:(2 * b + e + 1) * P],
                                        windows[2 * u + e][:, lo + b * P:lo + (b + 1) * P], ident[:])
            return ps

        def pair_up(u, k, ps):
            blocks = chunks[k][1]
            width = 2 * P * blocks
            pairs[u, k] = first_pairs[:, k * BANK:k * BANK + width] if u == 0 else held([P, width], BF16, "pairs%d" % k)[:]
            nc.scalar.copy(out=pairs[u, k].rearrange("c (b p e) -> c b p e", b=blocks, e=2),
                           in_=ps[:, 0:width].rearrange("c (b e p) -> c b p e", b=blocks, e=2))

        def turn_back(k):
            ps = bank(pair_banks[0][k])
            blocks = chunks[k][1]
            for u in range(2):
                words = pairs[u, k].bitcast(F32)
                for b in range(blocks):
                    nc.tensor.transpose(ps[:, (blocks * u + b) * P:(blocks * u + b + 1) * P], words[:, b * P:(b + 1) * P], ident[:])
            grouped = held([P, blocks * P * PACK], BF16, "turned_back%d" % k)
            nc.scalar.copy(out=grouped[:].bitcast(F32).rearrange("p (c u) -> p c u", u=2),
                           in_=ps[:, 0:2 * P * blocks].rearrange("p (u c) -> p c u", u=2))
            return grouped[:]

        for k in range(len(chunks)):
            pair_up(0, k, turn_planes(0, k))
        turned_planes = [turn_planes(1, k) for k in range(len(chunks))]
        for k in (0, 1):
            pair_up(1, k, turned_planes[k])
        late = []
        for k in range(len(chunks)):
            if k + 2 < len(chunks):
                pair_up(1, k + 2, turned_planes[k + 2])
            late.append(turn_back(k))

        spans = [(lo, min(lo + PIECE, DIRECT)) for lo in range(0, DIRECT, PIECE)]
        early = [held([P, (hi - lo) * PACK], BF16, "y_grouped%d" % c, tag="k_raw%d" % c)[:] for c, (lo, hi) in enumerate(spans)]
        for c, (lo, hi) in enumerate(spans):
            interleave(nc.vector.tensor_copy, early[c], rounded[1][:, :, lo - PIECE:hi - PIECE] if c else rounded[0][:])
            if c > 0:
                quantize_and_store(early[c - 1], *spans[c - 1])
        quantize_and_store(early[-1], *spans[-1])
        for k, (lo, blocks) in enumerate(chunks):
            quantize_and_store(late[k], lo, lo + blocks * P)
        scales_out = out_2.rearrange("a f c -> (a f) c").bitcast(I32).rearrange("f (a c) -> a f c", a=2)
        for quad in range(4):
            queue = nc.sync if quad % 2 == 0 else nc.scalar
            queue.dma_start(out=scales_out[:, 4 * quad:4 * quad + 4, :], in_=y_scales[32 * quad:32 * quad + 8, :].bitcast(I32))
